import numpy as np, ml_dtypes
CORES = [2,42,66,74,82,90,114]
N = 7
BF = ml_dtypes.bfloat16
def gentries(a):
    return np.ascontiguousarray(a.reshape(8, 16, -1).transpose(0, 2, 1)).reshape(8, -1)
def gtable(e):
    e = np.asarray(e); return np.ascontiguousarray(e.reshape(8, -1, 16).transpose(0, 2, 1)).reshape(128, -1).astype(np.int32)
W, T, Z, VI, SH = 4096, 192, 5, 4, 5
STEP = (0, 1, 2, 4)
kk = np.arange(16)
def parts(rng):
    return rng.integers(0, 64, (N, 8, 16, W)), rng.integers(0, W, (N, 8, 4, T, 16)), rng.integers(450, 850, (N, 8, 16))
def pack(x, h, th):
    return {"x": np.ascontiguousarray(x.reshape(N, 128, W)).astype(np.float32).astype(BF), "hom": np.stack([gtable(a.reshape(8, -1)) for a in h]),
            "th": np.ascontiguousarray(th.reshape(N, 128, 1)).astype(np.int32)}
def lay(z, u, v):
    z, u, v = np.broadcast_arrays(z, u, v); s = np.arange(4)[:, None, None]
    return np.where((s == 0) | (s == z[..., None, :, :] + 1), u[..., None, :, :], v[..., None, :, :])
def setup_inputs(rng):
    return pack(*parts(rng))
def setup_inputs_spread(rng):
    x, h, th = parts(rng)
    x = (64 * np.exp2(-rng.integers(0, 7, (N, 8, 1, W))) * rng.random((N, 8, 16, W))).astype(np.int64)
    h = (W * rng.random((N, 8, 4, T, 16)) ** rng.integers(1, 5, (N, 8, 1, 1, 1))).astype(np.int64)
    th = (2017 * rng.random((N, 8, 16)) ** 3).astype(np.int64)
    return pack(x, np.minimum(h, W - 1), np.minimum(th, 2016))
def setup_inputs_ends(rng):
    x = 63 * rng.integers(0, 2, (N, 8, 16, W)); h = (W - 1) * rng.integers(0, 2, (N, 8, 4, T, 16)); th = 2016 * rng.integers(0, 2, (N, 8, 16))
    four = np.array([1, 2, W - 17, W - 2])
    for g in (0, 2, 4, 6, 7):
        e = 63 * rng.integers(0, 2, (N, 1)); x[:, g, :, 0] = e; x[:, g, :, W - 1] = 63 - e
        for j in range(4):
            x[:, g, :, int(four[j])] = np.where((j == 0) | (kk % 3 == j - 1), e, 63 - e)
    def zip3(j):
        return np.where(j < 3 * (Z // 3), j % 3, 3)
    a, b = kk < Z, kk >= 16 - Z
    top = np.where(a, zip3(kk), np.where(b, zip3(kk - 16 + Z), 1 + (kk & 1)))
    t2 = np.where(a, 0, np.where(b, 1, 2)); t3 = np.where(a, 2, np.where(b, 0, 1))
    late = np.where(b, 0, 2)
    turn = np.array([[0, 1, 2, 3], [0, 2, 1, 3], [0, 2, 3, 1]])
    def seq(z, j):
        return np.where((j == Z - 1) | (j % 3 == 0), z, np.where(j % 3 == 1, 0, 3 - z))
    def great(zl, zr, at):
        z = np.where(b, seq(zr, kk - 16 + Z), np.where(a, seq(zl, kk), zl))
        return np.where(a | b | (kk == at), four[turn[z]].T, lay(np.zeros((1, 16), np.int64), 0, W - 1)[:, 0])
    for g in (0, 7):
        for i, z in ((0, top), (1, late), (2, t3), (3, t2), (T - 5, t3), (T - 3, late), (T - 2, t2), (T - 1, top)):
            h[:, g, :, i] = lay(z[None, :], 0, W - 1)[:, 0]
        h[:, g, :, 4] = 0; h[:, g, :, T - 4] = W - 1
        for i, s in ((5, great(2, 1, 15 - Z)), (6, great(1, 2, Z)), (T - 7, great(1, 2, 15 - Z)), (T - 6, great(2, 1, Z))):
            h[:, g, :, i] = s
    th[:, ::2, 15] = 2016; th[:, 1::2, 15] = 0; th[:, ::2, 0] = 0; th[:, 1::2, 0] = 2016
    return pack(x, h, th)
def setup_inputs_corners(rng):
    x, h, th = parts(rng); own = 16 * np.arange(T)[:, None] + kk
    th = rng.choice(np.array([0, 1, 31, 600, 700, 2015, 2016]), (N, 8, 16))
    for q in range(N):
        for g in range(8):
            c = (q + g) % 8
            if c == 0: h[q, g] = 0
            if c == 1: h[q, g] = W - 1
            if c == 2: h[q, g] = own
            if c == 3: h[q, g, 0] = own; h[q, g, 1] = W - 1 - own; h[q, g, 2] = 0; h[q, g, 3] = W - 1
            if c == 4: h[q, g] = h[q, g, 0].copy()
            if c == 5: h[q, g] = rng.choice(np.array([Z, 16 * (T - 1) + 16 - Z, 0, W - 1]), (4, T, 16))
            if c == 6: h[q, g, :, ::2] = 0
            if c == 7: h[q, g, :, 1::2] = rng.choice(W - np.array([3, 5, 7, 9, 19, 21]), (4, T // 2, 16)); th[q, g] = rng.choice(np.array([0, 1, 31]), 16)
    return pack(x, h, th)
def setup_inputs_crowd(rng):
    x, h, th = parts(rng)
    x[:, :, 0] = (x[:, :, 0] & 62) | (np.arange(W) & 1); x[..., 2::4] = x[..., 0::4]; x[..., 3::4] = x[..., 1::4]
    p = rng.integers(0, 3, (N, 8, T)); q = (p + rng.integers(1, 3, (N, 8, T))) % 3
    n = np.array([T, T - 1, 0, 1, 31, 32, T // 2, T - 32])[(np.arange(8)[None, :] + np.arange(N)[:, None]) % 8]
    n[N - 1] = np.array([T, T - 1, T, T - 1, T - 1, T - 1, T - 1, T])
    q = np.where(np.argsort(rng.random((N, 8, T)), axis=-1) < n[..., None], q, p)
    at = rng.integers(Z, 17 - Z, (N, 8, T)); at[..., 0] = Z; at[..., T - 1] = 16 - Z
    u = 2 * rng.integers(0, W // 2, (N, 8, T, 16)); v = 2 * rng.integers(0, W // 2, (N, 8, T, 16)) + 1
    h = lay(np.where(kk < at[..., None], p[..., None], q[..., None]), u, v) ^ (2 * rng.integers(0, 2, (N, 8, 4, T, 16)))
    return pack(x, h, th)
def setup_inputs_ties(rng):
    x, h, th = parts(rng); top = rng.integers(1, 4, (N, 8, 1, 1)); top[:, 7] = 1; top[:, 0] = 3
    x = np.minimum((rng.random((N, 8, 16, W)) * (top + 1)).astype(np.int64), top)
    h[:, ::2, :, ::2] = lay(rng.integers(0, 4, (N, 4, T // 2, 16)), rng.integers(0, W, (N, 4, T // 2, 16)), rng.integers(0, W, (N, 4, T // 2, 16)))
    return pack(x, h, rng.integers(0, 21, (N, 8, 16)))
def check_inputs(d):
    bad = []
    for k, lo, hi in (("x", 0, 63), ("hom", 0, W - 1), ("th", 0, 2016)):
        a = np.asarray(d[k]).astype(np.float64)
        if not (np.min(a) >= lo and np.max(a) <= hi): bad.append("range of " + k)
        elif np.any(a != np.floor(a)): bad.append("whole numbers in " + k)
    return bad
def reference(x, hom, th):
    v = x.astype(np.float32).astype(np.int32).reshape(N, 8, 16, W)
    s = np.stack([gentries(a) for a in hom]).astype(np.int64).reshape(N, 8, 4, T, 16)
    t = th.astype(np.int64).reshape(N, 8, 1, 16); A = np.zeros((N, 8), np.int64)
    strand = np.arange(4)[None, None, :, None, None]
    for visit in range(VI):
        p = [np.take_along_axis(v, s[:, :, a].reshape(N, 8, 1, 16 * T), 3) for a in range(4)]
        def dist(a, b):
            return np.add.reduce(np.abs(p[a] - p[b]), axis=2).reshape(N, 8, T, 16).astype(np.int64)
        c = np.stack([dist(0, 1) + dist(2, 3), dist(0, 2) + dist(1, 3), dist(0, 3) + dist(1, 2)])
        L = np.argmin(np.add.reduce(c[..., :Z], axis=-1), axis=0); R = np.argmin(np.add.reduce(c[..., 16 - Z:], axis=-1), axis=0)
        cl = np.take_along_axis(c, L[None, ..., None], 0)[0]; cr = np.take_along_axis(c, R[None, ..., None], 0)[0]
        tot = np.stack([np.add.reduce(cl[..., :m], axis=-1) + np.add.reduce(cr[..., m:], axis=-1) for m in range(Z, 17 - Z)])
        meet = Z + np.argmin(tot, axis=0)
        right = kk >= meet[..., None]
        over = np.where(right, cr, cl) > t + (A & 31)[:, :, None, None]
        mate = strand ^ (np.where(right, R[..., None], L[..., None])[:, :, None] + 1)
        new = ((s * np.take_along_axis(s, mate, 2) >> SH) + s + 37 * kk) & (W - 1)
        s = np.where(over[:, :, None] & (mate < strand), new, s)
        sw = L != R
        s = np.where((sw[..., None] & right)[:, :, None], np.take_along_axis(s, mate, 2), s)
        at = (kk == meet[..., None]).reshape(N, 8, 1, 16 * T)
        v[..., :16 * T] = np.where(at, (v[..., :16 * T] + p[0]) >> 1, v[..., :16 * T])
        A = np.add.reduce(sw.astype(np.int64), axis=-1)
        s = np.stack([np.roll(s[:, :, a], STEP[a], axis=0) for a in range(4)], axis=2)
    return {"yx": v.reshape(N, 128, W).astype(np.float32).astype(BF), "ys": np.stack([gtable(a.reshape(8, -1)) for a in s]).astype(np.float32)}

@@ -1,0 +1,575 @@
+from concourse.bass import DstId, RemoteDMATransfer
+from concourse.mybir import AluOpType as A, ActivationFunctionType as F
+
+VI = 4
+NC = 3
+HALF = 512
+STEP = (0, 1, 2, 4)
+PAIRS = ("02", "23", "03", "13", "01", "12")
+GORDER = ((2, 0), (0, 0), (2, 1), (0, 1), (3, 0), (3, 1), (1, 0), (1, 1))
+DG = ((0, 0), (0, 1))
+
+CY, PEC, GAM, SCA, WAKE, NET = 0.9, 0.45, 1.5, 3.5, 130.0, 7000.0
+TOL = 40.0
+BONUS = {'c0': 1702, 'c2': 2020, 'c1': -2022, 'u1': -2279, 'm2': -1645, 'u2': -478, 'g0': -8486, 'm1': 105, 'g1': -2946, 'm0': -4356, 'g2': -2143,
+         'u0': -1769}
+
+SCRATCH = {"xs": ("sbuf", [128, 4096], "bfloat16"), "homi": ("sbuf", [128, 768], "int32"), "lists": ("sbuf", [128, 12], "uint16"),
+           "thi": ("sbuf", [128, 1], "int32"), "ysb": ("sbuf", [128, 768], "float32"), "ici": ("sbuf", [128, 8], "int32"),
+           "ip": ("sbuf", [128, 1], "int32"), "accb": ("sbuf", [128, 4], "bfloat16")}
+PLACE = {}
+for _v in range(VI):
+    SCRATCH["off%d" % _v] = ("sbuf", [128, 768], "uint16")
+    SCRATCH["snd%d" % _v] = ("sbuf", [128, 576], "uint16" if _v < VI - 1 else "float32")
+for _s in range(4):
+    SCRATCH["g%d" % _s] = ("sbuf", [128, 3072], "bfloat16")
+for _b in range(8):
+    SCRATCH["pb%d" % _b] = ("psum", [128, 512], "float32")
+for _p in range(2):
+    for _n in PAIRS:
+        SCRATCH["d%s_%d" % (_n, _p)] = ("sbuf", [128, 1024], "bfloat16")
+
+
+def _pack(buf, dtype, names):
+    at = 0
+    for n, w in names:
+        PLACE[n] = (buf, at, w)
+        at += (w + 15) // 16 * 16
+    SCRATCH[buf] = ("sbuf", [128, at], dtype)
+
+
+for _p in range(NC):
+    for _k, _d, _l in (("h", "float16", (("ab", 128), ("c1", 64), ("y", 128), ("zz", 128), ("fs", 256), ("src", 192), ("vv", 64), ("ps", 256), ("st", 256),
+                                         ("gd", 256))),
+                       ("b", "bfloat16", (("u", 64), ("o", 64), ("tu", 128), ("om", 64), ("gs", 64), ("ts", 64), ("same", 64), ("xr", 320), ("fb", 128),
+                                          ("tq", 64))),
+                       ("f", "float32", (("m1", 64), ("lt", 32), ("sr", 128))),
+                       ("i", "int32", (("pp", 128), ("qq", 128), ("ui", 128), ("nb", 128)))):
+        _pack("w%s%d" % (_k, _p), _d, [("%s_%d" % (_n, _p), _w) for _n, _w in _l])
+_pack("conh", "float16", [(_n, 128) for _n in ("idh", "ndh", "i4h", "d37", "wza", "wzb", "wta", "wtb")])
+_pack("conb", "bfloat16", [(_n, 128) for _n in ("idb", "onb", "wc", "ca", "cb", "wr", "wrn", "wp2", "wsn", "wl0", "wl2", "bl0", "bl2", "br0", "br2", "b2k",
+                                                "rw")] + [("red", 144), ("reds", 144), ("ale", 131), ("alo", 131), ("m192", 64)])
+_pack("conf", "float32", [("ia", 144), ("onf", 128), ("nof", 128), ("idf", 128), ("ndf", 128), ("bm", 128), ("bm0", 128), ("jj", 128), ("kc", 1), ("ek", 16),
+                          ("acc", 4), ("thf", 2), ("j17", 17)] + [("t%d" % _n, 128) for _n in range(4)] + [("f%d" % _n, 17) for _n in range(8)] +
+      [("q%d" % _n, 17) for _n in range(4)] + [("col%d" % _n, 1) for _n in range(40)])
+SEMAPHORES = ["s_pe", "s_dve", "s_act", "s_pool", "sent", "dx", "dh", "dt", "dy0", "dy1", "dy2", "dy3", "dys"]
+SEMAPHORES += ["ds%d_%d_%d" % (_v, _c, _j) for _v in range(VI) for _c in range(NC) for _j in range(2)]
+SEMAPHORES += ["arr%d_%d" % (_v, _c) for _v in range(VI) for _c in range(NC)]
+CACHE = {}
+
+
+def schedule(nodes):
+    n = len(nodes)
+    succ = [[] for _ in range(n)]
+    for i, x in enumerate(nodes):
+        for d in x["deps"] | x["odeps"]:
+            succ[d].append(i)
+    level = [0.0] * n
+    prio = [0.0] * n
+    for i in range(n - 1, -1, -1):
+        x = nodes[i]
+        level[i] = x["cost"] + x["lat"] + max([level[j] + (WAKE if i in nodes[j]["deps"] else 0.0) for j in succ[i]] + [0.0])
+        prio[i] = level[i] + BONUS.get(x["lab"], 0.0)
+    left = [len(x["deps"] | x["odeps"]) for x in nodes]
+    ready = [0.0] * n
+    free, cand, order = {}, {}, []
+    for i, x in enumerate(nodes):
+        if left[i] == 0:
+            cand.setdefault(x["q"], []).append(i)
+    while len(order) < n:
+        best = None
+        for q, l in cand.items():
+            if not l:
+                continue
+            t = free.get(q, 0.0) if q is not None else 0.0
+            first = max(t, min(ready[i] for i in l))
+            i = max((i for i in l if ready[i] <= first + TOL), key=lambda i: (prio[i], -i))
+            if best is None or max(first, ready[i]) < best[0]:
+                best = (max(first, ready[i]), q, i)
+        s, q, i = best
+        cand[q].remove(i)
+        order.append(i)
+        x = nodes[i]
+        free[q] = s + x["cost"]
+        end = s + x["cost"] + x["lat"]
+        for j in succ[i]:
+            e = end + WAKE if i in nodes[j]["deps"] else s + x["cost"]
+            ready[j] = max(ready[j], e)
+            left[j] -= 1
+            if left[j] == 0:
+                cand.setdefault(nodes[j]["q"], []).append(j)
+    return order
+
+
+def rank_program(g, core, T, topo):
+    rank = T.rank_of(core)
+    if rank is None:
+        return
+    Q = {"pe": g.tensor, "dve": g.vector, "act": g.scalar, "pool": g, "sp": g.sync}
+    nodes, lastw, readers, banks = [], {}, {}, {}
+    pb = [T["pb%d" % b] for b in range(8)]
+    lab = [None]
+
+    def B(name, lo=0, hi=None, st=1):
+        buf, at, w = PLACE[name]
+        hi = w if hi is None else hi
+        return T[buf][:, at + lo:at + hi:st] if st > 1 else T[buf][:, at + lo:at + hi]
+
+    def op(q, fns, cost, r=(), w=(), b=(), ext=None, lat=0.0):
+        i = len(nodes)
+        deps, odeps = set(), set()
+        for t in r:
+            if t in lastw:
+                deps.add(lastw[t])
+        for t in w:
+            if t in lastw:
+                deps.add(lastw[t])
+            deps |= readers.get(t, set())
+        for t in b:
+            for q2, d in banks.get(t, {}).items():
+                (odeps if q2 == q else deps).add(d)
+        nodes.append({"q": q, "fns": fns, "cost": cost, "deps": deps, "odeps": odeps - deps, "ext": ext, "lat": lat, "lab": lab[0]})
+        for t in r:
+            readers.setdefault(t, set()).add(i)
+        for t in w:
+            lastw[t] = i
+            readers[t] = set()
+        for t in b:
+            banks.setdefault(t, {})[q] = i
+        return i
+
+    def tt(n, out, in0, in1, o, r=(), w=(), b=(), cost=None):
+        op("dve", [lambda: g.vector.tensor_tensor(out=out, in0=in0, in1=in1, op=o)], cost or CY * max(64, n * (1 if b else 2)), r, w, b)
+
+    def ts(n, out, in0, s1, o0, s2=None, o1=None, r=(), w=(), b=()):
+        if o1 is None:
+            op("dve", [lambda: g.vector.tensor_scalar(out=out, in0=in0, scalar1=s1, scalar2=None, op0=o0)], CY * max(64, n), r, w, b)
+        else:
+            op("dve", [lambda: g.vector.tensor_scalar(out=out, in0=in0, scalar1=s1, scalar2=s2, op0=o0, op1=o1)], CY * max(64, n), r, w, b)
+
+    def cp(n, out, in_, r=(), w=(), b=(), cost=None):
+        op("dve", [lambda: g.vector.tensor_copy(out=out, in_=in_)], cost or CY * max(64, n), r, w, b)
+
+    def act(n, out, in_, func, bias=0.0, accum=None, r=(), w=(), b=(), cost=None):
+        if accum is None:
+            op("act", [lambda: g.scalar.activation(out=out, in_=in_, func=func, bias=bias)], cost or CY * max(64, n), r, w, b)
+        else:
+            op("act", [lambda: g.scalar.activation(out=out, in_=in_, func=func, bias=bias, accum_out=accum)], cost or CY * max(64, n), r, w, b)
+
+    def mms(bank, lo, hi, terms, start=True, stop=True):
+        def one(l, x, s, e):
+            return lambda: g.tensor.matmul(out=pb[bank][:, lo:hi], lhsT=l, rhs=x, start=s, stop=e)
+        fns = [one(x[0], x[1], start and j == 0, stop and j == len(terms) - 1) for j, x in enumerate(terms)]
+        op("pe", fns, PEC * max(64, hi - lo) * len(terms), tuple({t for x in terms for t in x[2]}), (), (bank,))
+
+    def dma(q, eng, out, in_, sem, r=(), w=(), lat=2500.0):
+        op(q, [lambda: eng.dma_start(out=out, in_=in_)], 60.0, r, w, ext=(sem, 16), lat=lat)
+
+    dma("sp", g.sync, T.homi[:], T.hom[:], "dh", (), ("homi",), 3500.0)
+    dma("sp", g.sync, T.xs[:], T.x[:], "dx", (), ("x0", "x1", "x2", "x3"), 6500.0)
+    dma("act", g.scalar, T.thi[:], T.th[:], "dt", (), ("thi",))
+
+    def iota(out, pattern, base, cm, w, n, flag=True):
+        if flag:
+            op("pool", [lambda: g.iota(out, pattern, base, cm, allow_small_or_imprecise_dtypes=True)], 160 + 2 * n, (), (w,))
+        else:
+            op("pool", [lambda: g.iota(out, pattern, base, cm)], 160 + 2 * n, (), (w,))
+
+    def sel(out, in_, pattern, o, base, cm, r, w):
+        op("pool", [lambda: g.affine_select(out, in_, pattern, o, 0.0, base, cm)], 480, r, (w,))
+
+    def fill(name, x):
+        op("dve", [lambda: g.vector.memset(B(name), x)], 128, (), (name,))
+    iota(T.ip[:], [[0, 1]], 0, 1, "ip", 1, False)
+    iota(B("ia"), [[1, 144]], 0, 0, "ia", 144)
+    fill("onb", 1.0)
+    fill("onf", 1.0)
+    fill("nof", -1.0)
+    fill("m192", -192.0)
+    EYE = [[-1, 128]]
+    sel(B("idb"), B("onb"), EYE, A.is_equal, 0, 1, ("onb",), "idb")
+    iota(B("jj"), [[0, 8], [1, 16]], 0, 0, "jj", 128)
+    sel(B("bm0"), B("onf"), [[-16, 8], [0, 16]], A.is_ge, 0, 1, ("onf",), "bm0")
+    sel(B("bm"), B("bm0"), [[16, 8], [0, 16]], A.is_ge, 15, -1, ("bm0",), "bm")
+    sel(B("idf"), B("onf"), EYE, A.is_equal, 0, 1, ("onf",), "idf")
+    sel(B("ndf"), B("nof"), EYE, A.is_equal, 0, 1, ("nof",), "ndf")
+    iota(B("rw"), [[0, 4], [256, 32]], 0, 0, "rw", 128)
+    ncol = [0]
+
+    def col(n, in_, s1, o0, s2=None, o1=None, r=()):
+        name = "col%d" % ncol[0]
+        ncol[0] += 1
+        ts(n, B(name), in_, s1, o0, s2, o1, r=r, w=(name,))
+        return B(name), name
+    ici = T.ici
+    ts(1, ici[:, 0:1], T.ip[:], 15, A.bitwise_and, r=("ip",), w=("i0",))
+    ts(1, ici[:, 1:2], T.ip[:], 31, A.bitwise_and, r=("ip",), w=("i1",))
+    ts(1, ici[:, 2:3], T.ip[:], 16, A.bitwise_and, r=("ip",), w=("i2",))
+    pc, pct = col(1, T.ip[:], 0.0, A.add, r=("ip",))
+    kc, kct = B("kc"), "kc"
+    cp(1, kc, ici[:, 0:1], r=("i0",), w=(kct,))
+    tgb, tgbt = col(1, kc, -1.0, A.mult, pc, A.add, r=(kct, pct))
+    tgc, tgct = col(1, tgb, 15.0, A.add, r=(tgbt,))
+    ts(144, B("red"), B("ia"), tgc, A.is_equal, 2.0, A.mult, r=("ia", tgct), w=("red",))
+    ts(144, B("reds"), B("ia"), tgc, A.is_equal, r=("ia", tgct), w=("reds",))
+    ts(128, B("t0"), B("bm"), -512.0, A.mult, 512.0, A.add, r=("bm",), w=("t0",))
+    tt(128, B("jj"), B("jj"), B("t0"), A.add, r=("jj", "t0"), w=("jj",))
+    ts(16, B("ek"), B("ia", 0, 16), kc, A.is_equal, r=("ia", kct), w=("ek",))
+    cp(16, B("j17", 0, 16), B("ia", 0, 16), r=("ia",), w=("j17",))
+    cp(1, B("j17", 16, 17), kc, r=(kct,), w=("j17k",))
+    JT = ("j17", "j17k")
+
+    def fn(dst, start, steps):
+        for q, (co, t) in enumerate(steps):
+            tmp = "q%d" % (q % 4)
+            ts(17, B(tmp), B("j17"), float(t), A.is_ge, float(co), A.mult, r=JT, w=(tmp,))
+            if q == 0 and start is None:
+                tt(17, B(dst), B("j17"), B(tmp), A.add, r=JT + (tmp,), w=(dst,))
+            elif q == 0:
+                ts(17, B(dst), B(tmp), float(start), A.add, r=(tmp,), w=(dst,))
+            else:
+                tt(17, B(dst), B(dst), B(tmp), A.add, r=(tmp, dst), w=(dst,))
+
+    def both(name, out, n, in0, s1, o1, in1, s2, o2, mix, r):
+        ts(n, B("t0", 0, n), in0, s1, o1, r=r, w=("t0",))
+        ts(n, B("t1", 0, n), in1, s2, o2, r=r, w=("t1",))
+        tt(n, out, B("t0", 0, n), B("t1", 0, n), mix, r=("t0", "t1"), w=(name,))
+
+    def signs(name, p, m):
+        both(name, B(name), 128, B("jj"), B(p, 16, 17), A.is_equal, B("jj"), B(m, 16, 17), A.is_equal, A.subtract, ("jj", p, m))
+
+    def window(name, p, m):
+        both("t2", B("t2", 0, 16), 16, B(p, 0, 16), kc, A.is_le, B(m, 0, 16), kc, A.is_gt, A.mult, (p, m, kct))
+        for q in range(8):
+            ts(16, B(name, 16 * q, 16 * q + 16), B("t2", 0, 16), B("bm", 16 * q, 16 * q + 1), A.mult, r=("t2", "bm"), w=(name if q == 7 else name + str(q),))
+    r5, r5t = col(1, kc, 5.0, A.is_ge, 9000.0, A.mult, r=(kct,))
+    zl, zlt = col(1, kc, 11.0, A.is_ge, -8997.0, A.mult, r=(kct,))
+    lo, lot = col(1, r5, zl, A.add, r=(r5t, zlt))
+    l1, l1t = col(1, lo, 1.0, A.add, r=(lot,))
+    l2, l2t = col(1, lo, 2.0, A.add, r=(lot,))
+    ts(128, B("t3"), B("jj"), l1, A.is_le, r=("jj", l1t), w=("t3",))
+    ts(128, B("t2"), B("jj"), lo, A.is_ge, -1.0, A.mult, r=("jj", lot), w=("t2",))
+    tt(128, B("wza"), B("t2"), B("t3"), A.mult, r=("t2", "t3"), w=("wza",))
+    both("wzb", B("wzb"), 128, B("jj"), l1, A.is_ge, B("jj"), l2, A.is_le, A.mult, ("jj", l1t, l2t))
+
+    def spread(name, terms):
+        c = ct = None
+        for co, t in terms:
+            if c is None:
+                c, ct = col(1, B("ek", t, t + 1), float(co), A.mult, r=("ek",))
+            else:
+                c, ct = col(1, B("ek", t, t + 1), float(co), A.mult, c, A.add, r=("ek", ct))
+        ts(128, B(name), B("bm"), c, A.mult, r=("bm", ct), w=(name,))
+    fn("f0", 0.0, ((1, 2), (2, 3), (1, 5), (99, 6)))
+    fn("f1", 1.0, ((1, 1), (2, 3), (1, 4), (99, 6)))
+    signs("wc", "f0", "f1")
+    ts(8, B("wc", 15, 128, 16), B("bm", 15, 128, 16), B("ek", 15, 16), A.mult, 2.0, A.mult, r=("bm", "ek", "wc"), w=("wc",))
+    spread("wl0", ((1, 0), (-1, 3)))
+    spread("wl2", ((1, 2), (-1, 5)))
+    for wname, cname, a0, p, m in (("wta", "ca", (5, 7), ((-5, 5), (-6, 11), (99, 15)), ((-6, 5), (-4, 11), (99, 15))),
+                                   ("wtb", "cb", (99, 103), ((-99, 5), (-3, 8), (-2, 10), (99, 11)), ((-99, 5), (-2, 8), (-1, 10), (99, 11)))):
+        for q, (dst, steps) in enumerate((("f2", p), ("f3", m))):
+            fn(dst, None, steps)
+            ts(17, B(dst), B(dst), float(a0[q]), A.add, r=(dst,), w=(dst,))
+        window(wname, "f2", "f3")
+        signs(cname, "f2", "f3")
+    tE, tEt = col(1, ici[:, 2:3], 999.0, A.mult, r=("i2",))
+    ta, tat = col(1, ici[:, 1:2], -1.0, A.mult, pc, A.add, r=("i1", pct))
+    te, tet = col(1, ta, tE, A.add, 3.0, A.add, r=(tat, tEt))
+    to, tot = col(1, tE, -1.0, A.mult, ta, A.add, r=(tEt, tat))
+    to, tot = col(1, to, 16 * 999.0 + 3.0, A.add, r=(tot,))
+    ts(131, B("ale"), B("ia", 0, 131), te, A.is_equal, kc, A.mult, r=("ia", tet, kct), w=("ale",))
+    ts(131, B("alo"), B("ia", 0, 131), to, A.is_equal, kc, A.mult, r=("ia", tot, kct), w=("alo",))
+    k16, k16t = col(1, kc, 16.0, A.mult, r=(kct,))
+    cp(128, B("idh"), B("idf"), r=("idf",), w=("idh",))
+    cp(128, B("ndh"), B("ndf"), r=("ndf",), w=("ndh",))
+    ts(128, B("i4h"), B("idf"), 4096.0, A.mult, r=("idf",), w=("i4h",))
+    k37, k37t = col(1, kc, 37.0, A.mult, r=(kct,))
+    ts(128, B("d37"), B("idf"), k37, A.mult, r=("idf", k37t), w=("d37",))
+    both("wr", B("wr"), 128, B("jj"), kc, A.is_ge, B("bm"), 1.0, A.mult, A.mult, ("jj", kct, "bm"))
+    ts(128, B("wrn"), B("wr"), -1.0, A.mult, r=("wr",), w=("wrn",))
+    fn("f4", None, ((-3, 3), (99, 6)))
+    ts(128, B("wp2"), B("jj"), B("f4", 16, 17), A.is_equal, r=("jj", "f4"), w=("wp2",))
+    spread("wsn", ((-1, 0), (-1, 1), (-1, 2)))
+    spread("bl0", ((1, 0),))
+    spread("bl2", ((1, 2),))
+    spread("br0", ((1, 3), (-1, 15)))
+    spread("br2", ((1, 5), (-1, 15)))
+    spread("b2k", ((2048, 15),))
+    cp(1, B("thf", 0, 1), T.thi[:], r=("thi",), w=("thf0",))
+
+    for c in range(NC):
+        for s in (2, 0, 3, 1):
+            cp(64, T.off0[:, c * 256 + s * 64:c * 256 + s * 64 + 64], T.homi[:, s * 192 + c * 64:s * 192 + c * 64 + 64], r=("homi",), w=("off0_%d_%d" % (c, s),))
+
+    def gather(v, c, s, h):
+        lo = c * 256 + s * 64 + h * 32
+        at = c * 1024 + h * HALF
+        out, in_ = T["g%d" % s][:, at:at + HALF], T.xs[:, 0:4096].indirect(T["off%d" % v][:, lo:lo + 32])
+        r, w = ("x0", "x1", "x2", "x3", "off%d_%d_%d" % (v, c, s)), ("g%d_%d_%d" % (s, c, h),)
+        if c == 0 and (s, h) in DG:
+            cp(0, out, in_, r=r, w=w, cost=60 + GAM * HALF)
+        else:
+            act(0, out, in_, F.Copy, r=r, w=w, cost=70 + GAM * HALF)
+    uc = [0]
+
+    def ufill(c, s, h):
+        bank = uc[0] % 3
+        uc[0] += 1
+        at = c * 1024 + h * HALF
+        mms(bank, 0, 512, [(B("idb"), T["g%d" % s][:, at:at + HALF], ("idb", "g%d_%d_%d" % (s, c, h)))])
+        return bank
+
+    def pair(c, par, s, bank, name, h):
+        at = c * 1024 + h * HALF
+        tt(HALF, T["d%s_%d" % (name, par)][:, h * HALF:h * HALF + HALF], T["g%d" % s][:, at:at + HALF], pb[bank][:, 0:512], A.max,
+           r=("g%d_%d_%d" % (s, c, h),), w=("d%s_%d_%d" % (name, par, h),), b=(bank,))
+
+    def red(par, name, bank, at, first, last):
+        d = T["d%s_%d" % (name, par)]
+        toks = ("red", "d%s_%d_0" % (name, par), "d%s_%d_1" % (name, par))
+        for q in range(2):
+            mms(bank, at, at + 64, [(B("red", 15 - k, 143 - k), d[:, k:1024:16], toks) for k in range(8 * q, 8 * q + 8)],
+                first and q == 0, last and q == 1)
+
+    def add_up(v, c):
+        for j, (to_, s) in enumerate(((3, 2), (1, 0))):
+            toks = ["g%d_%d_%d" % (z, c, h) for z in (s, to_) for h in range(2)]
+            out, in_ = T["g%d" % to_][:, c * 1024:c * 1024 + 1024], T["g%d" % s][:, c * 1024:c * 1024 + 1024]
+            op("pool", [(lambda o_, i_: lambda: g.dma_start(out=o_, in_=i_, accum_op=A.add))(out, in_)], 1000.0, toks, toks[2:],
+               ext=("ds%d_%d_%d" % (v, c, j), 16), lat=3500.0)
+
+    def total(c, bk):
+        for q, s in enumerate((3, 1)):
+            for e in range(2):
+                mms(bk, 384, 448, [(B("reds", 15 - k, 143 - k), T["g%d" % s][:, c * 1024 + k:c * 1024 + 1024:16],
+                                    ("reds", "g%d_%d_0" % (s, c), "g%d_%d_1" % (s, c))) for k in range(8 * e, 8 * e + 8)], q + e == 0, q + e == 2)
+
+    def main(v, c):
+        par = (v * NC + c) % 2
+        u2 = [ufill(c, 2, 0), ufill(c, 2, 1)]
+        pair(c, par, 0, u2[0], "02", 0)
+        pair(c, par, 0, u2[1], "02", 1)
+        red(par, "02", 4, 0, True, False)
+        pair(c, par, 3, u2[0], "23", 0)
+        pair(c, par, 3, u2[1], "23", 1)
+        red(par, "23", 5, 0, True, False)
+        u3 = [ufill(c, 3, 0)]
+        pair(c, par, 0, u3[0], "03", 0)
+        u3.append(ufill(c, 3, 1))
+        pair(c, par, 0, u3[1], "03", 1)
+        pair(c, par, 1, u3[0], "13", 0)
+        pair(c, par, 1, u3[1], "13", 1)
+        red(par, "13", 4, 0, False, True)
+        u1 = [ufill(c, 1, 0)]
+        pair(c, par, 0, u1[0], "01", 0)
+        u1.append(ufill(c, 1, 1))
+        pair(c, par, 0, u1[1], "01", 1)
+        red(par, "01", 5, 0, False, True)
+        m1 = "m1_%d" % c
+        act(64, B(m1), pb[4][:, 0:64], F.Copy, w=(m1,), b=(4,))
+        red(par, "03", 4, 64, True, False)
+        tt(64, B("ab_%d" % c, 0, 64), pb[5][:, 0:64], B(m1), A.subtract, r=(m1,), w=("a_%d" % c,), b=(5,))
+        pair(c, par, 2, u1[0], "12", 0)
+        pair(c, par, 2, u1[1], "12", 1)
+        red(par, "12", 4, 64, False, True)
+        tt(64, B("ab_%d" % c, 64, 128), pb[4][:, 64:128], B(m1), A.subtract, r=(m1,), w=("b_%d" % c,), b=(4,))
+        add_up(v, c)
+
+    def crit(v, c):
+        bk = 6
+        n = lambda s: "%s_%d" % (s, c)
+        mms(bk, 0, 64, [(B("wza"), B(n("ab"), 0, 64), ("wza", n("a"))), (B("wzb"), B(n("ab"), 64, 128), ("wzb", n("b")))])
+        act(64, B(n("u")), pb[bk][:, 0:64], F.Sign, 0.5, w=(n("u"),), b=(bk,))
+        mms(bk, 64, 128, [(B("wc"), B(n("u")), ("wc", n("u")))])
+        act(64, B(n("o")), pb[bk][:, 64:128], F.Relu, -1.0, w=(n("o"),), b=(bk,))
+        mms(bk, 128, 192, [(B("wl0"), B(n("o")), ("wl0", n("o")))])
+        mms(bk, 192, 256, [(B("wl2"), B(n("o")), ("wl2", n("o")))])
+        tt(128, B(n("y")), B(n("ab")), pb[bk][:, 128:256], A.mult, r=(n("a"), n("b")), w=(n("y"),), b=(bk,))
+        for q, m in enumerate(("wta", "wtb")):
+            mt = tuple([m] + [m + str(e) for e in range(7)])
+            mms(bk, 256 + 64 * q, 320 + 64 * q, [(B(m), B(n("y"), 0, 64), mt + (n("y"),)), (B(m), B(n("y"), 64, 128), mt + (n("y"),))])
+        act(128, B(n("tu")), pb[bk][:, 256:384], F.Sign, 0.5, w=(n("tu"),), b=(bk,))
+        mms(bk, 384, 448, [(B("ca"), B(n("tu"), 0, 64), ("ca", n("tu"))), (B("cb"), B(n("tu"), 64, 128), ("cb", n("tu")))])
+        act(64, B(n("om")), pb[bk][:, 384:448], F.Relu, -5.0, w=(n("om"),), b=(bk,))
+        for q, m in enumerate(("ale", "alo")):
+            mms(bk, 448 + 16 * q, 464 + 16 * q, [(B("rw")[0:1, :], B("onb", 0, 16)[0:1, :], ("rw", "onb"))] +
+                [(B(m, 3 - r, 131 - r), B(n("om"), 16 * r, 16 * r + 16), (m, n("om"))) for r in range(4)])
+        op("dve", [lambda: g.vector.transpose(out=B(n("lt")), in_=pb[bk][:, 448:480])], 64, (), (n("lt"),), (bk,))
+        li, lit = T.lists[:, 4 * c:4 * c + 4], n("li")
+        ts(4, li, B(n("lt"), 0, 4), k16, A.add, r=(n("lt"), k16t), w=(lit,))
+        gr = (lit, "g0_%d_0" % c, "g0_%d_1" % c)
+        if c < NC - 1:
+            act(64, B(n("gs")), T.g0[:, c * 1024:c * 1024 + 1024].indirect(li), F.Copy, r=gr, w=(n("gs"),), cost=75 + 64 * GAM)
+        else:
+            cp(64, B(n("gs")), T.g0[:, c * 1024:c * 1024 + 1024].indirect(li), r=gr, w=(n("gs"),), cost=60 + 64 * GAM)
+        tt(64, B(n("ts")), T.xs[:, c * 1024:c * 1024 + 1024].indirect(li), B(n("gs")), A.add, r=(lit, n("gs"), "x%d" % c), w=(n("ts"),), cost=60 + 64 * GAM)
+        ts(64, B(n("tq")), B(n("ts")), 0.5, A.mult, 191.75, A.add, r=(n("ts"),), w=(n("tq"),))
+
+    def scatter(c):
+        tt(64, T.xs[:, c * 1024:c * 1024 + 1024].indirect(T.lists[:, 4 * c:4 * c + 4]), B("tq_%d" % c), B("m192"), A.add,
+           r=("tq_%d" % c, "m192", "li_%d" % c), w=("x%d" % c,), cost=60 + 64 * SCA)
+
+    def upd(v, c):
+        bk, bz = 7, 3
+        n = lambda s: "%s_%d" % (s, c)
+        st, stt = B(n("st")), n("st")
+        i16, n16, ib = B("idh"), B("ndh"), B("idb")
+        ts(256, st, T["off%d" % v][:, c * 256:c * 256 + 256], -2048.0, A.add, r=tuple("off%d_%d_%d" % (v, c, s) for s in range(4)), w=(stt,))
+        mms(bz, 448, 512, [(B("wp2"), B(n("o")), ("wp2", n("o")))])
+        act(64, B(n("same")), pb[bz][:, 448:512], F.Relu, -1.0, accum=B("acc", c, c + 1), w=(n("same"), "acc%d" % c), b=(bz,))
+        o, om = B(n("o")), B(n("om"))
+        for q, (m, w) in enumerate((("bl0", "wrn"), ("br0", "wr"), ("bl2", "wrn"), ("br2", "wr"))):
+            mms(bk, 64 * q, 64 * q + 64, [(B(m), o, (m, n("o"))), (B(w), om, (w, n("om")))])
+        mms(bk, 256, 320, [(B("wr"), om, ("wr", n("om"))), (B("wsn"), B(n("same")), ("wsn", n("same")))])
+        xr = n("xr")
+        act(320, B(xr), pb[bk][:, 0:320], F.Relu, w=(xr,), b=(bk,))
+        for q in range(4):
+            a = q // 2 * 128
+            mms(bz, 64 * q, 64 * q + 64, [(ib, B(xr, a, a + 64), ("idb", xr)), (ib, B(xr, a + 64, a + 128), ("idb", xr))])
+        fs = n("fs")
+        total(c, 5)
+        tt(64, B(n("c1")), B(n("m1")), pb[5][:, 384:448], A.subtract, r=(n("m1"),), w=(n("c1"),), b=(5,))
+        tt(128, B(fs, 0, 128), B(stt, 64, 192), pb[bz][:, 0:128], A.mult, r=(stt,), w=(fs,), b=(bz,))
+        tt(128, B(fs, 128, 256), B(stt, 128, 256), pb[bz][:, 128:256], A.mult, r=(stt,), w=(fs + "x",), b=(bz,))
+        tt(128, B(n("zz")), B(n("ab")), pb[bz][:, 64:192], A.mult, r=(n("a"), n("b")), w=(n("zz"),), b=(bz,))
+        act(128, B(n("fb")), pb[bz][:, 64:192], F.Copy, w=(n("fb"),), b=(bz,))
+        mms(5, 384, 448, [(i16, B(n("c1")), ("idh", n("c1"))), (i16, B(n("zz"), 0, 64), ("idh", n("zz"))), (i16, B(n("zz"), 64, 128), ("idh", n("zz")))])
+        ts(64, B(n("vv")), pb[5][:, 384:448], B("thf", v % 2, v % 2 + 1), A.is_gt, r=("thf%d" % (v % 2),), w=(n("vv"),), b=(5,))
+        f1, f2, h2, h3 = B(fs, 0, 64), B(fs, 64, 128), B(fs, 128, 192), B(fs, 192, 256)
+        s0, s1, s2, s3 = [B(stt, 64 * q, 64 * q + 64) for q in range(4)]
+        FT = ("idh", "ndh", stt, fs, fs + "x")
+        mms(bk, 320, 384, [(i16, s1, FT), (n16, f1, FT), (i16, f2, FT)])
+        cp(64, B(n("src"), 0, 64), pb[bk][:, 320:384], w=(n("src"),), b=(bk,))
+        k2 = (B("b2k"), o, ("b2k", n("o")))
+        qt = [(i16, s2, FT), (i16, f1, FT), (n16, f2, FT), (i16, h3, FT), (n16, h2, FT), k2]
+        tq = [(i16, s3, FT), (n16, h3, FT), (i16, h2, FT), k2]
+        mms(bk, 0, 64, qt)
+        mms(bk, 64, 128, tq)
+        vv = (B(n("vv")), ("idh", "d37", n("vv")))
+        v4 = (B("i4h"), B(n("vv")), ("i4h", n("vv")))
+        mms(bz, 128, 192, [(i16, s0, FT), v4])
+        mms(bz, 192, 256, [(i16, B(n("src"), 0, 64), ("idh", n("src"))), v4])
+        act(128, B(n("sr")), pb[bz][:, 128:256], F.Relu, b=(bz,), bias=-2048.0, w=(n("sr"),))
+        mms(bz, 256, 320, qt + [(B("d37"),) + vv])
+        mms(bz, 320, 384, tq + [(B("d37"),) + vv])
+        tt(128, B(n("pp")), B(n("sr")), pb[bk][:, 0:128], A.mult, r=(n("sr"),), w=(n("pp"),), b=(bk,))
+        ts(128, B(n("qq")), B(n("pp")), 5, A.arith_shift_right, r=(n("pp"),), w=(n("qq"),))
+        tt(128, B(n("ui")), B(n("qq")), pb[bz][:, 256:384], A.add, r=(n("qq"),), w=(n("ui"),), b=(bz,))
+        for q in range(3):
+            mms(bk, 64 * q, 64 * q + 64, [(ib, B(xr, 256, 320), ("idb", xr))])
+        ts(128, B(n("nb")), B(n("ui")), 4095, A.bitwise_and, r=(n("ui"),), w=(n("nb"),))
+        ps = n("ps")
+        ts(128, B(n("src"), 64, 192), B(n("nb")), -2048.0, A.add, r=(n("nb"),), w=(n("src") + "x",))
+        tt(64, B(ps, 0, 64), s0, pb[bk][:, 0:64], A.mult, r=(stt,), w=(ps,), b=(bk,))
+        tt(192, B(ps, 64, 256), B(n("src")), pb[bk][:, 0:192], A.mult, r=(n("src"), n("src") + "x"), w=(ps + "x",), b=(bk,))
+        r0, a1, b1 = [B(n("src"), 64 * q, 64 * q + 64) for q in range(3)]
+        e0, er, ea, eb = [B(ps, 64 * q, 64 * q + 64) for q in range(4)]
+        gd = n("gd")
+        SX = ["idh", "ndh", n("src"), n("src") + "x", ps, ps + "x", stt]
+        pos = lambda x: (i16, x, tuple(SX))
+        neg = lambda x: (n16, x, tuple(SX))
+        nq, nr, nt = [pos(a1), neg(ea), pos(e0)], [pos(r0), neg(er), pos(eb)], [pos(b1), neg(eb), pos(er)]
+        mms(bz, 192, 256, nq)
+        mms(bz, 256, 320, nr)
+        mms(bz, 320, 384, nt)
+        tt(64, B(gd, 0, 64), B(n("fb"), 0, 64), pb[bz][:, 192:256], A.mult, r=(n("fb"),), w=(gd,), b=(bz,))
+        tt(64, B(gd, 64, 128), B(n("fb"), 64, 128), pb[bz][:, 192:256], A.mult, r=(n("fb"),), w=(gd + "x",), b=(bz,))
+        tt(128, B(gd, 128, 256), B(n("fb")), pb[bz][:, 256:384], A.mult, r=(n("fb"),), w=(gd + "y",), b=(bz,))
+        SX += [gd, gd + "x", gd + "y"]
+        q1, q3, p1, p3 = [B(gd, 64 * q, 64 * q + 64) for q in range(4)]
+        mms(bk, 0, 64, [pos(s0), neg(e0), pos(ea)])
+        mms(bk, 64, 128, nr + [neg(p1), pos(q1)])
+        mms(bk, 128, 192, nq + [neg(q1), pos(p1), neg(q3), pos(p3)])
+        mms(bk, 192, 256, nt + [neg(p3), pos(q3)])
+        snd, sdt = T["snd%d" % v], "snd%d_%d" % (v, c)
+        if v < VI - 1:
+            ts(192, snd[:, c * 192:c * 192 + 192], pb[bk][:, 64:256], 2048.0, A.add, w=(sdt,), b=(bk,))
+            nxt = "off%d" % (v + 1)
+            ts(64, T[nxt][:, c * 256:c * 256 + 64], pb[bk][:, 0:64], 2048.0, A.add, w=("%s_%d_0" % (nxt, c),), b=(bk,))
+        else:
+            act(192, snd[:, c * 192:c * 192 + 192], pb[bk][:, 64:256], F.Identity, 2048.0, w=(sdt,), b=(bk,))
+            act(64, T.ysb[:, c * 64:c * 64 + 64], pb[bk][:, 0:64], F.Identity, 2048.0, w=("off%d_%d_0" % (VI, c),), b=(bk,))
+        tr = []
+        for s in (1, 2, 3):
+            dst = T.cores[(rank + STEP[s]) % len(T.cores)]
+            rid, pid, _ = topo.addr(dst)
+            e = topo.engines(core, dst)
+            if v < VI - 1:
+                land = T["off%d" % (v + 1)][:, c * 256 + s * 64:c * 256 + s * 64 + 64]
+            else:
+                land = T.ysb[:, s * 192 + c * 64:s * 192 + c * 64 + 64]
+            tr.append(RemoteDMATransfer(dst_ids=[DstId(rid=rid, pnc=pid)], dma_engine_mask=(1 << e[2 * s - 2]) | (1 << e[2 * s - 1]),
+                                        remote_sem=T.sem["arr%d_%d" % (v, c)], src=snd[:, (c * 3 + s - 1) * 64:(c * 3 + s) * 64], dst=land))
+        op("pool", [lambda: g.remote_dma_fused(tr, local_sem=T.sem.sent)], 1000.0, (sdt,), ("go",), ext="send")
+        op(None, [], 0.0, ("go",), tuple("off%d_%d_%d" % (v + 1, c, s) for s in (1, 2, 3)), ext=("arr%d_%d" % (v, c), 6), lat=NET)
+        if c == NC - 1 and v < VI - 1:
+            cp(4, T.accb[:, 0:3], B("acc", 0, 3), r=("acc0", "acc1", "acc2"), w=("accb",))
+            mms(bk, 0, 1, [(B("wsn"), T.accb[:, q:q + 1], ("wsn", "accb")) for q in range(3)])
+            cp(1, ici[:, 3:4], pb[bk][:, 0:1], w=("i3",), b=(bk,))
+            ts(1, ici[:, 4:5], ici[:, 3:4], 31, A.bitwise_and, r=("i3",), w=("i4",))
+            w = (v + 1) % 2
+            tt(1, B("thf", w, w + 1), ici[:, 4:5], T.thi[:], A.add, r=("i4", "thi"), w=("thf%d" % w,))
+
+    for v in range(VI):
+        for c in range(NC):
+            lab[0] = "g%d" % c
+            for s, h in GORDER:
+                gather(v, c, s, h)
+        for c in range(NC):
+            lab[0] = "m%d" % c
+            main(v, c)
+            lab[0] = "c%d" % c
+            crit(v, c)
+            scatter(c)
+            lab[0] = "u%d" % c
+            if v == VI - 1:
+                dma("sp", g.sync, T.yx[:, 1024 * c:1024 * c + 1024], T.xs[:, 1024 * c:1024 * c + 1024], ("dy0", "dy1", "dy3")[c], ("x%d" % c,))
+            upd(v, c)
+        if v == 0:
+            dma("sp", g.sync, T.yx[:, 3072:4096], T.xs[:, 3072:4096], "dy2", ("x3",))
+    dma("sp", g.sync, T.ys[:], T.ysb[:], "dys", tuple("off%d_%d_%d" % (VI, c, s) for c in range(NC) for s in range(4)))
+
+    if "order" not in CACHE:
+        CACHE["order"] = schedule(nodes)
+    known = {q: {} for q in Q}
+    cnt = {q: 0 for q in Q}
+    snap, ident, seen = {}, {}, set()
+
+    def wait(q, deps):
+        todo = sorted({d for d in deps if known[q].get(d[0], 0) < d[1]}, key=lambda d: (-len(snap.get(d, {})), d[0], -d[1]))
+        for s, k in todo:
+            if known[q].get(s, 0) >= k:
+                continue
+            Q[q].wait_ge(T.sem[s], k)
+            seen.add((s, k))
+            known[q][s] = k
+            for s2, k2 in snap.get((s, k), {}).items():
+                if known[q].get(s2, 0) < k2:
+                    known[q][s2] = k2
+    sent = 0
+    for i in CACHE["order"]:
+        x = nodes[i]
+        q = x["q"]
+        if q is None:
+            ident[i] = x["ext"]
+            continue
+        wait(q, [ident[d] for d in x["deps"] if d in ident])
+        for f in x["fns"]:
+            ins = f()
+            if x["ext"] is None:
+                cnt[q] += 1
+                ident[i] = ("s_" + q, cnt[q])
+                ins.then_inc(T.sem["s_" + q], 1)
+            elif x["ext"] == "send":
+                sent += 6
+            else:
+                ident[i] = x["ext"]
+                ins.then_inc(T.sem[x["ext"][0]], 16)
+        if i in ident:
+            snap[ident[i]] = dict(known[q])
+    ends = [("s_" + q, cnt[q]) for q in ("pe", "dve", "act", "pool")] + [("sent", sent)]
+    ends += [(s, 6 if s[:3] == "arr" else 16) for s in SEMAPHORES if s[:2] != "s_" and s != "sent"]
+    known["pool"].clear()
+    snap.clear()
+    wait("pool", [e for e in ends if e not in seen])

@@ -2,32 +2,36 @@ from concourse.bass import DstId, RemoteDMATransfer
 from concourse.mybir import AluOpType as A, ActivationFunctionType as F
 
 VI = 4
-NC = 3
-HALF = 512
+TW = 96
+SUB = 512
+CH = ((0, 1), (2,))
 STEP = (0, 1, 2, 4)
-PAIRS = ("02", "23", "03", "13", "01", "12")
-GORDER = ((2, 0), (0, 0), (2, 1), (0, 1), (3, 0), (3, 1), (1, 0), (1, 1))
-DG = ((0, 0), (0, 1))
+FILLS, SUMS, CRIT, UPD = (0, 1, 2), 3, (4, 5), (6, 7)
+ND, NT, NW = 3, 4, 4
+BYDMA = lambda v, H, c: False
+BYABS = lambda v, H, p: p == 1
+BYVEC = lambda v, H, p, s: v == 0 and H == 0 and s in (0, 1) and p < 2
 
-CY, PEC, GAM, SCA, WAKE, NET = 0.9, 0.45, 1.5, 3.5, 130.0, 7000.0
+CY, PEC, GAM, SCA, WAKE, NET, FIX = 0.9, 0.45, 1.4, 3.2, 120.0, 5000.0, 10.0
 TOL = 40.0
-BONUS = {'c0': 1702, 'c2': 2020, 'c1': -2022, 'u1': -2279, 'm2': -1645, 'u2': -478, 'g0': -8486, 'm1': 105, 'g1': -2946, 'm0': -4356, 'g2': -2143,
-         'u0': -1769}
+BONUS = {}
 
-SCRATCH = {"xs": ("sbuf", [128, 4096], "bfloat16"), "homi": ("sbuf", [128, 768], "int32"), "lists": ("sbuf", [128, 12], "uint16"),
-           "thi": ("sbuf", [128, 1], "int32"), "ysb": ("sbuf", [128, 768], "float32"), "ici": ("sbuf", [128, 8], "int32"),
-           "ip": ("sbuf", [128, 1], "int32"), "accb": ("sbuf", [128, 4], "bfloat16")}
+SCRATCH = {"thi": ("sbuf", [128, 8], "int32"), "ici": ("sbuf", [128, 16], "int32"), "ip": ("sbuf", [128, 1], "int32")}
 PLACE = {}
+for _h in range(2):
+    SCRATCH["xs%d" % _h] = ("sbuf", [128, 4096], "bfloat16")
+    SCRATCH["homi%d" % _h] = ("sbuf", [128, 768], "int32")
+    SCRATCH["ysb%d" % _h] = ("sbuf", [128, 384], "float32")
+    SCRATCH["lists%d" % _h] = ("sbuf", [128, 32], "uint16")
+    for _s in range(4):
+        SCRATCH["g%d_%d" % (_s, _h)] = ("sbuf", [128, 1536], "bfloat16")
 for _v in range(VI):
     SCRATCH["off%d" % _v] = ("sbuf", [128, 768], "uint16")
     SCRATCH["snd%d" % _v] = ("sbuf", [128, 576], "uint16" if _v < VI - 1 else "float32")
-for _s in range(4):
-    SCRATCH["g%d" % _s] = ("sbuf", [128, 3072], "bfloat16")
 for _b in range(8):
     SCRATCH["pb%d" % _b] = ("psum", [128, 512], "float32")
-for _p in range(2):
-    for _n in PAIRS:
-        SCRATCH["d%s_%d" % (_n, _p)] = ("sbuf", [128, 1024], "bfloat16")
+for _p in range(ND):
+    SCRATCH["d%d" % _p] = ("sbuf", [128, 6 * SUB], "bfloat16")
 
 
 def _pack(buf, dtype, names):
@@ -38,23 +42,23 @@ def _pack(buf, dtype, names):
     SCRATCH[buf] = ("sbuf", [128, at], dtype)
 
 
-for _p in range(NC):
-    for _k, _d, _l in (("h", "float16", (("ab", 128), ("c1", 64), ("y", 128), ("zz", 128), ("fs", 256), ("src", 192), ("vv", 64), ("ps", 256), ("st", 256),
-                                         ("gd", 256))),
-                       ("b", "bfloat16", (("u", 64), ("o", 64), ("tu", 128), ("om", 64), ("gs", 64), ("ts", 64), ("same", 64), ("xr", 320), ("fb", 128),
-                                          ("tq", 64))),
-                       ("f", "float32", (("m1", 64), ("lt", 32), ("sr", 128))),
-                       ("i", "int32", (("pp", 128), ("qq", 128), ("ui", 128), ("nb", 128)))):
-        _pack("w%s%d" % (_k, _p), _d, [("%s_%d" % (_n, _p), _w) for _n, _w in _l])
-_pack("conh", "float16", [(_n, 128) for _n in ("idh", "ndh", "i4h", "d37", "wza", "wzb", "wta", "wtb")])
-_pack("conb", "bfloat16", [(_n, 128) for _n in ("idb", "onb", "wc", "ca", "cb", "wr", "wrn", "wp2", "wsn", "wl0", "wl2", "bl0", "bl2", "br0", "br2", "b2k",
-                                                "rw")] + [("red", 144), ("reds", 144), ("ale", 131), ("alo", 131), ("m192", 64)])
-_pack("conf", "float32", [("ia", 144), ("onf", 128), ("nof", 128), ("idf", 128), ("ndf", 128), ("bm", 128), ("bm0", 128), ("jj", 128), ("kc", 1), ("ek", 16),
-                          ("acc", 4), ("thf", 2), ("j17", 17)] + [("t%d" % _n, 128) for _n in range(4)] + [("f%d" % _n, 17) for _n in range(8)] +
-      [("q%d" % _n, 17) for _n in range(4)] + [("col%d" % _n, 1) for _n in range(40)])
-SEMAPHORES = ["s_pe", "s_dve", "s_act", "s_pool", "sent", "dx", "dh", "dt", "dy0", "dy1", "dy2", "dy3", "dys"]
-SEMAPHORES += ["ds%d_%d_%d" % (_v, _c, _j) for _v in range(VI) for _c in range(NC) for _j in range(2)]
-SEMAPHORES += ["arr%d_%d" % (_v, _c) for _v in range(VI) for _c in range(NC)]
+for _p in range(NW):
+    for _k, _d, _l in (("h", "float16", (("ab", 3), ("y", 2), ("zz", 2), ("st", 4), ("f1", 2), ("f2", 2), ("vv", 1), ("e1", 2), ("e2", 2), ("src", 2),
+                                         ("g1", 2), ("g2", 2), ("am", 3))),
+                       ("b", "bfloat16", (("u", 1), ("o", 1), ("tu", 2), ("pm", 2))),
+                       ("f", "float32", (("sr", 2), ("pp", 2))),
+                       ("i", "int32", (("ui", 2), ("nb", 2)))):
+        _pack("w%s%d" % (_k, _p), _d, [("%s_%d" % (_n, _p), 64 * _w) for _n, _w in _l])
+_pack("cts", "float16", [("ct%d" % _p, 400) for _p in range(NT)] + [("dk", 128)])
+_pack("blb", "bfloat16", [("%s%d" % (_n, _h), _w) for _h in range(2) for _n, _w in (("om", 96), ("gs", 96), ("gx", 96), ("tq", 192), ("accb", 4))])
+_pack("conb", "bfloat16", [(_n, 128) for _n in ("idb", "nid", "i32", "n32", "i4k", "onb", "t2k", "tbig", "teps", "sel", "pi", "bm0", "bm", "lt0", "lt1", "lt",
+                                                "wr", "w5", "wl0", "wl2", "sp0", "sp2", "rw", "dke", "dko")] +
+      [("hm", 256), ("wsn", 192), ("red0", 104), ("red1", 104), ("red", 104), ("m192", 192), ("wz", 384), ("ca", 256), ("cat", 256), ("wt", 256), ("mz", 256),
+       ("al", 288), ("ia", 160), ("jr", 160), ("zero", 400)] + [("tm%d" % _n, 160) for _n in range(11)])
+_pack("conf", "float32", [("kf", 8), ("ek", 16), ("acc", 8), ("thf", 4), ("lt32", 64), ("two", 8)] + [("col%d" % _n, 1) for _n in range(24)])
+SEMAPHORES = ["s_pe", "s_dve", "s_act", "s_pool", "sent", "dout"] + ["d%s%d" % (_n, _h) for _n in "xht" for _h in range(4)]
+SEMAPHORES += ["ds%d_%d_%d" % (_v, _c, _j) for _v in range(VI) for _c in range(2 * len(CH)) for _j in range(3) if BYDMA(_v, _c // len(CH), _c % len(CH))]
+SEMAPHORES += ["arr%d_%d" % (_v, _c) for _v in range(VI) for _c in range(2 * len(CH))]
 CACHE = {}
 
 
@@ -139,402 +143,415 @@ def rank_program(g, core, T, topo):
         return i
 
     def tt(n, out, in0, in1, o, r=(), w=(), b=(), cost=None):
-        op("dve", [lambda: g.vector.tensor_tensor(out=out, in0=in0, in1=in1, op=o)], cost or CY * max(64, n * (1 if b else 2)), r, w, b)
+        op("dve", [lambda: g.vector.tensor_tensor(out=out, in0=in0, in1=in1, op=o)], cost or FIX + CY * max(64, n * (1 if b else 2)), r, w, b)
 
-    def ts(n, out, in0, s1, o0, s2=None, o1=None, r=(), w=(), b=()):
+    def ts(n, out, in0, s1, o0, s2=None, o1=None, r=(), w=(), b=(), cost=None):
         if o1 is None:
-            op("dve", [lambda: g.vector.tensor_scalar(out=out, in0=in0, scalar1=s1, scalar2=None, op0=o0)], CY * max(64, n), r, w, b)
+            op("dve", [lambda: g.vector.tensor_scalar(out=out, in0=in0, scalar1=s1, scalar2=None, op0=o0)], cost or FIX + CY * max(64, n), r, w, b)
         else:
-            op("dve", [lambda: g.vector.tensor_scalar(out=out, in0=in0, scalar1=s1, scalar2=s2, op0=o0, op1=o1)], CY * max(64, n), r, w, b)
+            op("dve", [lambda: g.vector.tensor_scalar(out=out, in0=in0, scalar1=s1, scalar2=s2, op0=o0, op1=o1)], cost or FIX + CY * max(64, n), r, w, b)
 
     def cp(n, out, in_, r=(), w=(), b=(), cost=None):
-        op("dve", [lambda: g.vector.tensor_copy(out=out, in_=in_)], cost or CY * max(64, n), r, w, b)
+        op("dve", [lambda: g.vector.tensor_copy(out=out, in_=in_)], cost or FIX + CY * max(64, n), r, w, b)
 
-    def act(n, out, in_, func, bias=0.0, accum=None, r=(), w=(), b=(), cost=None):
-        if accum is None:
-            op("act", [lambda: g.scalar.activation(out=out, in_=in_, func=func, bias=bias)], cost or CY * max(64, n), r, w, b)
-        else:
-            op("act", [lambda: g.scalar.activation(out=out, in_=in_, func=func, bias=bias, accum_out=accum)], cost or CY * max(64, n), r, w, b)
+    def act(n, out, in_, func, bias=0.0, scale=1.0, accum=None, r=(), w=(), b=(), cost=None):
+        kw = {} if accum is None else {"accum_out": accum}
+        op("act", [lambda: g.scalar.activation(out=out, in_=in_, func=func, bias=bias, scale=scale, **kw)], cost or FIX + CY * max(64, n), r, w, b)
+
+    def mm(bank, out, n, terms, start=True, stop=True):
+        def one(l, x, s, e):
+            return lambda: g.tensor.matmul(out=out, lhsT=l, rhs=x, start=s, stop=e)
+        fns = [one(x[0], x[1], start and j == 0, stop and j == len(terms) - 1) for j, x in enumerate(terms)]
+        op("pe", fns, PEC * max(64, n) * len(terms), tuple({t for x in terms for t in x[2]}), (), (bank,))
 
     def mms(bank, lo, hi, terms, start=True, stop=True):
-        def one(l, x, s, e):
-            return lambda: g.tensor.matmul(out=pb[bank][:, lo:hi], lhsT=l, rhs=x, start=s, stop=e)
-        fns = [one(x[0], x[1], start and j == 0, stop and j == len(terms) - 1) for j, x in enumerate(terms)]
-        op("pe", fns, PEC * max(64, hi - lo) * len(terms), tuple({t for x in terms for t in x[2]}), (), (bank,))
+        mm(bank, pb[bank][:, lo:hi], hi - lo, terms, start, stop)
 
-    def dma(q, eng, out, in_, sem, r=(), w=(), lat=2500.0):
-        op(q, [lambda: eng.dma_start(out=out, in_=in_)], 60.0, r, w, ext=(sem, 16), lat=lat)
+    def dma(q, out, in_, sem, r=(), w=(), lat=2500.0):
+        op(q, [lambda: Q[q].dma_start(out=out, in_=in_)], 60.0, r, w, ext=(sem, 16), lat=lat)
 
-    dma("sp", g.sync, T.homi[:], T.hom[:], "dh", (), ("homi",), 3500.0)
-    dma("sp", g.sync, T.xs[:], T.x[:], "dx", (), ("x0", "x1", "x2", "x3"), 6500.0)
-    dma("act", g.scalar, T.thi[:], T.th[:], "dt", (), ("thi",))
+    for H in range(2):
+        for c in range(2):
+            rows, to = slice(64 * H, 64 * H + 64), slice(64 * c, 64 * c + 64)
+            dma("act", T["homi%d" % H][to, 0:768 - TW * c], T.hom[rows, TW * c:768], "dh%d" % (2 * H + c), (), ("homi%d_%d" % (H, c),), 3000.0 + 3000 * H)
+            dma("sp", T["xs%d" % H][to, :], T.x[rows, :], "dx%d" % (2 * H + c), (), ("xl%d_%d" % (H, c),), 5000.0 + 3000 * H)
+    for H in range(2):
+        for c in range(2):
+            dma("sp", T.thi[64 * c:64 * c + 64, 4 * H:4 * H + 1], T.th[64 * H:64 * H + 64, :], "dt%d" % (2 * H + c), (), ("thi%d_%d" % (H, c),), 8000.0)
 
     def iota(out, pattern, base, cm, w, n, flag=True):
-        if flag:
-            op("pool", [lambda: g.iota(out, pattern, base, cm, allow_small_or_imprecise_dtypes=True)], 160 + 2 * n, (), (w,))
-        else:
-            op("pool", [lambda: g.iota(out, pattern, base, cm)], 160 + 2 * n, (), (w,))
+        kw = {"allow_small_or_imprecise_dtypes": True} if flag else {}
+        op("pool", [lambda: g.iota(out, pattern, base, cm, **kw)], 140 + 2 * CY * n, (), (w,))
 
-    def sel(out, in_, pattern, o, base, cm, r, w):
-        op("pool", [lambda: g.affine_select(out, in_, pattern, o, 0.0, base, cm)], 480, r, (w,))
+    def sel(name, src, pattern, o, base, cm, n=128, rows=slice(0, 128), tok=None):
+        out, in_ = B(name)[rows, :], B(src)[rows, :]
+        op("pool", [lambda: g.affine_select(out, in_, pattern, o, 0.0, base, cm)], 180 + 2 * CY * n, (src,), (tok or name,))
 
-    def fill(name, x):
-        op("dve", [lambda: g.vector.memset(B(name), x)], 128, (), (name,))
-    iota(T.ip[:], [[0, 1]], 0, 1, "ip", 1, False)
-    iota(B("ia"), [[1, 144]], 0, 0, "ia", 144)
-    fill("onb", 1.0)
-    fill("onf", 1.0)
-    fill("nof", -1.0)
-    fill("m192", -192.0)
-    EYE = [[-1, 128]]
-    sel(B("idb"), B("onb"), EYE, A.is_equal, 0, 1, ("onb",), "idb")
-    iota(B("jj"), [[0, 8], [1, 16]], 0, 0, "jj", 128)
-    sel(B("bm0"), B("onf"), [[-16, 8], [0, 16]], A.is_ge, 0, 1, ("onf",), "bm0")
-    sel(B("bm"), B("bm0"), [[16, 8], [0, 16]], A.is_ge, 15, -1, ("bm0",), "bm")
-    sel(B("idf"), B("onf"), EYE, A.is_equal, 0, 1, ("onf",), "idf")
-    sel(B("ndf"), B("nof"), EYE, A.is_equal, 0, 1, ("nof",), "ndf")
-    iota(B("rw"), [[0, 4], [256, 32]], 0, 0, "rw", 128)
+    def fill(name, x, lo=0, hi=None):
+        op("dve", [lambda: g.vector.memset(B(name, lo, hi), x)], FIX + CY * 64, (), (name,))
     ncol = [0]
 
-    def col(n, in_, s1, o0, s2=None, o1=None, r=()):
+    def col(in_, s1, o0, s2=None, o1=None, r=()):
         name = "col%d" % ncol[0]
         ncol[0] += 1
-        ts(n, B(name), in_, s1, o0, s2, o1, r=r, w=(name,))
+        ts(1, B(name), in_, s1, o0, s2, o1, r=r, w=(name,))
         return B(name), name
+
+    def summed(name, lo, n, bank, parts):
+        for j, terms in enumerate(parts):
+            mms(bank, n * j, n * j + n, terms)
+        act(n * len(parts), B(name, lo, lo + n * len(parts)), pb[bank][:, 0:n * len(parts)], F.Copy, w=(name,), b=(bank,))
+    iota(T.ip[:], [[0, 1]], 0, 1, "ip", 1, False)
+    fill("onb", 1.0)
+    sel("idb", "onb", [[-1, 128]], A.is_equal, 0, 1)
+    for lo, hi, x in ((0, 104, 0.0), (8, 16, 2.0), (32, 72, -1.0), (48, 56, 0.0), (72, 80, 1.0), (80, 96, -2.0), (96, 104, 2.0)):
+        fill("red0", x, lo, hi)
+    sel("red1", "red0", [[0, 13], [-16, 8]], A.is_ge, 0, 1, 104)
+    sel("red", "red1", [[0, 13], [16, 8]], A.is_ge, 15, -1, 104)
+    RB, RA, RS, RE, RD, RC = [B("red", 8 * j, 8 * j + 24) for j in (0, 1, 2, 4, 7, 10)]
+    iota(B("ia"), [[1, 160]], 0, 0, "ia", 160)
+    sel("sel", "onb", [[-1, 4], [-4, 32]], A.is_equal, 0, 1)
+    sel("bm0", "onb", [[-16, 8], [0, 16]], A.is_ge, 0, 1)
+    sel("bm", "bm0", [[16, 8], [0, 16]], A.is_ge, 15, -1)
+    sel("lt0", "onb", [[-16, 8], [0, 16]], A.is_ge, -5, 1)
+    sel("lt1", "lt0", [[16, 8], [0, 16]], A.is_ge, 11, -1)
+    TURN = [[-16, 8], [-1, 4], [-4, 4]]
+    sel("lt", "lt1", TURN, A.is_gt, 0, 1)
+    sel("pi", "onb", TURN, A.is_equal, 0, 1)
+    sel("wr", "bm", [[1, 128]], A.is_ge, 0, -1)
+    iota(B("rw"), [[0, 8], [256, 16]], 0, 0, "rw", 128)
+    fill("zero", 0.0)
+    for j in range(NT):
+        cp(200, B("ct%d" % j), B("zero"), r=("zero",), w=("ct%d" % j,))
+    for name, x in (("t2k", 2048.0), ("tbig", 65536.0 - 2.0 ** 23), ("teps", 0.125), ("m192", -192.0)):
+        fill(name, x)
+    for name, x in (("nid", -1.0), ("i32", 32.0), ("n32", -32.0), ("i4k", 4096.0)):
+        ts(64, B(name), B("idb"), x, A.mult, r=("idb",), w=(name,))
+    I, N_ = B("idb"), B("nid")
     ici = T.ici
-    ts(1, ici[:, 0:1], T.ip[:], 15, A.bitwise_and, r=("ip",), w=("i0",))
-    ts(1, ici[:, 1:2], T.ip[:], 31, A.bitwise_and, r=("ip",), w=("i1",))
-    ts(1, ici[:, 2:3], T.ip[:], 16, A.bitwise_and, r=("ip",), w=("i2",))
-    pc, pct = col(1, T.ip[:], 0.0, A.add, r=("ip",))
-    kc, kct = B("kc"), "kc"
-    cp(1, kc, ici[:, 0:1], r=("i0",), w=(kct,))
-    tgb, tgbt = col(1, kc, -1.0, A.mult, pc, A.add, r=(kct, pct))
-    tgc, tgct = col(1, tgb, 15.0, A.add, r=(tgbt,))
-    ts(144, B("red"), B("ia"), tgc, A.is_equal, 2.0, A.mult, r=("ia", tgct), w=("red",))
-    ts(144, B("reds"), B("ia"), tgc, A.is_equal, r=("ia", tgct), w=("reds",))
-    ts(128, B("t0"), B("bm"), -512.0, A.mult, 512.0, A.add, r=("bm",), w=("t0",))
-    tt(128, B("jj"), B("jj"), B("t0"), A.add, r=("jj", "t0"), w=("jj",))
-    ts(16, B("ek"), B("ia", 0, 16), kc, A.is_equal, r=("ia", kct), w=("ek",))
-    cp(16, B("j17", 0, 16), B("ia", 0, 16), r=("ia",), w=("j17",))
-    cp(1, B("j17", 16, 17), kc, r=(kct,), w=("j17k",))
-    JT = ("j17", "j17k")
+    for j, (sh, m) in enumerate(((0, 15), (0, 3), (2, 3), (0, 7), (5, 3), (5, 1), (4, 1), (6, 1))):
+        ts(1, ici[:, j:j + 1], T.ip[:], sh, A.arith_shift_right, m, A.bitwise_and, r=("ip",), w=("i%d" % j,))
+    cp(8, B("kf"), ici[:, 0:8], r=tuple("i%d" % j for j in range(8)), w=("kf",))
+    kc, cc, sd, i8, hb, gp, od, cpy = [B("kf", j, j + 1) for j in range(8)]
+    KF = ("kf",)
+    ts(128, B("dk"), I, kc, A.mult, 1184.0, A.mult, r=("idb", "kf"), w=("dk",))
+    tg, tgt = col(T.ip[:], kc, A.subtract, 16.0, A.add, r=("ip", "kf"))
+    ts(80, B("jr"), B("ia"), tg, A.subtract, r=("ia", tgt), w=("jr",))
+    ntm = [0]
 
-    def fn(dst, start, steps):
-        for q, (co, t) in enumerate(steps):
-            tmp = "q%d" % (q % 4)
-            ts(17, B(tmp), B("j17"), float(t), A.is_ge, float(co), A.mult, r=JT, w=(tmp,))
-            if q == 0 and start is None:
-                tt(17, B(dst), B("j17"), B(tmp), A.add, r=JT + (tmp,), w=(dst,))
-            elif q == 0:
-                ts(17, B(dst), B(tmp), float(start), A.add, r=(tmp,), w=(dst,))
-            else:
-                tt(17, B(dst), B(dst), B(tmp), A.add, r=(tmp, dst), w=(dst,))
+    def term(src, a, b_, r):
+        name = "tm%d" % ntm[0]
+        ntm[0] += 1
+        ts(80, B(name), B(src), a, A.subtract, b_, A.is_equal, r=(src,) + r, w=(name,))
+        return lambda d, n=128: (B(name, 16 - d, 16 - d + n), name)
+    pos = lambda x: (I, x[0], ("idb", x[1]))
+    neg = lambda x: (N_, x[0], ("nid", x[1]))
+    post = lambda x: (x[0], I, ("idb", x[1]))
+    negt = lambda x: (x[0], N_, ("nid", x[1]))
+    kt, ktt = col(cc, 4.0, A.mult, sd, A.add, r=KF)
+    z1, z1t = col(kt, 5.0, A.is_ge, 999.0, A.mult, r=(ktt,))
+    z2, z2t = col(kt, 11.0, A.is_ge, -995.0, A.mult, r=(ktt,))
+    Z = term("jr", z1, z2, (z1t, z2t))
+    n8, n8t = col(kc, 8.0, A.is_ge, -1.0, A.mult, r=KF)
+    v1, v1t = col(cc, 3.0, A.is_ge, 999.0, A.mult, r=KF)
+    v2, v2t = col(n8, -999.0, A.mult, v1, A.add, r=(n8t, v1t))
+    v3, v3t = col(sd, 4.0, A.mult, v2, A.add, r=("kf", v2t))
+    c1, c1t = col(cc, 1.0, A.is_ge, r=KF)
+    c2, c2t = col(cc, 2.0, A.is_ge, r=KF)
+    LO, HI, LO8, HI8 = [term("jr", a, b_, (at, bt)) for a, at, b_, bt in ((c2, c2t, v3, v3t), (c1, c1t, v3, v3t), (c2, c2t, v2, v2t), (c1, c1t, v2, v2t))]
+    summed("wz", 0, 128, 4, [[neg(Z(0)), neg(Z(1))], [pos(Z(1)), pos(Z(2))], [pos(LO(0)), neg(HI(1)), pos(LO8(8)), neg(HI8(9))]])
+    a1, a1t = col(i8, 7.0, A.is_ge, 999.0, A.mult, r=KF)
+    a2, a2t = col(i8, n8, A.subtract, r=("kf", n8t))
+    a3, a3t = col(kc, 7.0, A.is_ge, 999.0, A.mult, r=KF)
+    TA, TA2, TB = term("jr", i8, a1, ("kf", a1t)), term("jr", a2, a1, (a1t, a2t)), term("jr", kc, a3, ("kf", a3t))
+    summed("cat", 0, 128, 5, [[negt(TA(5)), post(TA2(6)), post(TA2(-1))], [negt(TB(5)), post(TB(8)), post(TB(1))]])
+    summed("ca", 0, 128, 6, [[pos(TA(5)), neg(TA2(6)), neg(TA2(-1))], [pos(TB(5)), neg(TB(8)), neg(TB(1))]])
+    summed("wt", 0, 256, 5, [[(B("lt"), B("cat"), ("lt", "cat"))]])
+    ts(16, B("ek"), B("ia", 0, 16), kc, A.is_equal, r=("ia", "kf"), w=("ek",))
+    two = B("two")
+    tt(2, two[:, 0:2], B("ek", 0, 3, 2), B("ek", 4, 7, 2), A.subtract, r=("ek",), w=("two0",))
+    tt(2, two[:, 2:4], B("ek", 4, 7, 2), B("ek", 8, 11, 2), A.subtract, r=("ek",), w=("two1",))
+    for j in range(2):
+        ts(1, two[:, 4 + j:5 + j], B("ek", 2 * j, 2 * j + 1), 2.0, A.mult, two[:, 2 + j:3 + j], A.add, r=("ek", "two1"), w=("two%d" % (2 + j),))
+        ts(64, B(("wl0", "wl2")[j]), B("bm"), two[:, j:j + 1], A.mult, r=("bm", "two0"), w=(("wl0", "wl2")[j],))
+        ts(64, B(("sp0", "sp2")[j]), B("bm"), two[:, 4 + j:5 + j], A.mult, r=("bm", "two%d" % (2 + j)), w=(("sp0", "sp2")[j],))
+    ts(64, B("wsn", 0, 128), B("bm"), n8, A.mult, r=("bm", n8t), w=("wsn",))
+    cp(64, B("wsn", 128, 192), B("wsn", 0, 64), r=("wsn",), w=("wsnx",))
+    op("pool", [lambda: g.affine_select(B("w5"), B("wsn", 0, 128), [[0, 8], [1, 16]], A.is_ge, 0.0, -5, 0)], 410, ("wsn",), ("w5",))
+    summed("mz", 0, 128, 7, [[pos((B("w5"), "w5")), pos((B(s), s))] for s in ("sp2", "sp0")])
+    b1, b1t = col(gp, 32.0, A.mult, 16.0, A.add, r=KF)
+    b2, b2t = col(cpy, 6.0, A.mult, b1, A.add, r=("kf", b1t))
+    b3, b3t = col(hb, 32.0, A.mult, 32.0, A.add, r=KF)
+    UA, UB, UC = term("ia", b2, 0.0, (b2t,)), term("ia", b2, 64.0, (b2t,)), term("ia", b3, 0.0, (b3t,))
+    ko, kot = col(kc, od, A.mult, r=KF)
+    ke, ket = col(kc, ko, A.subtract, r=("kf", kot))
+    ts(64, B("dke"), I, ke, A.mult, r=("idb", ket), w=("dke",))
+    ts(64, B("dko"), I, ko, A.mult, r=("idb", kot), w=("dko",))
+    summed("al", 0, 144, 7, [[(B(m), u(16, 144)[0], (m, u(0)[1])) for u in (UA, UB, UC)] for m in ("dke", "dko")])
+    summed("hm", 0, 64, 6, [[pos((B("idb", 64 * (j // 2), 64 * (j // 2) + 64), "idb"))] for j in range(4)])
+    k16, k16t = col(kc, 16.0, A.mult, r=KF)
+    k17, k17t = col(cpy, 1536.0, A.mult, k16, A.add, r=("kf", k16t))
+    for H in range(2):
+        cp(1, B("thf", 2 * H, 2 * H + 1), T.thi[:, 4 * H:4 * H + 1], r=("thi%d_0" % H, "thi%d_1" % H), w=("thf%d_0" % H,))
 
-    def both(name, out, n, in0, s1, o1, in1, s2, o2, mix, r):
-        ts(n, B("t0", 0, n), in0, s1, o1, r=r, w=("t0",))
-        ts(n, B("t1", 0, n), in1, s2, o2, r=r, w=("t1",))
-        tt(n, out, B("t0", 0, n), B("t1", 0, n), mix, r=("t0", "t1"), w=(name,))
+    first = [32 * c[0] for c in CH]
+    wid = [32 * len(c) for c in CH]
 
-    def signs(name, p, m):
-        both(name, B(name), 128, B("jj"), B(p, 16, 17), A.is_equal, B("jj"), B(m, 16, 17), A.is_equal, A.subtract, ("jj", p, m))
+    def tab(H, c, s, n=1, per=4):
+        lo = per * (TW * H + first[c]) + s * wid[c]
+        return slice(lo, lo + n * wid[c])
+    otok = lambda v, H, c, s: "off%d_%d_%d_%d" % (v, H, c, s)
+    for H in range(2):
+        for c in range(len(CH)):
+            for s in (0, 2, 1, 3):
+                lo = s * 192 + first[c]
+                cp(wid[c], T.off0[:, tab(H, c, s)], T["homi%d" % H][:, lo:lo + wid[c]], r=("homi%d_0" % H, "homi%d_1" % H), w=(otok(0, H, c, s),))
+    xt = lambda H: ("x%d" % H, "xl%d_0" % H, "xl%d_1" % H)
+    G = lambda s, H, p, lo=0, st=1: T["g%d_%d" % (s, H)][:, SUB * p + lo:SUB * p + SUB:st]
+    gt = lambda s, H, p: "g%d_%d_%d" % (s, H, p)
 
-    def window(name, p, m):
-        both("t2", B("t2", 0, 16), 16, B(p, 0, 16), kc, A.is_le, B(m, 0, 16), kc, A.is_gt, A.mult, (p, m, kct))
-        for q in range(8):
-            ts(16, B(name, 16 * q, 16 * q + 16), B("t2", 0, 16), B("bm", 16 * q, 16 * q + 1), A.mult, r=("t2", "bm"), w=(name if q == 7 else name + str(q),))
-    r5, r5t = col(1, kc, 5.0, A.is_ge, 9000.0, A.mult, r=(kct,))
-    zl, zlt = col(1, kc, 11.0, A.is_ge, -8997.0, A.mult, r=(kct,))
-    lo, lot = col(1, r5, zl, A.add, r=(r5t, zlt))
-    l1, l1t = col(1, lo, 1.0, A.add, r=(lot,))
-    l2, l2t = col(1, lo, 2.0, A.add, r=(lot,))
-    ts(128, B("t3"), B("jj"), l1, A.is_le, r=("jj", l1t), w=("t3",))
-    ts(128, B("t2"), B("jj"), lo, A.is_ge, -1.0, A.mult, r=("jj", lot), w=("t2",))
-    tt(128, B("wza"), B("t2"), B("t3"), A.mult, r=("t2", "t3"), w=("wza",))
-    both("wzb", B("wzb"), 128, B("jj"), l1, A.is_ge, B("jj"), l2, A.is_le, A.mult, ("jj", l1t, l2t))
-
-    def spread(name, terms):
-        c = ct = None
-        for co, t in terms:
-            if c is None:
-                c, ct = col(1, B("ek", t, t + 1), float(co), A.mult, r=("ek",))
-            else:
-                c, ct = col(1, B("ek", t, t + 1), float(co), A.mult, c, A.add, r=("ek", ct))
-        ts(128, B(name), B("bm"), c, A.mult, r=("bm", ct), w=(name,))
-    fn("f0", 0.0, ((1, 2), (2, 3), (1, 5), (99, 6)))
-    fn("f1", 1.0, ((1, 1), (2, 3), (1, 4), (99, 6)))
-    signs("wc", "f0", "f1")
-    ts(8, B("wc", 15, 128, 16), B("bm", 15, 128, 16), B("ek", 15, 16), A.mult, 2.0, A.mult, r=("bm", "ek", "wc"), w=("wc",))
-    spread("wl0", ((1, 0), (-1, 3)))
-    spread("wl2", ((1, 2), (-1, 5)))
-    for wname, cname, a0, p, m in (("wta", "ca", (5, 7), ((-5, 5), (-6, 11), (99, 15)), ((-6, 5), (-4, 11), (99, 15))),
-                                   ("wtb", "cb", (99, 103), ((-99, 5), (-3, 8), (-2, 10), (99, 11)), ((-99, 5), (-2, 8), (-1, 10), (99, 11)))):
-        for q, (dst, steps) in enumerate((("f2", p), ("f3", m))):
-            fn(dst, None, steps)
-            ts(17, B(dst), B(dst), float(a0[q]), A.add, r=(dst,), w=(dst,))
-        window(wname, "f2", "f3")
-        signs(cname, "f2", "f3")
-    tE, tEt = col(1, ici[:, 2:3], 999.0, A.mult, r=("i2",))
-    ta, tat = col(1, ici[:, 1:2], -1.0, A.mult, pc, A.add, r=("i1", pct))
-    te, tet = col(1, ta, tE, A.add, 3.0, A.add, r=(tat, tEt))
-    to, tot = col(1, tE, -1.0, A.mult, ta, A.add, r=(tEt, tat))
-    to, tot = col(1, to, 16 * 999.0 + 3.0, A.add, r=(tot,))
-    ts(131, B("ale"), B("ia", 0, 131), te, A.is_equal, kc, A.mult, r=("ia", tet, kct), w=("ale",))
-    ts(131, B("alo"), B("ia", 0, 131), to, A.is_equal, kc, A.mult, r=("ia", tot, kct), w=("alo",))
-    k16, k16t = col(1, kc, 16.0, A.mult, r=(kct,))
-    cp(128, B("idh"), B("idf"), r=("idf",), w=("idh",))
-    cp(128, B("ndh"), B("ndf"), r=("ndf",), w=("ndh",))
-    ts(128, B("i4h"), B("idf"), 4096.0, A.mult, r=("idf",), w=("i4h",))
-    k37, k37t = col(1, kc, 37.0, A.mult, r=(kct,))
-    ts(128, B("d37"), B("idf"), k37, A.mult, r=("idf", k37t), w=("d37",))
-    both("wr", B("wr"), 128, B("jj"), kc, A.is_ge, B("bm"), 1.0, A.mult, A.mult, ("jj", kct, "bm"))
-    ts(128, B("wrn"), B("wr"), -1.0, A.mult, r=("wr",), w=("wrn",))
-    fn("f4", None, ((-3, 3), (99, 6)))
-    ts(128, B("wp2"), B("jj"), B("f4", 16, 17), A.is_equal, r=("jj", "f4"), w=("wp2",))
-    spread("wsn", ((-1, 0), (-1, 1), (-1, 2)))
-    spread("bl0", ((1, 0),))
-    spread("bl2", ((1, 2),))
-    spread("br0", ((1, 3), (-1, 15)))
-    spread("br2", ((1, 5), (-1, 15)))
-    spread("b2k", ((2048, 15),))
-    cp(1, B("thf", 0, 1), T.thi[:], r=("thi",), w=("thf0",))
-
-    for c in range(NC):
-        for s in (2, 0, 3, 1):
-            cp(64, T.off0[:, c * 256 + s * 64:c * 256 + s * 64 + 64], T.homi[:, s * 192 + c * 64:s * 192 + c * 64 + 64], r=("homi",), w=("off0_%d_%d" % (c, s),))
-
-    def gather(v, c, s, h):
-        lo = c * 256 + s * 64 + h * 32
-        at = c * 1024 + h * HALF
-        out, in_ = T["g%d" % s][:, at:at + HALF], T.xs[:, 0:4096].indirect(T["off%d" % v][:, lo:lo + 32])
-        r, w = ("x0", "x1", "x2", "x3", "off%d_%d_%d" % (v, c, s)), ("g%d_%d_%d" % (s, c, h),)
-        if c == 0 and (s, h) in DG:
-            cp(0, out, in_, r=r, w=w, cost=60 + GAM * HALF)
+    def gather(v, H, c, p, s):
+        lo = tab(H, c, s).start + 32 * p - first[c]
+        in_ = T["xs%d" % H][:, 0:4096].indirect(T["off%d" % v][:, lo:lo + 32])
+        r, w = xt(H) + (otok(v, H, c, s),), (gt(s, H, p),)
+        sc = -1.0 if BYDMA(v, H, c) and s else 1.0
+        if BYVEC(v, H, p, s):
+            ts(0, G(s, H, p), in_, sc, A.mult, r=r, w=w, cost=55 + GAM * SUB)
         else:
-            act(0, out, in_, F.Copy, r=r, w=w, cost=70 + GAM * HALF)
-    uc = [0]
+            act(0, G(s, H, p), in_, F.Copy, scale=sc, r=r, w=w, cost=70 + GAM * SUB)
+    turn = {"f": 0, "d": 0, "t": 0}
 
-    def ufill(c, s, h):
-        bank = uc[0] % 3
-        uc[0] += 1
-        at = c * 1024 + h * HALF
-        mms(bank, 0, 512, [(B("idb"), T["g%d" % s][:, at:at + HALF], ("idb", "g%d_%d_%d" % (s, c, h)))])
-        return bank
+    def piece(v, H, c, p, C):
+        dn = turn["d"] % ND
+        turn["d"] += 1
+        D = lambda j, lo=0, st=1: T["d%d" % dn][:, SUB * j + lo:SUB * j + SUB:st]
+        dt = lambda j: "d%d_%d" % (dn, j)
+        todo = [10 - (1 if BYDMA(v, H, c) else 0), 0]
 
-    def pair(c, par, s, bank, name, h):
-        at = c * 1024 + h * HALF
-        tt(HALF, T["d%s_%d" % (name, par)][:, h * HALF:h * HALF + HALF], T["g%d" % s][:, at:at + HALF], pb[bank][:, 0:512], A.max,
-           r=("g%d_%d_%d" % (s, c, h),), w=("d%s_%d_%d" % (name, par, h),), b=(bank,))
+        def red(view, m, tok):
+            for k in range(4):
+                mm(SUMS, pb[SUMS][:, k:96:4], 64, [(view(k), m, (tok, "red"))], todo[1] == 0 and k == 0, todo[1] == todo[0] - 1 and k == 3)
+            todo[1] += 1
 
-    def red(par, name, bank, at, first, last):
-        d = T["d%s_%d" % (name, par)]
-        toks = ("red", "d%s_%d_0" % (name, par), "d%s_%d_1" % (name, par))
-        for q in range(2):
-            mms(bank, at, at + 64, [(B("red", 15 - k, 143 - k), d[:, k:1024:16], toks) for k in range(8 * q, 8 * q + 8)],
-                first and q == 0, last and q == 1)
+        def fills(terms):
+            bank = FILLS[turn["f"] % len(FILLS)]
+            turn["f"] += 1
+            mms(bank, 0, SUB, [(m, G(s, H, p), (mt, gt(s, H, p))) for m, mt, s in terms])
+            return bank
 
-    def add_up(v, c):
-        for j, (to_, s) in enumerate(((3, 2), (1, 0))):
-            toks = ["g%d_%d_%d" % (z, c, h) for z in (s, to_) for h in range(2)]
-            out, in_ = T["g%d" % to_][:, c * 1024:c * 1024 + 1024], T["g%d" % s][:, c * 1024:c * 1024 + 1024]
-            op("pool", [(lambda o_, i_: lambda: g.dma_start(out=o_, in_=i_, accum_op=A.add))(out, in_)], 1000.0, toks, toks[2:],
-               ext=("ds%d_%d_%d" % (v, c, j), 16), lat=3500.0)
+        def pair(j, s, bank, m):
+            tt(SUB, D(j), G(s, H, p), pb[bank][:, 0:SUB], A.max, r=(gt(s, H, p),), w=(dt(j),), b=(bank,))
+            red(lambda k: D(j, k, 4), m, dt(j))
 
-    def total(c, bk):
-        for q, s in enumerate((3, 1)):
-            for e in range(2):
-                mms(bk, 384, 448, [(B("reds", 15 - k, 143 - k), T["g%d" % s][:, c * 1024 + k:c * 1024 + 1024:16],
-                                    ("reds", "g%d_%d_0" % (s, c), "g%d_%d_1" % (s, c))) for k in range(8 * e, 8 * e + 8)], q + e == 0, q + e == 2)
-
-    def main(v, c):
-        par = (v * NC + c) % 2
-        u2 = [ufill(c, 2, 0), ufill(c, 2, 1)]
-        pair(c, par, 0, u2[0], "02", 0)
-        pair(c, par, 0, u2[1], "02", 1)
-        red(par, "02", 4, 0, True, False)
-        pair(c, par, 3, u2[0], "23", 0)
-        pair(c, par, 3, u2[1], "23", 1)
-        red(par, "23", 5, 0, True, False)
-        u3 = [ufill(c, 3, 0)]
-        pair(c, par, 0, u3[0], "03", 0)
-        u3.append(ufill(c, 3, 1))
-        pair(c, par, 0, u3[1], "03", 1)
-        pair(c, par, 1, u3[0], "13", 0)
-        pair(c, par, 1, u3[1], "13", 1)
-        red(par, "13", 4, 0, False, True)
-        u1 = [ufill(c, 1, 0)]
-        pair(c, par, 0, u1[0], "01", 0)
-        u1.append(ufill(c, 1, 1))
-        pair(c, par, 0, u1[1], "01", 1)
-        red(par, "01", 5, 0, False, True)
-        m1 = "m1_%d" % c
-        act(64, B(m1), pb[4][:, 0:64], F.Copy, w=(m1,), b=(4,))
-        red(par, "03", 4, 64, True, False)
-        tt(64, B("ab_%d" % c, 0, 64), pb[5][:, 0:64], B(m1), A.subtract, r=(m1,), w=("a_%d" % c,), b=(5,))
-        pair(c, par, 2, u1[0], "12", 0)
-        pair(c, par, 2, u1[1], "12", 1)
-        red(par, "12", 4, 64, False, True)
-        tt(64, B("ab_%d" % c, 64, 128), pb[4][:, 64:128], B(m1), A.subtract, r=(m1,), w=("b_%d" % c,), b=(4,))
-        add_up(v, c)
-
-    def crit(v, c):
-        bk = 6
-        n = lambda s: "%s_%d" % (s, c)
-        mms(bk, 0, 64, [(B("wza"), B(n("ab"), 0, 64), ("wza", n("a"))), (B("wzb"), B(n("ab"), 64, 128), ("wzb", n("b")))])
-        act(64, B(n("u")), pb[bk][:, 0:64], F.Sign, 0.5, w=(n("u"),), b=(bk,))
-        mms(bk, 64, 128, [(B("wc"), B(n("u")), ("wc", n("u")))])
-        act(64, B(n("o")), pb[bk][:, 64:128], F.Relu, -1.0, w=(n("o"),), b=(bk,))
-        mms(bk, 128, 192, [(B("wl0"), B(n("o")), ("wl0", n("o")))])
-        mms(bk, 192, 256, [(B("wl2"), B(n("o")), ("wl2", n("o")))])
-        tt(128, B(n("y")), B(n("ab")), pb[bk][:, 128:256], A.mult, r=(n("a"), n("b")), w=(n("y"),), b=(bk,))
-        for q, m in enumerate(("wta", "wtb")):
-            mt = tuple([m] + [m + str(e) for e in range(7)])
-            mms(bk, 256 + 64 * q, 320 + 64 * q, [(B(m), B(n("y"), 0, 64), mt + (n("y"),)), (B(m), B(n("y"), 64, 128), mt + (n("y"),))])
-        act(128, B(n("tu")), pb[bk][:, 256:384], F.Sign, 0.5, w=(n("tu"),), b=(bk,))
-        mms(bk, 384, 448, [(B("ca"), B(n("tu"), 0, 64), ("ca", n("tu"))), (B("cb"), B(n("tu"), 64, 128), ("cb", n("tu")))])
-        act(64, B(n("om")), pb[bk][:, 384:448], F.Relu, -5.0, w=(n("om"),), b=(bk,))
-        for q, m in enumerate(("ale", "alo")):
-            mms(bk, 448 + 16 * q, 464 + 16 * q, [(B("rw")[0:1, :], B("onb", 0, 16)[0:1, :], ("rw", "onb"))] +
-                [(B(m, 3 - r, 131 - r), B(n("om"), 16 * r, 16 * r + 16), (m, n("om"))) for r in range(4)])
-        op("dve", [lambda: g.vector.transpose(out=B(n("lt")), in_=pb[bk][:, 448:480])], 64, (), (n("lt"),), (bk,))
-        li, lit = T.lists[:, 4 * c:4 * c + 4], n("li")
-        ts(4, li, B(n("lt"), 0, 4), k16, A.add, r=(n("lt"), k16t), w=(lit,))
-        gr = (lit, "g0_%d_0" % c, "g0_%d_1" % c)
-        if c < NC - 1:
-            act(64, B(n("gs")), T.g0[:, c * 1024:c * 1024 + 1024].indirect(li), F.Copy, r=gr, w=(n("gs"),), cost=75 + 64 * GAM)
+        def strand(s, m):
+            red(lambda k: G(s, H, p, k, 4), m, gt(s, H, p))
+        if BYDMA(v, H, c):
+            u = fills([(I, "idb", 2)])
+            for j, (s, m) in enumerate(((2, RC), (1, RA), (3, RB))):
+                ts(SUB // 2, D(j), G(s, H, p), 0.0, A.max, r=(gt(s, H, p),), w=(dt(j),))
+                red(lambda k: D(j, k, 4), m, dt(j))
+                strand(s, RS)
+            pair(3, 1, u, RB)
+            u1 = fills([(I, "idb", 1)])
+            pair(4, 3, u, RA)
+            pair(5, 3, u1, RC)
         else:
-            cp(64, B(n("gs")), T.g0[:, c * 1024:c * 1024 + 1024].indirect(li), r=gr, w=(n("gs"),), cost=60 + 64 * GAM)
-        tt(64, B(n("ts")), T.xs[:, c * 1024:c * 1024 + 1024].indirect(li), B(n("gs")), A.add, r=(lit, n("gs"), "x%d" % c), w=(n("ts"),), cost=60 + 64 * GAM)
-        ts(64, B(n("tq")), B(n("ts")), 0.5, A.mult, 191.75, A.add, r=(n("ts"),), w=(n("tq"),))
-
-    def scatter(c):
-        tt(64, T.xs[:, c * 1024:c * 1024 + 1024].indirect(T.lists[:, 4 * c:4 * c + 4]), B("tq_%d" % c), B("m192"), A.add,
-           r=("tq_%d" % c, "m192", "li_%d" % c), w=("x%d" % c,), cost=60 + 64 * SCA)
-
-    def upd(v, c):
-        bk, bz = 7, 3
-        n = lambda s: "%s_%d" % (s, c)
-        st, stt = B(n("st")), n("st")
-        i16, n16, ib = B("idh"), B("ndh"), B("idb")
-        ts(256, st, T["off%d" % v][:, c * 256:c * 256 + 256], -2048.0, A.add, r=tuple("off%d_%d_%d" % (v, c, s) for s in range(4)), w=(stt,))
-        mms(bz, 448, 512, [(B("wp2"), B(n("o")), ("wp2", n("o")))])
-        act(64, B(n("same")), pb[bz][:, 448:512], F.Relu, -1.0, accum=B("acc", c, c + 1), w=(n("same"), "acc%d" % c), b=(bz,))
-        o, om = B(n("o")), B(n("om"))
-        for q, (m, w) in enumerate((("bl0", "wrn"), ("br0", "wr"), ("bl2", "wrn"), ("br2", "wr"))):
-            mms(bk, 64 * q, 64 * q + 64, [(B(m), o, (m, n("o"))), (B(w), om, (w, n("om")))])
-        mms(bk, 256, 320, [(B("wr"), om, ("wr", n("om"))), (B("wsn"), B(n("same")), ("wsn", n("same")))])
-        xr = n("xr")
-        act(320, B(xr), pb[bk][:, 0:320], F.Relu, w=(xr,), b=(bk,))
-        for q in range(4):
-            a = q // 2 * 128
-            mms(bz, 64 * q, 64 * q + 64, [(ib, B(xr, a, a + 64), ("idb", xr)), (ib, B(xr, a + 64, a + 128), ("idb", xr))])
-        fs = n("fs")
-        total(c, 5)
-        tt(64, B(n("c1")), B(n("m1")), pb[5][:, 384:448], A.subtract, r=(n("m1"),), w=(n("c1"),), b=(5,))
-        tt(128, B(fs, 0, 128), B(stt, 64, 192), pb[bz][:, 0:128], A.mult, r=(stt,), w=(fs,), b=(bz,))
-        tt(128, B(fs, 128, 256), B(stt, 128, 256), pb[bz][:, 128:256], A.mult, r=(stt,), w=(fs + "x",), b=(bz,))
-        tt(128, B(n("zz")), B(n("ab")), pb[bz][:, 64:192], A.mult, r=(n("a"), n("b")), w=(n("zz"),), b=(bz,))
-        act(128, B(n("fb")), pb[bz][:, 64:192], F.Copy, w=(n("fb"),), b=(bz,))
-        mms(5, 384, 448, [(i16, B(n("c1")), ("idh", n("c1"))), (i16, B(n("zz"), 0, 64), ("idh", n("zz"))), (i16, B(n("zz"), 64, 128), ("idh", n("zz")))])
-        ts(64, B(n("vv")), pb[5][:, 384:448], B("thf", v % 2, v % 2 + 1), A.is_gt, r=("thf%d" % (v % 2),), w=(n("vv"),), b=(5,))
-        f1, f2, h2, h3 = B(fs, 0, 64), B(fs, 64, 128), B(fs, 128, 192), B(fs, 192, 256)
-        s0, s1, s2, s3 = [B(stt, 64 * q, 64 * q + 64) for q in range(4)]
-        FT = ("idh", "ndh", stt, fs, fs + "x")
-        mms(bk, 320, 384, [(i16, s1, FT), (n16, f1, FT), (i16, f2, FT)])
-        cp(64, B(n("src"), 0, 64), pb[bk][:, 320:384], w=(n("src"),), b=(bk,))
-        k2 = (B("b2k"), o, ("b2k", n("o")))
-        qt = [(i16, s2, FT), (i16, f1, FT), (n16, f2, FT), (i16, h3, FT), (n16, h2, FT), k2]
-        tq = [(i16, s3, FT), (n16, h3, FT), (i16, h2, FT), k2]
-        mms(bk, 0, 64, qt)
-        mms(bk, 64, 128, tq)
-        vv = (B(n("vv")), ("idh", "d37", n("vv")))
-        v4 = (B("i4h"), B(n("vv")), ("i4h", n("vv")))
-        mms(bz, 128, 192, [(i16, s0, FT), v4])
-        mms(bz, 192, 256, [(i16, B(n("src"), 0, 64), ("idh", n("src"))), v4])
-        act(128, B(n("sr")), pb[bz][:, 128:256], F.Relu, b=(bz,), bias=-2048.0, w=(n("sr"),))
-        mms(bz, 256, 320, qt + [(B("d37"),) + vv])
-        mms(bz, 320, 384, tq + [(B("d37"),) + vv])
-        tt(128, B(n("pp")), B(n("sr")), pb[bk][:, 0:128], A.mult, r=(n("sr"),), w=(n("pp"),), b=(bk,))
-        ts(128, B(n("qq")), B(n("pp")), 5, A.arith_shift_right, r=(n("pp"),), w=(n("qq"),))
-        tt(128, B(n("ui")), B(n("qq")), pb[bz][:, 256:384], A.add, r=(n("qq"),), w=(n("ui"),), b=(bz,))
+            ab = BYABS(v, H, p)
+            u0 = fills([(I, "idb", 0)])
+            strand(0, RS)
+            pair(0, 2, u0, RC)
+            u2 = fills([(I, "idb", 2)])
+            strand(2, RS)
+            pair(1, 1, u0, RA)
+            pair(2, 1, u2, RB)
+            strand(1, RE if ab else RS)
+            pair(3, 3, u0, RB)
+            u1 = fills([(I, "idb", 1)] + ([(N_, "nid", 3)] if ab else []))
+            pair(4, 3, u2, RA)
+            strand(3, RE if ab else RS)
+            if ab:
+                act(SUB, D(5), pb[u1][:, 0:SUB], F.Abs, w=(dt(5),), b=(u1,))
+                red(lambda k: D(5, k, 4), RD, dt(5))
+            else:
+                pair(5, 3, u1, RC)
+        ct = "ct%d" % (turn["t"] % NT)
+        turn["t"] += 1
+        cp(96, B(ct, 3, 387, 4), pb[SUMS][:, 0:96], w=(ct,), b=(SUMS,))
         for q in range(3):
-            mms(bk, 64 * q, 64 * q + 64, [(ib, B(xr, 256, 320), ("idb", xr))])
-        ts(128, B(n("nb")), B(n("ui")), 4095, A.bitwise_and, r=(n("ui"),), w=(n("nb"),))
-        ps = n("ps")
-        ts(128, B(n("src"), 64, 192), B(n("nb")), -2048.0, A.add, r=(n("nb"),), w=(n("src") + "x",))
-        tt(64, B(ps, 0, 64), s0, pb[bk][:, 0:64], A.mult, r=(stt,), w=(ps,), b=(bk,))
-        tt(192, B(ps, 64, 256), B(n("src")), pb[bk][:, 0:192], A.mult, r=(n("src"), n("src") + "x"), w=(ps + "x",), b=(bk,))
-        r0, a1, b1 = [B(n("src"), 64 * q, 64 * q + 64) for q in range(3)]
-        e0, er, ea, eb = [B(ps, 64 * q, 64 * q + 64) for q in range(4)]
-        gd = n("gd")
-        SX = ["idh", "ndh", n("src"), n("src") + "x", ps, ps + "x", stt]
-        pos = lambda x: (i16, x, tuple(SX))
-        neg = lambda x: (n16, x, tuple(SX))
-        nq, nr, nt = [pos(a1), neg(ea), pos(e0)], [pos(r0), neg(er), pos(eb)], [pos(b1), neg(eb), pos(er)]
-        mms(bz, 192, 256, nq)
-        mms(bz, 256, 320, nr)
-        mms(bz, 320, 384, nt)
-        tt(64, B(gd, 0, 64), B(n("fb"), 0, 64), pb[bz][:, 192:256], A.mult, r=(n("fb"),), w=(gd,), b=(bz,))
-        tt(64, B(gd, 64, 128), B(n("fb"), 64, 128), pb[bz][:, 192:256], A.mult, r=(n("fb"),), w=(gd + "x",), b=(bz,))
-        tt(128, B(gd, 128, 256), B(n("fb")), pb[bz][:, 256:384], A.mult, r=(n("fb"),), w=(gd + "y",), b=(bz,))
-        SX += [gd, gd + "x", gd + "y"]
-        q1, q3, p1, p3 = [B(gd, 64 * q, 64 * q + 64) for q in range(4)]
-        mms(bk, 0, 64, [pos(s0), neg(e0), pos(ea)])
-        mms(bk, 64, 128, nr + [neg(p1), pos(q1)])
-        mms(bk, 128, 192, nq + [neg(q1), pos(p1), neg(q3), pos(p3)])
-        mms(bk, 192, 256, nt + [neg(p3), pos(q3)])
-        snd, sdt = T["snd%d" % v], "snd%d_%d" % (v, c)
+            lo = q * wid[c] + 32 * p - first[c]
+            mms(C, lo, lo + 32, [(B(ct, 3 - h + 128 * q, 131 - h + 128 * q), B("sel", 32 * h, 32 * h + 32), (ct, "sel")) for h in range(4)])
+
+    def chunk(v, H, c, k):
+        C, U, w = CRIT[k % len(CRIT)], UPD[k % len(UPD)], wid[c]
+        n = lambda s: "%s_%d" % (s, k % NW)
+        P = lambda s, a, b_=None: B(n(s), a * w, (a + 1 if b_ is None else b_) * w)
+        pc = lambda a, b_: pb[C][:, a * w:b_ * w]
+        pu = lambda a, b_: pb[U][:, a * w:b_ * w]
+        mc = lambda a, b_, terms: mms(C, a * w, b_ * w, terms)
+        mu = lambda a, b_, terms, start=False, stop=False: mms(U, a * w, b_ * w, terms, start, stop)
+        up = lambda s, a, b_=None: (I, P(s, a, b_), ("idb", n(s)))
+        dn = lambda s, a, b_=None: (N_, P(s, a, b_), ("nid", n(s)))
+        lab[0] = "c"
+        cp(3 * w, P("ab", 0, 3), pc(0, 3), w=(n("ab"),), b=(C,))
+        mc(3, 4, [(B("wz", 128 * q, 128 * q + 128), P("ab", q), ("wz", n("ab"))) for q in range(2)])
+        act(w, P("u", 0), pc(3, 4), F.Sign, 0.5, w=(n("u"),), b=(C,))
+        mc(4, 5, [(B("wz", 256, 384), P("u", 0), ("wz", n("u")))])
+        at = "acc%d_%d" % (H, c)
+        act(w, P("o", 0), pc(4, 5), F.Relu, n8, 0.5, accum=B("acc", 4 * H + c, 4 * H + c + 1), r=(n8t,), w=(n("o"), at), b=(C,))
+        o = P("o", 0)
+        mc(5, 6, [(B("wl0"), o, ("wl0", n("o")))])
+        mc(6, 7, [(B("wl2"), o, ("wl2", n("o")))])
+        tt(2 * w, P("y", 0, 2), P("ab", 0, 2), pc(5, 7), A.mult, r=(n("ab"),), w=(n("y"),), b=(C,))
+        for q in range(2):
+            m = B("wt", 128 * q, 128 * q + 128)
+            mc(q, q + 1, [(m, B("teps", 0, w), ("wt", "teps")), (m, P("y", 0), (n("y"),)), (m, P("y", 1), (n("y"),))])
+        act(2 * w, P("tu", 0, 2), pc(0, 2), F.Sign, w=(n("tu"),), b=(C,))
+        mc(2, 3, [(B("ca", 128 * q, 128 * q + 128), P("tu", q), ("ca", n("tu"))) for q in range(2)])
+        om, omt = B("om%d" % H, first[c], first[c] + w), "om%d_%d" % (H, c)
+        act(w, om, pc(2, 3), F.Relu, -5.0, w=(omt,), b=(C,))
+        lab[0] = "u"
+        ts(2 * w, P("st", 0, 4), T["off%d" % v][:, tab(H, c, 0, 4)], -2048.0, A.add, r=tuple(otok(v, H, c, s) for s in range(4)), w=(n("st"),))
+        mu(0, 3, [up("st", 0, 3)], True, True)
+        gm = (B("wr"), om, ("wr", omt))
+        mc(0, 1, [(B("pi"), P("ab", 1), ("pi", n("ab")))])
+        mc(1, 2, [(B("pi"), P("ab", 0), ("pi", n("ab")))])
+        for q in range(2):
+            mc(3 + q, 4 + q, [(B("mz", 128 * q, 128 * q + 128), o, ("mz", n("o"))), gm])
+        for q in range(2):
+            mc(5 + q, 6 + q, [(B("w5"), o, ("w5", n("o"))), gm])
+        pm = P("pm", 0, 2)
+        ts(2 * w, pm, pc(3, 5), 2.0, A.is_equal, w=(n("pm"),), b=(C,))
+        tt(2 * w, P("zz", 0, 2), pm, pc(0, 2), A.mult, r=(n("pm"),), w=(n("zz"),), b=(C,))
+        mc(2, 3, [(B("pi"), P("ab", 2), ("pi", n("ab"))), up("zz", 0), up("zz", 1)])
+        th = "thf%d_%d" % (H, v % 2)
+        ts(w, P("vv", 0), pc(2, 3), B("thf", 2 * H + v % 2, 2 * H + v % 2 + 1), A.is_gt, r=(th,), w=(n("vv"),), b=(C,))
+        tt(2 * w, P("f1", 0, 2), pm, pb[U][:, 0:2 * w], A.mult, r=(n("pm"),), w=(n("f1"),), b=(U,))
+        tt(2 * w, P("f2", 0, 2), pm, pu(1, 3), A.mult, r=(n("pm"),), w=(n("f2"),), b=(U,))
+        mu(3, 6, [up("st", 0, 3)], True, False)
+        mu(3, 5, [up("f2", 0, 2), dn("f1", 0, 2)], False, False)
+        mu(4, 6, [up("f1", 0, 2), dn("f2", 0, 2)], False, True)
+        act(3 * w, P("am", 0, 3), pu(3, 6), F.Copy, w=(n("am"),), b=(U,))
+        vv = P("vv", 0)
+        mu(6, 8, [(I, B("t2k", 0, 2 * w), ("idb", "t2k"))], True, False)
+        mu(7, 8, [up("st", 3)], False, False)
+        mu(6, 7, [up("am", 2)], False, False)
+        mu(0, 2, [up("am", 0, 2)], False, False)
+        for q in range(2):
+            mu(q, q + 1, [(B("i4k"), vv, ("i4k", n("vv")))], False, q == 1)
+        act(2 * w, P("sr", 0, 2), pu(0, 2), F.Relu, -2048.0, w=(n("sr"),), b=(U,))
+        big = (I, B("tbig", 0, w), ("idb", "tbig"))
+        dk = (B("dk"), vv, ("dk", n("vv")))
+        mc(3, 4, [big, (B("i32"), P("am", 2), ("i32", n("am"))), dk])
+        mc(4, 5, [big, (B("i32"), P("st", 3), ("i32", n("st"))), dk])
+        tt(2 * w, P("e1", 0, 2), P("am", 0, 2), pc(5, 7), A.mult, r=(n("am"),), w=(n("e1"),), b=(C,))
+        tt(2 * w, P("pp", 0, 2), P("sr", 0, 2), pu(6, 8), A.mult, r=(n("sr"),), w=(n("pp"),), b=(U,))
+        tt(2 * w, P("ui", 0, 2), P("pp", 0, 2), pc(3, 5), A.add, r=(n("pp"),), w=(n("ui"),), b=(C,))
+        ts(2 * w, P("nb", 0, 2), P("ui", 0, 2), 5, A.arith_shift_right, 4095, A.bitwise_and, r=(n("ui"),), w=(n("nb"),))
+        ts(2 * w, P("src", 0, 2), P("nb", 0, 2), -2048.0, A.add, r=(n("nb"),), w=(n("src"),))
+        tt(2 * w, P("e2", 0, 2), P("src", 0, 2), pc(5, 7), A.mult, r=(n("src"),), w=(n("e2"),), b=(C,))
+        low = [up("am", 0, 2), dn("e1", 0, 2), up("e2", 0, 2)]
+        mu(4, 6, low[:2], True, False)
+        mu(6, 7, [up("e1", 0), up("src", 0), dn("e2", 0)], False, False)
+        mu(4, 6, low[2:], False, True)
+        tt(2 * w, P("g1", 0, 2), pm, pu(4, 6), A.mult, r=(n("pm"),), w=(n("g1"),), b=(U,))
+        tt(2 * w, P("g2", 0, 2), pm, pu(5, 7), A.mult, r=(n("pm"),), w=(n("g2"),), b=(U,))
+        mu(0, 2, low, True, False)
+        mu(2, 4, [up("e1", 0, 2), up("src", 0, 2), dn("e2", 0, 2)], False, False)
+        mu(0, 2, [up("g2", 0, 2), dn("g1", 0, 2)], False, False)
+        mu(1, 3, [up("g1", 0, 2), dn("g2", 0, 2)], False, True)
+        snd, sdt, ysb = T["snd%d" % v], "snd%d_%d_%d" % (v, H, c), T["ysb%d" % H]
         if v < VI - 1:
-            ts(192, snd[:, c * 192:c * 192 + 192], pb[bk][:, 64:256], 2048.0, A.add, w=(sdt,), b=(bk,))
-            nxt = "off%d" % (v + 1)
-            ts(64, T[nxt][:, c * 256:c * 256 + 64], pb[bk][:, 0:64], 2048.0, A.add, w=("%s_%d_0" % (nxt, c),), b=(bk,))
+            ts(3 * w, snd[:, tab(H, c, 0, 3, 3)], pu(1, 4), 2048.0, A.add, w=(sdt,), b=(U,))
+            ts(w, T["off%d" % (v + 1)][:, tab(H, c, 0)], pu(0, 1), 2048.0, A.add, w=(otok(v + 1, H, c, 0),), b=(U,))
         else:
-            act(192, snd[:, c * 192:c * 192 + 192], pb[bk][:, 64:256], F.Identity, 2048.0, w=(sdt,), b=(bk,))
-            act(64, T.ysb[:, c * 64:c * 64 + 64], pb[bk][:, 0:64], F.Identity, 2048.0, w=("off%d_%d_0" % (VI, c),), b=(bk,))
+            act(3 * w, snd[:, tab(H, c, 0, 3, 3)], pu(1, 4), F.Identity, 2048.0, w=(sdt,), b=(U,))
+            act(w, ysb[:, first[c]:first[c] + w], pu(0, 1), F.Identity, 2048.0, w=(otok(VI, H, c, 0),), b=(U,))
         tr = []
         for s in (1, 2, 3):
             dst = T.cores[(rank + STEP[s]) % len(T.cores)]
             rid, pid, _ = topo.addr(dst)
             e = topo.engines(core, dst)
             if v < VI - 1:
-                land = T["off%d" % (v + 1)][:, c * 256 + s * 64:c * 256 + s * 64 + 64]
+                land = T["off%d" % (v + 1)][:, tab(H, c, s)]
             else:
-                land = T.ysb[:, s * 192 + c * 64:s * 192 + c * 64 + 64]
+                land = ysb[:, s * TW + first[c]:s * TW + first[c] + w]
             tr.append(RemoteDMATransfer(dst_ids=[DstId(rid=rid, pnc=pid)], dma_engine_mask=(1 << e[2 * s - 2]) | (1 << e[2 * s - 1]),
-                                        remote_sem=T.sem["arr%d_%d" % (v, c)], src=snd[:, (c * 3 + s - 1) * 64:(c * 3 + s) * 64], dst=land))
+                                        remote_sem=T.sem["arr%d_%d" % (v, k % (2 * len(CH)))], src=snd[:, tab(H, c, s - 1, 1, 3)], dst=land))
         op("pool", [lambda: g.remote_dma_fused(tr, local_sem=T.sem.sent)], 1000.0, (sdt,), ("go",), ext="send")
-        op(None, [], 0.0, ("go",), tuple("off%d_%d_%d" % (v + 1, c, s) for s in (1, 2, 3)), ext=("arr%d_%d" % (v, c), 6), lat=NET)
-        if c == NC - 1 and v < VI - 1:
-            cp(4, T.accb[:, 0:3], B("acc", 0, 3), r=("acc0", "acc1", "acc2"), w=("accb",))
-            mms(bk, 0, 1, [(B("wsn"), T.accb[:, q:q + 1], ("wsn", "accb")) for q in range(3)])
-            cp(1, ici[:, 3:4], pb[bk][:, 0:1], w=("i3",), b=(bk,))
-            ts(1, ici[:, 4:5], ici[:, 3:4], 31, A.bitwise_and, r=("i3",), w=("i4",))
-            w = (v + 1) % 2
-            tt(1, B("thf", w, w + 1), ici[:, 4:5], T.thi[:], A.add, r=("i4", "thi"), w=("thf%d" % w,))
+        op(None, [], 0.0, ("go",), tuple(otok(v + 1, H, c, s) for s in (1, 2, 3)), ext=("arr%d_%d" % (v, k % (2 * len(CH))), 6), lat=NET)
 
+    def blend(v, H, k):
+        C, xs, li = CRIT[k % len(CRIT)], T["xs%d" % H], T["lists%d" % H]
+        lab[0] = "b"
+        oms = tuple("om%d_%d" % (H, c) for c in range(len(CH)))
+        for e in range(2):
+            mms(C, 480 + 16 * e, 496 + 16 * e, [(B("rw")[0:1, :], B("onb", 0, 16)[0:1, :], ("rw", "onb"))] +
+                [(B("al", 144 * e + 16 - r, 144 * e + 144 - r), B("om%d" % H, 16 * r, 16 * r + 16), ("al",) + oms) for r in range(6)])
+        lt, ltt, lit = B("lt32", 32 * H, 32 * H + 32), "lt32_%d" % H, "li%d" % H
+        op("dve", [lambda: g.vector.transpose(out=lt, in_=pb[C][:, 480:512])], FIX + 64 * CY, (), (ltt,), (C,))
+        ts(22, li[:, 0:22], lt[:, 0:22], k16, A.add, r=(ltt, k16t), w=(lit,))
+        ts(6, li[:, 24:30], lt[:, 16:22], k17, A.add, r=(ltt, k17t), w=(lit + "x",))
+        gs, gx, tq = ["%s%d" % (s, H) for s in ("gs", "gx", "tq")]
+        act(0, B(gs), T["g0_%d" % H][:, 0:1536].indirect(li[:, 16:22]), F.Copy, r=(lit,) + tuple(gt(0, H, p) for p in range(3)), w=(gs,), cost=70 + TW * GAM)
+        act(0, B(gx), xs[:, 0:3072].indirect(li[:, 24:30]), F.Copy, r=(lit + "x",) + xt(H), w=(gx,), cost=70 + TW * GAM)
+        at = 0 if wid[-1] == 64 else 256
+        last = v == VI - 1
+        if last:
+            mms(C, at, at + TW, [(I, B(s), ("idb", s)) for s in (gs, gx)])
+        else:
+            for c in range(2):
+                mms(C, at + TW * c, at + TW * c + TW, [(B("hm", 128 * c, 128 * c + 128), B(s), ("hm", s)) for s in (gs, gx)])
+        nn = TW if last else 2 * TW
+        act(nn, B(tq, 0, nn), pb[C][:, at:at + nn], F.Identity, 191.75, 0.5, w=(tq,), b=(C,))
+        tt(0, xs[:, 0:3072].indirect(li[:, 24:30] if last else li[:, 0:12]), B(tq, 0, nn), B("m192", 0, nn), A.add,
+           r=(tq, "m192", lit, lit + "x"), w=("x%d" % H,), cost=55 + nn * SCA)
+        if last:
+            for c in range(2):
+                dma("sp", T.yx[64 * H:64 * H + 64, 1536 * c:1536 * c + 1536], xs[64 * c:64 * c + 64, 1536 * c:1536 * c + 1536], "dout", ("x%d" % H,))
+            return
+        nc, ab = len(CH), "accb%d" % H
+        cp(4, B(ab, 0, nc), B("acc", 4 * H, 4 * H + nc), r=tuple("acc%d_%d" % (H, c) for c in range(nc)), w=(ab,))
+        mms(C, 479, 480, [(B("wsn", 64 * e, 64 * e + 128), B(ab, q, q + 1), ("wsn", "wsnx", ab)) for q in range(nc) for e in range(2)])
+        cp(1, ici[:, 8 + 2 * H:9 + 2 * H], pb[C][:, 479:480], w=("ia%d" % H,), b=(C,))
+        ts(1, ici[:, 9 + 2 * H:10 + 2 * H], ici[:, 8 + 2 * H:9 + 2 * H], 31, A.bitwise_and, r=("ia%d" % H,), w=("ib%d" % H,))
+        w = (v + 1) % 2
+        tt(1, B("thf", 2 * H + w, 2 * H + w + 1), ici[:, 9 + 2 * H:10 + 2 * H], T.thi[:, 4 * H:4 * H + 1], A.add, r=("ib%d" % H, "thi%d_0" % H, "thi%d_1" % H), w=("thf%d_%d" % (H, w),))
+
+    k = 0
     for v in range(VI):
-        for c in range(NC):
-            lab[0] = "g%d" % c
-            for s, h in GORDER:
-                gather(v, c, s, h)
-        for c in range(NC):
-            lab[0] = "m%d" % c
-            main(v, c)
-            lab[0] = "c%d" % c
-            crit(v, c)
-            scatter(c)
-            lab[0] = "u%d" % c
-            if v == VI - 1:
-                dma("sp", g.sync, T.yx[:, 1024 * c:1024 * c + 1024], T.xs[:, 1024 * c:1024 * c + 1024], ("dy0", "dy1", "dy3")[c], ("x%d" % c,))
-            upd(v, c)
-        if v == 0:
-            dma("sp", g.sync, T.yx[:, 3072:4096], T.xs[:, 3072:4096], "dy2", ("x3",))
-    dma("sp", g.sync, T.ys[:], T.ysb[:], "dys", tuple("off%d_%d_%d" % (VI, c, s) for c in range(NC) for s in range(4)))
+        for H in range(2):
+            for c, ps in enumerate(CH):
+                lab[0] = "g"
+                for p in ps:
+                    for s in (0, 2, 1, 3):
+                        gather(v, H, c, p, s)
+                if BYDMA(v, H, c):
+                    for j, s in enumerate((2, 1, 3)):
+                        cols = slice(SUB * ps[0], SUB * ps[-1] + SUB)
+                        mine = tuple(gt(s, H, p) for p in ps)
+                        op("pool", [(lambda o_, i_: lambda: g.dma_start(out=o_, in_=i_, accum_op=A.add))(T["g%d_%d" % (s, H)][:, cols], T["g0_%d" % H][:, cols])],
+                           1000.0, mine + tuple(gt(0, H, p) for p in ps), mine, ext=("ds%d_%d_%d" % (v, H * len(CH) + c, j), 16), lat=3500.0)
+                lab[0] = "m"
+                for p in ps:
+                    piece(v, H, c, p, CRIT[k % len(CRIT)])
+                chunk(v, H, c, k)
+                if c == len(CH) - 1:
+                    blend(v, H, k)
+                k += 1
+            if v == 0:
+                dma("sp", T.yx[64 * H:64 * H + 64, 3072:4096], T["xs%d" % H][0:64, 3072:4096], "dout", ("xl%d_0" % H,))
+    for H in range(2):
+        for s in range(4):
+            for c in range(2):
+                lo = 192 * s + TW * c
+                dma(("sp", "act")[c], T.ys[64 * H:64 * H + 64, lo:lo + TW], T["ysb%d" % H][64 * c:64 * c + 64, TW * s:TW * s + TW], "dout",
+                    tuple(otok(VI, H, e, s) for e in range(len(CH))))
 
     if "order" not in CACHE:
         CACHE["order"] = schedule(nodes)
     known = {q: {} for q in Q}
     cnt = {q: 0 for q in Q}
-    snap, ident, seen = {}, {}, set()
+    snap, ident, seen, total = {}, {}, set(), {}
 
     def wait(q, deps):
         todo = sorted({d for d in deps if known[q].get(d[0], 0) < d[1]}, key=lambda d: (-len(snap.get(d, {})), d[0], -d[1]))
@@ -547,29 +564,29 @@ def rank_program(g, core, T, topo):
             for s2, k2 in snap.get((s, k), {}).items():
                 if known[q].get(s2, 0) < k2:
                     known[q][s2] = k2
-    sent = 0
     for i in CACHE["order"]:
         x = nodes[i]
         q = x["q"]
         if q is None:
             ident[i] = x["ext"]
+            total[x["ext"][0]] = x["ext"][1]
             continue
         wait(q, [ident[d] for d in x["deps"] if d in ident])
-        for f in x["fns"]:
+        for j, f in enumerate(x["fns"]):
             ins = f()
             if x["ext"] is None:
                 cnt[q] += 1
                 ident[i] = ("s_" + q, cnt[q])
                 ins.then_inc(T.sem["s_" + q], 1)
             elif x["ext"] == "send":
-                sent += 6
+                total["sent"] = total.get("sent", 0) + 6
             else:
                 ident[i] = x["ext"]
+                total[x["ext"][0]] = total.get(x["ext"][0], 0) + 16
                 ins.then_inc(T.sem[x["ext"][0]], 16)
         if i in ident:
             snap[ident[i]] = dict(known[q])
-    ends = [("s_" + q, cnt[q]) for q in ("pe", "dve", "act", "pool")] + [("sent", sent)]
-    ends += [(s, 6 if s[:3] == "arr" else 16) for s in SEMAPHORES if s[:2] != "s_" and s != "sent"]
+    ends = [("s_" + q, cnt[q]) for q in ("pe", "dve", "act", "pool")] + sorted(total.items())
     known["pool"].clear()
     snap.clear()
     wait("pool", [e for e in ends if e not in seen])

@@ -4,16 +4,17 @@ from concourse.mybir import AluOpType as A, ActivationFunctionType as F
 VI = 4
 TW = 96
 SUB = 512
-CH = ((0, 1), (2,))
+CH = ((0,), (1,), (2,))
 STEP = (0, 1, 2, 4)
-FILLS, SUMS, CRIT, UPD = (0, 1, 2), 3, (4, 5), (6, 7)
-ND, NT, NW = 3, 4, 4
+FILLS, SUMS, CRIT, UPD = (0, 1), 2, (3, 4), (5, 6, 7)
+ONVEC = ("src", "snd")
+ND, NT, NW = 4, 6, 6
 BYDMA = lambda v, H, c: False
-BYABS = lambda v, H, p: p == 1
-BYVEC = lambda v, H, p, s: v == 0 and H == 0 and s in (0, 1) and p < 2
+BYABS = lambda v, H, p: False
+BYVEC = lambda v, H, p, s: v == 0 and H == 0 and s in (0, 1) and p == 0
 
-CY, PEC, GAM, SCA, WAKE, NET, FIX = 0.9, 0.45, 1.4, 3.2, 120.0, 5000.0, 10.0
-TOL = 40.0
+CY, PEC, GAM, SCA, WAKE, NET, FIX = 0.9, 0.45, 1.4, 3.2, 140.0, 6500.0, 10.0
+TOL, SWEEPS = 40.0, 8
 BONUS = {}
 
 SCRATCH = {"thi": ("sbuf", [128, 8], "int32"), "ici": ("sbuf", [128, 16], "int32"), "ip": ("sbuf", [128, 1], "int32")}
@@ -64,45 +65,54 @@ CACHE = {}
 
 def schedule(nodes):
     n = len(nodes)
-    succ = [[] for _ in range(n)]
+    fwd, back = [[] for _ in range(n)], [[] for _ in range(n)]
     for i, x in enumerate(nodes):
         for d in x["deps"] | x["odeps"]:
-            succ[d].append(i)
-    level = [0.0] * n
+            gap = nodes[d]["lat"] + WAKE if d in x["deps"] else 0.0
+            fwd[d].append((i, gap))
+            back[i].append((d, gap))
+    cost = [x["cost"] for x in nodes]
+    tail = [x["lat"] for x in nodes]
+
+    def sweep(succ, pred, prio, ready):
+        left = [len(p) for p in pred]
+        free, cand, order, end = {}, {}, [], [0.0] * n
+        for i, x in enumerate(nodes):
+            if left[i] == 0:
+                cand.setdefault(x["q"], []).append(i)
+        while len(order) < n:
+            best = None
+            for q, l in cand.items():
+                if not l:
+                    continue
+                t = free.get(q, 0.0) if q is not None else 0.0
+                first = max(t, min(ready[i] for i in l))
+                i = max((i for i in l if ready[i] <= first + TOL), key=lambda i: prio[i])
+                if best is None or max(first, ready[i]) < best[0]:
+                    best = (max(first, ready[i]), q, i)
+            s, q, i = best
+            cand[q].remove(i)
+            order.append(i)
+            free[q] = end[i] = s + cost[i]
+            for j, gap in succ[i]:
+                ready[j] = max(ready[j], end[i] + gap)
+                left[j] -= 1
+                if left[j] == 0:
+                    cand.setdefault(nodes[j]["q"], []).append(j)
+        return order, end
     prio = [0.0] * n
     for i in range(n - 1, -1, -1):
-        x = nodes[i]
-        level[i] = x["cost"] + x["lat"] + max([level[j] + (WAKE if i in nodes[j]["deps"] else 0.0) for j in succ[i]] + [0.0])
-        prio[i] = level[i] + BONUS.get(x["lab"], 0.0)
-    left = [len(x["deps"] | x["odeps"]) for x in nodes]
-    ready = [0.0] * n
-    free, cand, order = {}, {}, []
-    for i, x in enumerate(nodes):
-        if left[i] == 0:
-            cand.setdefault(x["q"], []).append(i)
-    while len(order) < n:
-        best = None
-        for q, l in cand.items():
-            if not l:
-                continue
-            t = free.get(q, 0.0) if q is not None else 0.0
-            first = max(t, min(ready[i] for i in l))
-            i = max((i for i in l if ready[i] <= first + TOL), key=lambda i: (prio[i], -i))
-            if best is None or max(first, ready[i]) < best[0]:
-                best = (max(first, ready[i]), q, i)
-        s, q, i = best
-        cand[q].remove(i)
-        order.append(i)
-        x = nodes[i]
-        free[q] = s + x["cost"]
-        end = s + x["cost"] + x["lat"]
-        for j in succ[i]:
-            e = end + WAKE if i in nodes[j]["deps"] else s + x["cost"]
-            ready[j] = max(ready[j], e)
-            left[j] -= 1
-            if left[j] == 0:
-                cand.setdefault(nodes[j]["q"], []).append(j)
-    return order
+        prio[i] = cost[i] + max([prio[j] + gap for j, gap in fwd[i]] + [tail[i]])
+    prio = [p + BONUS.get(x["lab"], 0.0) for p, x in zip(prio, nodes)]
+    best = None
+    for _ in range(SWEEPS):
+        order, end = sweep(fwd, back, prio, [0.0] * n)
+        span = max(e + t for e, t in zip(end, tail))
+        if best is None or span < best[0]:
+            best = (span, order)
+        prio = sweep(back, fwd, [e + t for e, t in zip(end, tail)], list(tail))[1]
+    CACHE["span"] = best[0]
+    return best[1]
 
 
 def rank_program(g, core, T, topo):
@@ -132,7 +142,7 @@ def rank_program(g, core, T, topo):
         for t in b:
             for q2, d in banks.get(t, {}).items():
                 (odeps if q2 == q else deps).add(d)
-        nodes.append({"q": q, "fns": fns, "cost": cost, "deps": deps, "odeps": odeps - deps, "ext": ext, "lat": lat, "lab": lab[0]})
+        nodes.append({"q": q, "fns": fns, "cost": cost, "deps": deps, "odeps": odeps - deps, "ext": ext, "lat": lat, "lab": lab[0], "w": w, "b": b})
         for t in r:
             readers.setdefault(t, set()).add(i)
         for t in w:
@@ -157,6 +167,18 @@ def rank_program(g, core, T, topo):
     def act(n, out, in_, func, bias=0.0, scale=1.0, accum=None, r=(), w=(), b=(), cost=None):
         kw = {} if accum is None else {"accum_out": accum}
         op("act", [lambda: g.scalar.activation(out=out, in_=in_, func=func, bias=bias, scale=scale, **kw)], cost or FIX + CY * max(64, n), r, w, b)
+
+    def copy(kind, n, out, in_, w, bank):
+        if kind in ONVEC:
+            cp(n, out, in_, w=w, b=(bank,))
+        else:
+            act(n, out, in_, F.Copy, w=w, b=(bank,))
+
+    def shift(kind, n, out, in_, x, r=(), w=(), b=()):
+        if kind in ONVEC:
+            ts(n, out, in_, x, A.add, r=r, w=w, b=b)
+        else:
+            act(n, out, in_, F.Identity, x, r=r, w=w, b=b)
 
     def mm(bank, out, n, terms, start=True, stop=True):
         def one(l, x, s, e):
@@ -329,8 +351,8 @@ def rank_program(g, core, T, topo):
         todo = [10 - (1 if BYDMA(v, H, c) else 0), 0]
 
         def red(view, m, tok):
-            for k in range(4):
-                mm(SUMS, pb[SUMS][:, k:96:4], 64, [(view(k), m, (tok, "red"))], todo[1] == 0 and k == 0, todo[1] == todo[0] - 1 and k == 3)
+            one = lambda k, l, s, e: lambda: g.tensor.matmul(out=pb[SUMS][:, k:96:4], lhsT=l, rhs=m, start=s, stop=e)
+            op("pe", [one(k, view(k), todo[1] == 0 and k == 0, todo[1] == todo[0] - 1 and k == 3) for k in range(4)], PEC * 256, (tok, "red"), (), (SUMS,))
             todo[1] += 1
 
         def fills(terms):
@@ -376,7 +398,7 @@ def rank_program(g, core, T, topo):
                 pair(5, 3, u1, RC)
         ct = "ct%d" % (turn["t"] % NT)
         turn["t"] += 1
-        cp(96, B(ct, 3, 387, 4), pb[SUMS][:, 0:96], w=(ct,), b=(SUMS,))
+        copy("ct", 96, B(ct, 3, 387, 4), pb[SUMS][:, 0:96], (ct,), SUMS)
         for q in range(3):
             lo = q * wid[c] + 32 * p - first[c]
             mms(C, lo, lo + 32, [(B(ct, 3 - h + 128 * q, 131 - h + 128 * q), B("sel", 32 * h, 32 * h + 32), (ct, "sel")) for h in range(4)])
@@ -388,16 +410,19 @@ def rank_program(g, core, T, topo):
         pc = lambda a, b_: pb[C][:, a * w:b_ * w]
         pu = lambda a, b_: pb[U][:, a * w:b_ * w]
         mc = lambda a, b_, terms: mms(C, a * w, b_ * w, terms)
-        mu = lambda a, b_, terms, start=False, stop=False: mms(U, a * w, b_ * w, terms, start, stop)
+        mu = lambda a, b_, terms, start=True, stop=True: mms(U, a * w, b_ * w, terms, start, stop)
         up = lambda s, a, b_=None: (I, P(s, a, b_), ("idb", n(s)))
         dn = lambda s, a, b_=None: (N_, P(s, a, b_), ("nid", n(s)))
         lab[0] = "c"
-        cp(3 * w, P("ab", 0, 3), pc(0, 3), w=(n("ab"),), b=(C,))
+        copy("ab", 3 * w, P("ab", 0, 3), pc(0, 3), (n("ab"),), C)
         mc(3, 4, [(B("wz", 128 * q, 128 * q + 128), P("ab", q), ("wz", n("ab"))) for q in range(2)])
-        act(w, P("u", 0), pc(3, 4), F.Sign, 0.5, w=(n("u"),), b=(C,))
+        if "u" in ONVEC:
+            ts(w, P("u", 0), pc(3, 4), 0.0, A.is_ge, 0.5, A.subtract, w=(n("u"),), b=(C,))
+        else:
+            act(w, P("u", 0), pc(3, 4), F.Sign, 0.5, w=(n("u"),), b=(C,))
         mc(4, 5, [(B("wz", 256, 384), P("u", 0), ("wz", n("u")))])
         at = "acc%d_%d" % (H, c)
-        act(w, P("o", 0), pc(4, 5), F.Relu, n8, 0.5, accum=B("acc", 4 * H + c, 4 * H + c + 1), r=(n8t,), w=(n("o"), at), b=(C,))
+        act(w, P("o", 0), pc(4, 5), F.Relu, n8, 1.0 if "u" in ONVEC else 0.5, accum=B("acc", 4 * H + c, 4 * H + c + 1), r=(n8t,), w=(n("o"), at), b=(C,))
         o = P("o", 0)
         mc(5, 6, [(B("wl0"), o, ("wl0", n("o")))])
         mc(6, 7, [(B("wl2"), o, ("wl2", n("o")))])
@@ -405,64 +430,75 @@ def rank_program(g, core, T, topo):
         for q in range(2):
             m = B("wt", 128 * q, 128 * q + 128)
             mc(q, q + 1, [(m, B("teps", 0, w), ("wt", "teps")), (m, P("y", 0), (n("y"),)), (m, P("y", 1), (n("y"),))])
-        act(2 * w, P("tu", 0, 2), pc(0, 2), F.Sign, w=(n("tu"),), b=(C,))
+        if "tu" in ONVEC:
+            ts(2 * w, P("tu", 0, 2), pc(0, 2), 0.0, A.is_gt, 0.5, A.subtract, w=(n("tu"),), b=(C,))
+        else:
+            act(2 * w, P("tu", 0, 2), pc(0, 2), F.Sign, w=(n("tu"),), b=(C,))
         mc(2, 3, [(B("ca", 128 * q, 128 * q + 128), P("tu", q), ("ca", n("tu"))) for q in range(2)])
         om, omt = B("om%d" % H, first[c], first[c] + w), "om%d_%d" % (H, c)
-        act(w, om, pc(2, 3), F.Relu, -5.0, w=(omt,), b=(C,))
+        z = 2.0 if "tu" in ONVEC else 1.0
+        if "om" in ONVEC:
+            ts(w, om, pc(2, 3), 5.5 / z, A.is_ge, w=(omt,), b=(C,))
+        else:
+            act(w, om, pc(2, 3), F.Relu, -5.0, z, w=(omt,), b=(C,))
+        if c == len(CH) - 1:
+            blend(v, H, k)
         lab[0] = "u"
         ts(2 * w, P("st", 0, 4), T["off%d" % v][:, tab(H, c, 0, 4)], -2048.0, A.add, r=tuple(otok(v, H, c, s) for s in range(4)), w=(n("st"),))
-        mu(0, 3, [up("st", 0, 3)], True, True)
+        mu(2, 5, [up("st", 0, 3)])
+        mu(0, 1, [(B("pi"), P("ab", 1), ("pi", n("ab")))])
+        mu(1, 2, [(B("pi"), P("ab", 0), ("pi", n("ab")))])
         gm = (B("wr"), om, ("wr", omt))
-        mc(0, 1, [(B("pi"), P("ab", 1), ("pi", n("ab")))])
-        mc(1, 2, [(B("pi"), P("ab", 0), ("pi", n("ab")))])
         for q in range(2):
-            mc(3 + q, 4 + q, [(B("mz", 128 * q, 128 * q + 128), o, ("mz", n("o"))), gm])
-        for q in range(2):
-            mc(5 + q, 6 + q, [(B("w5"), o, ("w5", n("o"))), gm])
+            mu(5 + q, 6 + q, [(B("mz", 128 * q, 128 * q + 128), o, ("mz", n("o"))), gm])
         pm = P("pm", 0, 2)
-        ts(2 * w, pm, pc(3, 5), 2.0, A.is_equal, w=(n("pm"),), b=(C,))
-        tt(2 * w, P("zz", 0, 2), pm, pc(0, 2), A.mult, r=(n("pm"),), w=(n("zz"),), b=(C,))
-        mc(2, 3, [(B("pi"), P("ab", 2), ("pi", n("ab"))), up("zz", 0), up("zz", 1)])
-        th = "thf%d_%d" % (H, v % 2)
-        ts(w, P("vv", 0), pc(2, 3), B("thf", 2 * H + v % 2, 2 * H + v % 2 + 1), A.is_gt, r=(th,), w=(n("vv"),), b=(C,))
-        tt(2 * w, P("f1", 0, 2), pm, pb[U][:, 0:2 * w], A.mult, r=(n("pm"),), w=(n("f1"),), b=(U,))
-        tt(2 * w, P("f2", 0, 2), pm, pu(1, 3), A.mult, r=(n("pm"),), w=(n("f2"),), b=(U,))
-        mu(3, 6, [up("st", 0, 3)], True, False)
-        mu(3, 5, [up("f2", 0, 2), dn("f1", 0, 2)], False, False)
-        mu(4, 6, [up("f1", 0, 2), dn("f2", 0, 2)], False, True)
-        act(3 * w, P("am", 0, 3), pu(3, 6), F.Copy, w=(n("am"),), b=(U,))
-        vv = P("vv", 0)
-        mu(6, 8, [(I, B("t2k", 0, 2 * w), ("idb", "t2k"))], True, False)
-        mu(7, 8, [up("st", 3)], False, False)
-        mu(6, 7, [up("am", 2)], False, False)
-        mu(0, 2, [up("am", 0, 2)], False, False)
+        ts(2 * w, pm, pu(5, 7), 2.0, A.is_equal, w=(n("pm"),), b=(U,))
+        tt(2 * w, P("f1", 0, 2), pm, pu(2, 4), A.mult, r=(n("pm"),), w=(n("f1"),), b=(U,))
+        tt(2 * w, P("f2", 0, 2), pm, pu(3, 5), A.mult, r=(n("pm"),), w=(n("f2"),), b=(U,))
+        tt(2 * w, P("zz", 0, 2), pm, pu(0, 2), A.mult, r=(n("pm"),), w=(n("zz"),), b=(U,))
         for q in range(2):
-            mu(q, q + 1, [(B("i4k"), vv, ("i4k", n("vv")))], False, q == 1)
-        act(2 * w, P("sr", 0, 2), pu(0, 2), F.Relu, -2048.0, w=(n("sr"),), b=(U,))
+            mu(6 + q, 7 + q, [(B("w5"), o, ("w5", n("o"))), gm])
+        mu(1, 4, [up("st", 0, 3)], True, False)
+        mu(1, 3, [up("f2", 0, 2), dn("f1", 0, 2)], False, False)
+        mu(2, 4, [up("f1", 0, 2), dn("f2", 0, 2)], False, True)
+        mu(0, 1, [(B("pi"), P("ab", 2), ("pi", n("ab"))), up("zz", 0), up("zz", 1)])
+        th = "thf%d_%d" % (H, v % 2)
+        ts(w, P("vv", 0), pu(0, 1), B("thf", 2 * H + v % 2, 2 * H + v % 2 + 1), A.is_gt, r=(th,), w=(n("vv"),), b=(U,))
+        copy("am", 3 * w, P("am", 0, 3), pu(1, 4), (n("am"),), U)
+        vv = P("vv", 0)
         big = (I, B("tbig", 0, w), ("idb", "tbig"))
         dk = (B("dk"), vv, ("dk", n("vv")))
-        mc(3, 4, [big, (B("i32"), P("am", 2), ("i32", n("am"))), dk])
-        mc(4, 5, [big, (B("i32"), P("st", 3), ("i32", n("st"))), dk])
-        tt(2 * w, P("e1", 0, 2), P("am", 0, 2), pc(5, 7), A.mult, r=(n("am"),), w=(n("e1"),), b=(C,))
-        tt(2 * w, P("pp", 0, 2), P("sr", 0, 2), pu(6, 8), A.mult, r=(n("sr"),), w=(n("pp"),), b=(U,))
-        tt(2 * w, P("ui", 0, 2), P("pp", 0, 2), pc(3, 5), A.add, r=(n("pp"),), w=(n("ui"),), b=(C,))
+        mu(0, 2, [up("am", 0, 2)], True, False)
+        for q in range(2):
+            mu(q, q + 1, [(B("i4k"), vv, ("i4k", n("vv")))], False, False)
+        mu(4, 6, [(I, B("t2k", 0, 2 * w), ("idb", "t2k"))], False, False)
+        mu(5, 6, [up("st", 3)], False, False)
+        mu(4, 5, [up("am", 2)], False, True)
+        mu(2, 3, [big, (B("i32"), P("am", 2), ("i32", n("am"))), dk])
+        mu(3, 4, [big, (B("i32"), P("st", 3), ("i32", n("st"))), dk])
+        if "sr" in ONVEC:
+            ts(2 * w, P("sr", 0, 2), pu(0, 2), -2048.0, A.add, 0.0, A.max, w=(n("sr"),), b=(U,))
+        else:
+            act(2 * w, P("sr", 0, 2), pu(0, 2), F.Relu, -2048.0, w=(n("sr"),), b=(U,))
+        tt(2 * w, P("pp", 0, 2), P("sr", 0, 2), pu(4, 6), A.mult, r=(n("sr"),), w=(n("pp"),), b=(U,))
+        tt(2 * w, P("e1", 0, 2), P("am", 0, 2), pu(6, 8), A.mult, r=(n("am"),), w=(n("e1"),), b=(U,))
+        tt(2 * w, P("ui", 0, 2), P("pp", 0, 2), pu(2, 4), A.add, r=(n("pp"),), w=(n("ui"),), b=(U,))
         ts(2 * w, P("nb", 0, 2), P("ui", 0, 2), 5, A.arith_shift_right, 4095, A.bitwise_and, r=(n("ui"),), w=(n("nb"),))
-        ts(2 * w, P("src", 0, 2), P("nb", 0, 2), -2048.0, A.add, r=(n("nb"),), w=(n("src"),))
-        tt(2 * w, P("e2", 0, 2), P("src", 0, 2), pc(5, 7), A.mult, r=(n("src"),), w=(n("e2"),), b=(C,))
+        shift("src", 2 * w, P("src", 0, 2), P("nb", 0, 2), -2048.0, r=(n("nb"),), w=(n("src"),))
         low = [up("am", 0, 2), dn("e1", 0, 2), up("e2", 0, 2)]
-        mu(4, 6, low[:2], True, False)
-        mu(6, 7, [up("e1", 0), up("src", 0), dn("e2", 0)], False, False)
-        mu(4, 6, low[2:], False, True)
-        tt(2 * w, P("g1", 0, 2), pm, pu(4, 6), A.mult, r=(n("pm"),), w=(n("g1"),), b=(U,))
-        tt(2 * w, P("g2", 0, 2), pm, pu(5, 7), A.mult, r=(n("pm"),), w=(n("g2"),), b=(U,))
+        tt(2 * w, P("e2", 0, 2), P("src", 0, 2), pu(6, 8), A.mult, r=(n("src"),), w=(n("e2"),), b=(U,))
+        mu(4, 6, low, True, False)
+        mu(6, 7, [up("e1", 0), up("src", 0), dn("e2", 0)], False, True)
         mu(0, 2, low, True, False)
         mu(2, 4, [up("e1", 0, 2), up("src", 0, 2), dn("e2", 0, 2)], False, False)
+        tt(2 * w, P("g1", 0, 2), pm, pu(4, 6), A.mult, r=(n("pm"),), w=(n("g1"),), b=(U,))
+        tt(2 * w, P("g2", 0, 2), pm, pu(5, 7), A.mult, r=(n("pm"),), w=(n("g2"),), b=(U,))
         mu(0, 2, [up("g2", 0, 2), dn("g1", 0, 2)], False, False)
         mu(1, 3, [up("g1", 0, 2), dn("g2", 0, 2)], False, True)
         snd, sdt, ysb = T["snd%d" % v], "snd%d_%d_%d" % (v, H, c), T["ysb%d" % H]
         if v < VI - 1:
-            ts(3 * w, snd[:, tab(H, c, 0, 3, 3)], pu(1, 4), 2048.0, A.add, w=(sdt,), b=(U,))
-            ts(w, T["off%d" % (v + 1)][:, tab(H, c, 0)], pu(0, 1), 2048.0, A.add, w=(otok(v + 1, H, c, 0),), b=(U,))
+            shift("snd", 3 * w, snd[:, tab(H, c, 0, 3, 3)], pu(1, 4), 2048.0, w=(sdt,), b=(U,))
+            shift("snd", w, T["off%d" % (v + 1)][:, tab(H, c, 0)], pu(0, 1), 2048.0, w=(otok(v + 1, H, c, 0),), b=(U,))
         else:
             act(3 * w, snd[:, tab(H, c, 0, 3, 3)], pu(1, 4), F.Identity, 2048.0, w=(sdt,), b=(U,))
             act(w, ysb[:, first[c]:first[c] + w], pu(0, 1), F.Identity, 2048.0, w=(otok(VI, H, c, 0),), b=(U,))
@@ -477,8 +513,8 @@ def rank_program(g, core, T, topo):
                 land = ysb[:, s * TW + first[c]:s * TW + first[c] + w]
             tr.append(RemoteDMATransfer(dst_ids=[DstId(rid=rid, pnc=pid)], dma_engine_mask=(1 << e[2 * s - 2]) | (1 << e[2 * s - 1]),
                                         remote_sem=T.sem["arr%d_%d" % (v, k % (2 * len(CH)))], src=snd[:, tab(H, c, s - 1, 1, 3)], dst=land))
-        op("pool", [lambda: g.remote_dma_fused(tr, local_sem=T.sem.sent)], 1000.0, (sdt,), ("go",), ext="send")
-        op(None, [], 0.0, ("go",), tuple(otok(v + 1, H, c, s) for s in (1, 2, 3)), ext=("arr%d_%d" % (v, k % (2 * len(CH))), 6), lat=NET)
+        op("pool", [lambda: g.remote_dma_fused(tr, local_sem=T.sem.sent)], 1000.0, (sdt,), ("go%d" % k,), ext="send")
+        op(None, [], 0.0, ("go%d" % k,), tuple(otok(v + 1, H, c, s) for s in (1, 2, 3)), ext=("arr%d_%d" % (v, k % (2 * len(CH))), 6), lat=NET)
 
     def blend(v, H, k):
         C, xs, li = CRIT[k % len(CRIT)], T["xs%d" % H], T["lists%d" % H]
@@ -494,7 +530,7 @@ def rank_program(g, core, T, topo):
         gs, gx, tq = ["%s%d" % (s, H) for s in ("gs", "gx", "tq")]
         act(0, B(gs), T["g0_%d" % H][:, 0:1536].indirect(li[:, 16:22]), F.Copy, r=(lit,) + tuple(gt(0, H, p) for p in range(3)), w=(gs,), cost=70 + TW * GAM)
         act(0, B(gx), xs[:, 0:3072].indirect(li[:, 24:30]), F.Copy, r=(lit + "x",) + xt(H), w=(gx,), cost=70 + TW * GAM)
-        at = 0 if wid[-1] == 64 else 256
+        at = 0
         last = v == VI - 1
         if last:
             mms(C, at, at + TW, [(I, B(s), ("idb", s)) for s in (gs, gx)])
@@ -535,8 +571,6 @@ def rank_program(g, core, T, topo):
                 for p in ps:
                     piece(v, H, c, p, CRIT[k % len(CRIT)])
                 chunk(v, H, c, k)
-                if c == len(CH) - 1:
-                    blend(v, H, k)
                 k += 1
             if v == 0:
                 dma("sp", T.yx[64 * H:64 * H + 64, 3072:4096], T["xs%d" % H][0:64, 3072:4096], "dout", ("xl%d_0" % H,))
@@ -549,6 +583,7 @@ def rank_program(g, core, T, topo):
 
     if "order" not in CACHE:
         CACHE["order"] = schedule(nodes)
+        CACHE["nodes"] = nodes
     known = {q: {} for q in Q}
     cnt = {q: 0 for q in Q}
     snap, ident, seen, total = {}, {}, set(), {}

@@ -5,17 +5,20 @@ VI = 4
 TW = 96
 SUB = 512
 CH = ((0,), (1,), (2,))
+PORD = (0, 1, 2)
+VVC = 2
 STEP = (0, 1, 2, 4)
+CALLS = (((1, 0, 2), (2, 2, 6), (3, 6, 8)),)
 FILLS, SUMS, CRIT, UPD = (0, 1), 2, (3, 4), (5, 6, 7)
-ONVEC = ("src", "snd")
+ONVEC = ("src",)
 ND, NT, NW = 4, 6, 6
-BYDMA = lambda v, H, c: False
-BYABS = lambda v, H, p: False
-BYVEC = lambda v, H, p, s: v == 0 and H == 0 and s in (0, 1) and p == 0
+GC = ((0,), (2,), (1,), (3,))
+BYVEC = lambda v, H, p, s: H == 0 and p == 0 and s == 0
 
-CY, PEC, GAM, SCA, WAKE, NET, FIX = 0.9, 0.45, 1.4, 3.2, 140.0, 6500.0, 10.0
-TOL, SWEEPS = 40.0, 8
-BONUS = {}
+CY, PEC, GAM, SCA, WAKE, NET, FIX = 0.85, 0.38, 1.3, 3.0, 220.0, 5000.0, 12.0
+TOL, SWEEPS, SHAKE = 80.0, 900, 60.0
+CASES = ((0.95, 0.95, 200.0, 3500.0), (0.95, 0.95, 280.0, 5500.0), (1.0, 1.3, 200.0, 4000.0), (1.0, 0.75, 200.0, 4000.0), (1.3, 1.0, 200.0, 4500.0))
+QUEUES = ("pe", "dve", "act", "pool", "sp", None)
 
 SCRATCH = {"thi": ("sbuf", [128, 8], "int32"), "ici": ("sbuf", [128, 16], "int32"), "ip": ("sbuf", [128, 1], "int32")}
 PLACE = {}
@@ -24,8 +27,8 @@ for _h in range(2):
     SCRATCH["homi%d" % _h] = ("sbuf", [128, 768], "int32")
     SCRATCH["ysb%d" % _h] = ("sbuf", [128, 384], "float32")
     SCRATCH["lists%d" % _h] = ("sbuf", [128, 32], "uint16")
-    for _s in range(4):
-        SCRATCH["g%d_%d" % (_s, _h)] = ("sbuf", [128, 1536], "bfloat16")
+    SCRATCH["g0_%d" % _h] = ("sbuf", [128, 1536], "bfloat16")
+    SCRATCH["g1_%d" % _h] = ("sbuf", [128, 4608], "bfloat16")
 for _v in range(VI):
     SCRATCH["off%d" % _v] = ("sbuf", [128, 768], "uint16")
     SCRATCH["snd%d" % _v] = ("sbuf", [128, 576], "uint16" if _v < VI - 1 else "float32")
@@ -45,21 +48,20 @@ def _pack(buf, dtype, names):
 
 for _p in range(NW):
     for _k, _d, _l in (("h", "float16", (("ab", 3), ("y", 2), ("zz", 2), ("st", 4), ("f1", 2), ("f2", 2), ("vv", 1), ("e1", 2), ("e2", 2), ("src", 2),
-                                         ("g1", 2), ("g2", 2), ("am", 3))),
+                                         ("g1", 2), ("g2", 2), ("am", 4))),
                        ("b", "bfloat16", (("u", 1), ("o", 1), ("tu", 2), ("pm", 2))),
                        ("f", "float32", (("sr", 2), ("pp", 2))),
                        ("i", "int32", (("ui", 2), ("nb", 2)))):
         _pack("w%s%d" % (_k, _p), _d, [("%s_%d" % (_n, _p), 64 * _w) for _n, _w in _l])
-_pack("cts", "float16", [("ct%d" % _p, 400) for _p in range(NT)] + [("dk", 128)])
+_pack("cts", "float16", [("ct%d" % _p, 96) for _p in range(NT)] + [("dk", 128)])
 _pack("blb", "bfloat16", [("%s%d" % (_n, _h), _w) for _h in range(2) for _n, _w in (("om", 96), ("gs", 96), ("gx", 96), ("tq", 192), ("accb", 4))])
-_pack("conb", "bfloat16", [(_n, 128) for _n in ("idb", "nid", "i32", "n32", "i4k", "onb", "t2k", "tbig", "teps", "sel", "pi", "bm0", "bm", "lt0", "lt1", "lt",
+_pack("conb", "bfloat16", [(_n, 128) for _n in ("idb", "nid", "i32", "npt", "i4k", "onb", "t2k", "tbig", "pit", "bt0", "bt", "sel", "pi", "bm0", "bm", "lt0", "lt1", "lt",
                                                 "wr", "w5", "wl0", "wl2", "sp0", "sp2", "rw", "dke", "dko")] +
-      [("hm", 256), ("wsn", 192), ("red0", 104), ("red1", 104), ("red", 104), ("m192", 192), ("wz", 384), ("ca", 256), ("cat", 256), ("wt", 256), ("mz", 256),
-       ("al", 288), ("ia", 160), ("jr", 160), ("zero", 400)] + [("tm%d" % _n, 160) for _n in range(11)])
+      [("hm", 256), ("wsn", 192), ("red0", 64), ("red1", 64), ("red", 64), ("m192", 192), ("wz", 384), ("ca", 256), ("cat", 256), ("wt", 256), ("mz", 256),
+       ("al", 288), ("ia", 160), ("jr", 160)] + [("tm%d" % _n, 160) for _n in range(11)])
 _pack("conf", "float32", [("kf", 8), ("ek", 16), ("acc", 8), ("thf", 4), ("lt32", 64), ("two", 8)] + [("col%d" % _n, 1) for _n in range(24)])
 SEMAPHORES = ["s_pe", "s_dve", "s_act", "s_pool", "sent", "dout"] + ["d%s%d" % (_n, _h) for _n in "xht" for _h in range(4)]
-SEMAPHORES += ["ds%d_%d_%d" % (_v, _c, _j) for _v in range(VI) for _c in range(2 * len(CH)) for _j in range(3) if BYDMA(_v, _c // len(CH), _c % len(CH))]
-SEMAPHORES += ["arr%d_%d" % (_v, _c) for _v in range(VI) for _c in range(2 * len(CH))]
+SEMAPHORES += ["arr%d_%d_%d" % (_v, _c, _j) for _v in range(VI) for _c in range(2 * len(CH)) for _j in range(len(CALLS))]
 CACHE = {}
 
 
@@ -73,45 +75,60 @@ def schedule(nodes):
             back[i].append((d, gap))
     cost = [x["cost"] for x in nodes]
     tail = [x["lat"] for x in nodes]
+    on = [x["q"] for x in nodes]
 
     def sweep(succ, pred, prio, ready):
         left = [len(p) for p in pred]
-        free, cand, order, end = {}, {}, [], [0.0] * n
-        for i, x in enumerate(nodes):
+        free, cand, pick, order, end = {q: 0.0 for q in QUEUES}, {q: [] for q in QUEUES}, {}, [], [0.0] * n
+        for i in range(n):
             if left[i] == 0:
-                cand.setdefault(x["q"], []).append(i)
-        while len(order) < n:
-            best = None
-            for q, l in cand.items():
-                if not l:
-                    continue
-                t = free.get(q, 0.0) if q is not None else 0.0
-                first = max(t, min(ready[i] for i in l))
-                i = max((i for i in l if ready[i] <= first + TOL), key=lambda i: prio[i])
-                if best is None or max(first, ready[i]) < best[0]:
-                    best = (max(first, ready[i]), q, i)
-            s, q, i = best
-            cand[q].remove(i)
+                cand[on[i]].append(i)
+        dirty = QUEUES
+        while True:
+            for q in dirty:
+                pick[q] = None
+                if cand[q]:
+                    first = max(free[q] if q else 0.0, min([ready[i] for i in cand[q]]))
+                    i = max([i for i in cand[q] if ready[i] <= first + TOL], key=lambda i: prio[i])
+                    pick[q] = (max(first, ready[i]), i)
+            if len(order) == n:
+                return order, end
+            s, i = min([p for p in pick.values() if p])
+            cand[on[i]].remove(i)
             order.append(i)
-            free[q] = end[i] = s + cost[i]
+            e = free[on[i]] = end[i] = s + cost[i]
+            dirty = [on[i]]
             for j, gap in succ[i]:
-                ready[j] = max(ready[j], end[i] + gap)
+                ready[j] = max(ready[j], e + gap)
                 left[j] -= 1
                 if left[j] == 0:
-                    cand.setdefault(nodes[j]["q"], []).append(j)
-        return order, end
+                    cand[on[j]].append(j)
+                    dirty.append(on[j])
+
+    def span(order, f, gam, wake, net):
+        free, end = {q: 0.0 for q in QUEUES}, [0.0] * n
+        for i in order:
+            x, q = nodes[i], on[i]
+            t = max([end[d] for d in x["deps"]] + [free[q] if q else 0.0]) + cost[i] * (1.0 if q in ("pool", "sp") else f * gam if x["lab"] == "g" else f)
+            free[q] = t
+            end[i] = t + wake + (tail[i] if q else net)
+        return max(end)
     prio = [0.0] * n
     for i in range(n - 1, -1, -1):
         prio[i] = cost[i] + max([prio[j] + gap for j, gap in fwd[i]] + [tail[i]])
-    prio = [p + BONUS.get(x["lab"], 0.0) for p, x in zip(prio, nodes)]
-    best = None
-    for _ in range(SWEEPS):
+    best, seed = None, 1
+    for it in range(SWEEPS):
         order, end = sweep(fwd, back, prio, [0.0] * n)
-        span = max(e + t for e, t in zip(end, tail))
-        if best is None or span < best[0]:
-            best = (span, order)
         prio = sweep(back, fwd, [e + t for e, t in zip(end, tail)], list(tail))[1]
-    CACHE["span"] = best[0]
+        total = sum(span(order, *m) for m in CASES)
+        if best is None or total < best[0]:
+            best = (total, order, prio)
+        if it % 3 == 2:
+            prio = []
+            for p in best[2]:
+                seed = seed * 16807 % 2147483647
+                prio.append(p + SHAKE * (seed / 1073741823.5 - 1.0))
+    CACHE["span"] = best[0] / len(CASES)
     return best[1]
 
 
@@ -122,7 +139,7 @@ def rank_program(g, core, T, topo):
     Q = {"pe": g.tensor, "dve": g.vector, "act": g.scalar, "pool": g, "sp": g.sync}
     nodes, lastw, readers, banks = [], {}, {}, {}
     pb = [T["pb%d" % b] for b in range(8)]
-    lab = [None]
+    lab = ["", ""]
 
     def B(name, lo=0, hi=None, st=1):
         buf, at, w = PLACE[name]
@@ -195,7 +212,7 @@ def rank_program(g, core, T, topo):
     for H in range(2):
         for c in range(2):
             rows, to = slice(64 * H, 64 * H + 64), slice(64 * c, 64 * c + 64)
-            dma("act", T["homi%d" % H][to, 0:768 - TW * c], T.hom[rows, TW * c:768], "dh%d" % (2 * H + c), (), ("homi%d_%d" % (H, c),), 3000.0 + 3000 * H)
+            dma("act", T["homi%d" % H][to, 0:672], T.hom[rows, TW * c:TW * c + 672], "dh%d" % (2 * H + c), (), ("homi%d_%d" % (H, c),), 3000.0 + 3000 * H)
             dma("sp", T["xs%d" % H][to, :], T.x[rows, :], "dx%d" % (2 * H + c), (), ("xl%d_%d" % (H, c),), 5000.0 + 3000 * H)
     for H in range(2):
         for c in range(2):
@@ -226,29 +243,29 @@ def rank_program(g, core, T, topo):
     iota(T.ip[:], [[0, 1]], 0, 1, "ip", 1, False)
     fill("onb", 1.0)
     sel("idb", "onb", [[-1, 128]], A.is_equal, 0, 1)
-    for lo, hi, x in ((0, 104, 0.0), (8, 16, 2.0), (32, 72, -1.0), (48, 56, 0.0), (72, 80, 1.0), (80, 96, -2.0), (96, 104, 2.0)):
+    for lo, hi, x in ((0, 32, 0.0), (8, 64, 2.0), (16, 32, 0.0), (32, 40, -1.0), (40, 56, -2.0)):
         fill("red0", x, lo, hi)
-    sel("red1", "red0", [[0, 13], [-16, 8]], A.is_ge, 0, 1, 104)
-    sel("red", "red1", [[0, 13], [16, 8]], A.is_ge, 15, -1, 104)
-    RB, RA, RS, RE, RD, RC = [B("red", 8 * j, 8 * j + 24) for j in (0, 1, 2, 4, 7, 10)]
+    sel("red1", "red0", [[0, 8], [-16, 8]], A.is_ge, 0, 1, 64)
+    sel("red", "red1", [[0, 8], [16, 8]], A.is_ge, 15, -1, 64)
+    RA, RB, RS, RC = [B("red", 8 * j, 8 * j + 24) for j in (0, 1, 2, 5)]
     iota(B("ia"), [[1, 160]], 0, 0, "ia", 160)
     sel("sel", "onb", [[-1, 4], [-4, 32]], A.is_equal, 0, 1)
     sel("bm0", "onb", [[-16, 8], [0, 16]], A.is_ge, 0, 1)
     sel("bm", "bm0", [[16, 8], [0, 16]], A.is_ge, 15, -1)
-    sel("lt0", "onb", [[-16, 8], [0, 16]], A.is_ge, -5, 1)
-    sel("lt1", "lt0", [[16, 8], [0, 16]], A.is_ge, 11, -1)
-    TURN = [[-16, 8], [-1, 4], [-4, 4]]
+    sel("lt0", "onb", [[0, 4], [-16, 8], [0, 4]], A.is_ge, -5, 1)
+    sel("lt1", "lt0", [[0, 4], [16, 8], [0, 4]], A.is_ge, 11, -1)
+    TURN = [[-4, 4], [-16, 8], [-1, 4]]
     sel("lt", "lt1", TURN, A.is_gt, 0, 1)
-    sel("pi", "onb", TURN, A.is_equal, 0, 1)
+    sel("pit", "onb", TURN, A.is_equal, 0, 1)
+    sel("pi", "onb", [[-4, 8], [-32, 4], [-1, 4]], A.is_equal, 0, 1)
+    sel("bt0", "onb", [[0, 4], [-16, 8], [0, 4]], A.is_ge, 0, 1)
+    sel("bt", "bt0", [[0, 4], [16, 8], [0, 4]], A.is_ge, 15, -1)
     sel("wr", "bm", [[1, 128]], A.is_ge, 0, -1)
     iota(B("rw"), [[0, 8], [256, 16]], 0, 0, "rw", 128)
-    fill("zero", 0.0)
-    for j in range(NT):
-        cp(200, B("ct%d" % j), B("zero"), r=("zero",), w=("ct%d" % j,))
-    for name, x in (("t2k", 2048.0), ("tbig", 65536.0 - 2.0 ** 23), ("teps", 0.125), ("m192", -192.0)):
+    for name, x in (("t2k", 2048.0), ("tbig", 65536.0 - 2.0 ** 23), ("m192", -192.0)):
         fill(name, x)
-    for name, x in (("nid", -1.0), ("i32", 32.0), ("n32", -32.0), ("i4k", 4096.0)):
-        ts(64, B(name), B("idb"), x, A.mult, r=("idb",), w=(name,))
+    for name, src, x in (("nid", "idb", -1.0), ("i32", "idb", 32.0), ("i4k", "idb", 4096.0), ("npt", "pit", -1.0)):
+        act(128, B(name), B(src), F.Identity, scale=x, r=(src,), w=(name,))
     I, N_ = B("idb"), B("nid")
     ici = T.ici
     for j, (sh, m) in enumerate(((0, 15), (0, 3), (2, 3), (0, 7), (5, 3), (5, 1), (4, 1), (6, 1))):
@@ -268,11 +285,10 @@ def rank_program(g, core, T, topo):
         return lambda d, n=128: (B(name, 16 - d, 16 - d + n), name)
     pos = lambda x: (I, x[0], ("idb", x[1]))
     neg = lambda x: (N_, x[0], ("nid", x[1]))
-    post = lambda x: (x[0], I, ("idb", x[1]))
-    negt = lambda x: (x[0], N_, ("nid", x[1]))
-    kt, ktt = col(cc, 4.0, A.mult, sd, A.add, r=KF)
-    z1, z1t = col(kt, 5.0, A.is_ge, 999.0, A.mult, r=(ktt,))
-    z2, z2t = col(kt, 11.0, A.is_ge, -995.0, A.mult, r=(ktt,))
+    post = lambda x: (B("pit"), x[0], ("pit", x[1]))
+    negt = lambda x: (B("npt"), x[0], ("npt", x[1]))
+    z1, z1t = col(kc, 5.0, A.is_ge, 999.0, A.mult, r=KF)
+    z2, z2t = col(kc, 11.0, A.is_ge, -995.0, A.mult, r=KF)
     Z = term("jr", z1, z2, (z1t, z2t))
     n8, n8t = col(kc, 8.0, A.is_ge, -1.0, A.mult, r=KF)
     v1, v1t = col(cc, 3.0, A.is_ge, 999.0, A.mult, r=KF)
@@ -281,13 +297,16 @@ def rank_program(g, core, T, topo):
     c1, c1t = col(cc, 1.0, A.is_ge, r=KF)
     c2, c2t = col(cc, 2.0, A.is_ge, r=KF)
     LO, HI, LO8, HI8 = [term("jr", a, b_, (at, bt)) for a, at, b_, bt in ((c2, c2t, v3, v3t), (c1, c1t, v3, v3t), (c2, c2t, v2, v2t), (c1, c1t, v2, v2t))]
-    summed("wz", 0, 128, 4, [[neg(Z(0)), neg(Z(1))], [pos(Z(1)), pos(Z(2))], [pos(LO(0)), neg(HI(1)), pos(LO8(8)), neg(HI8(9))]])
+    summed("wz", 0, 128, 4, [[post(Z(1)), post(Z(2))], [negt(Z(0)), negt(Z(1))], [pos(LO(0)), neg(HI(1)), pos(LO8(8)), neg(HI8(9))]])
     a1, a1t = col(i8, 7.0, A.is_ge, 999.0, A.mult, r=KF)
     a2, a2t = col(i8, n8, A.subtract, r=("kf", n8t))
     a3, a3t = col(kc, 7.0, A.is_ge, 999.0, A.mult, r=KF)
     TA, TA2, TB = term("jr", i8, a1, ("kf", a1t)), term("jr", a2, a1, (a1t, a2t)), term("jr", kc, a3, ("kf", a3t))
-    summed("cat", 0, 128, 5, [[negt(TA(5)), post(TA2(6)), post(TA2(-1))], [negt(TB(5)), post(TB(8)), post(TB(1))]])
-    summed("ca", 0, 128, 6, [[pos(TA(5)), neg(TA2(6)), neg(TA2(-1))], [pos(TB(5)), neg(TB(8)), neg(TB(1))]])
+    for q, (terms, x, xt_, lim) in enumerate((([pos(TA(5)), neg(TA2(6)), neg(TA2(-1))], a2, a2t, 6.0), ([pos(TB(5)), neg(TB(8)), neg(TB(1))], kc, "kf", 4.0))):
+        sg, sgt = col(x, lim, A.is_lt, 0.5, A.subtract, r=(xt_,))
+        mms(6, 128 * q, 128 * q + 128, terms)
+        act(128, B("ca", 128 * q, 128 * q + 128), pb[6][:, 128 * q:128 * q + 128], F.Identity, scale=sg, r=(sgt,), w=("ca",), b=(6,))
+    summed("cat", 0, 128, 5, [[(B("ca", 128 * q, 128 * q + 128), N_, ("ca", "nid"))] for q in range(2)])
     summed("wt", 0, 256, 5, [[(B("lt"), B("cat"), ("lt", "cat"))]])
     ts(16, B("ek"), B("ia", 0, 16), kc, A.is_equal, r=("ia", "kf"), w=("ek",))
     two = B("two")
@@ -295,7 +314,7 @@ def rank_program(g, core, T, topo):
     tt(2, two[:, 2:4], B("ek", 4, 7, 2), B("ek", 8, 11, 2), A.subtract, r=("ek",), w=("two1",))
     for j in range(2):
         ts(1, two[:, 4 + j:5 + j], B("ek", 2 * j, 2 * j + 1), 2.0, A.mult, two[:, 2 + j:3 + j], A.add, r=("ek", "two1"), w=("two%d" % (2 + j),))
-        ts(64, B(("wl0", "wl2")[j]), B("bm"), two[:, j:j + 1], A.mult, r=("bm", "two0"), w=(("wl0", "wl2")[j],))
+        ts(64, B(("wl0", "wl2")[j]), B("bt"), two[:, j:j + 1], A.mult, r=("bt", "two0"), w=(("wl0", "wl2")[j],))
         ts(64, B(("sp0", "sp2")[j]), B("bm"), two[:, 4 + j:5 + j], A.mult, r=("bm", "two%d" % (2 + j)), w=(("sp0", "sp2")[j],))
     ts(64, B("wsn", 0, 128), B("bm"), n8, A.mult, r=("bm", n8t), w=("wsn",))
     cp(64, B("wsn", 128, 192), B("wsn", 0, 64), r=("wsn",), w=("wsnx",))
@@ -307,8 +326,8 @@ def rank_program(g, core, T, topo):
     UA, UB, UC = term("ia", b2, 0.0, (b2t,)), term("ia", b2, 64.0, (b2t,)), term("ia", b3, 0.0, (b3t,))
     ko, kot = col(kc, od, A.mult, r=KF)
     ke, ket = col(kc, ko, A.subtract, r=("kf", kot))
-    ts(64, B("dke"), I, ke, A.mult, r=("idb", ket), w=("dke",))
-    ts(64, B("dko"), I, ko, A.mult, r=("idb", kot), w=("dko",))
+    act(128, B("dke"), I, F.Identity, scale=ke, r=("idb", ket), w=("dke",))
+    act(128, B("dko"), I, F.Identity, scale=ko, r=("idb", kot), w=("dko",))
     summed("al", 0, 144, 7, [[(B(m), u(16, 144)[0], (m, u(0)[1])) for u in (UA, UB, UC)] for m in ("dke", "dko")])
     summed("hm", 0, 64, 6, [[pos((B("idb", 64 * (j // 2), 64 * (j // 2) + 64), "idb"))] for j in range(4)])
     k16, k16t = col(kc, 16.0, A.mult, r=KF)
@@ -329,18 +348,20 @@ def rank_program(g, core, T, topo):
                 lo = s * 192 + first[c]
                 cp(wid[c], T.off0[:, tab(H, c, s)], T["homi%d" % H][:, lo:lo + wid[c]], r=("homi%d_0" % H, "homi%d_1" % H), w=(otok(0, H, c, s),))
     xt = lambda H: ("x%d" % H, "xl%d_0" % H, "xl%d_1" % H)
-    G = lambda s, H, p, lo=0, st=1: T["g%d_%d" % (s, H)][:, SUB * p + lo:SUB * p + SUB:st]
     gt = lambda s, H, p: "g%d_%d_%d" % (s, H, p)
 
-    def gather(v, H, c, p, s):
-        lo = tab(H, c, s).start + 32 * p - first[c]
-        in_ = T["xs%d" % H][:, 0:4096].indirect(T["off%d" % v][:, lo:lo + 32])
-        r, w = xt(H) + (otok(v, H, c, s),), (gt(s, H, p),)
-        sc = -1.0 if BYDMA(v, H, c) and s else 1.0
+    def G(s, H, p, lo=0, st=1, n=1):
+        at = SUB * (3 * p + s - 1 if s else p)
+        return T["g%d_%d" % (min(s, 1), H)][:, at + lo:at + n * SUB:st]
+
+    def gather(v, H, c, p, call):
+        s, n = call[0], len(call)
+        in_ = T["xs%d" % H][:, 0:4096].indirect(T["off%d" % v][:, tab(H, c, s, n)])
+        r, w = xt(H) + tuple(otok(v, H, c, e) for e in call), tuple(gt(e, H, p) for e in call)
         if BYVEC(v, H, p, s):
-            ts(0, G(s, H, p), in_, sc, A.mult, r=r, w=w, cost=55 + GAM * SUB)
+            cp(0, G(s, H, p, n=n), in_, r=r, w=w, cost=55 + GAM * SUB * n)
         else:
-            act(0, G(s, H, p), in_, F.Copy, scale=sc, r=r, w=w, cost=70 + GAM * SUB)
+            act(0, G(s, H, p, n=n), in_, F.Copy, r=r, w=w, cost=70 + GAM * SUB * n)
     turn = {"f": 0, "d": 0, "t": 0}
 
     def piece(v, H, c, p, C):
@@ -348,60 +369,40 @@ def rank_program(g, core, T, topo):
         turn["d"] += 1
         D = lambda j, lo=0, st=1: T["d%d" % dn][:, SUB * j + lo:SUB * j + SUB:st]
         dt = lambda j: "d%d_%d" % (dn, j)
-        todo = [10 - (1 if BYDMA(v, H, c) else 0), 0]
+        todo = [10, 0]
 
         def red(view, m, tok):
             one = lambda k, l, s, e: lambda: g.tensor.matmul(out=pb[SUMS][:, k:96:4], lhsT=l, rhs=m, start=s, stop=e)
             op("pe", [one(k, view(k), todo[1] == 0 and k == 0, todo[1] == todo[0] - 1 and k == 3) for k in range(4)], PEC * 256, (tok, "red"), (), (SUMS,))
             todo[1] += 1
 
-        def fills(terms):
+        def fills(s):
             bank = FILLS[turn["f"] % len(FILLS)]
             turn["f"] += 1
-            mms(bank, 0, SUB, [(m, G(s, H, p), (mt, gt(s, H, p))) for m, mt, s in terms])
+            mms(bank, 0, SUB, [(I, G(s, H, p), ("idb", gt(s, H, p)))])
+            red(lambda k: G(s, H, p, k, 4), RS, gt(s, H, p))
             return bank
 
-        def pair(j, s, bank, m):
+        def pair(j, s, other, bank):
             tt(SUB, D(j), G(s, H, p), pb[bank][:, 0:SUB], A.max, r=(gt(s, H, p),), w=(dt(j),), b=(bank,))
-            red(lambda k: D(j, k, 4), m, dt(j))
-
-        def strand(s, m):
-            red(lambda k: G(s, H, p, k, 4), m, gt(s, H, p))
-        if BYDMA(v, H, c):
-            u = fills([(I, "idb", 2)])
-            for j, (s, m) in enumerate(((2, RC), (1, RA), (3, RB))):
-                ts(SUB // 2, D(j), G(s, H, p), 0.0, A.max, r=(gt(s, H, p),), w=(dt(j),))
-                red(lambda k: D(j, k, 4), m, dt(j))
-                strand(s, RS)
-            pair(3, 1, u, RB)
-            u1 = fills([(I, "idb", 1)])
-            pair(4, 3, u, RA)
-            pair(5, 3, u1, RC)
-        else:
-            ab = BYABS(v, H, p)
-            u0 = fills([(I, "idb", 0)])
-            strand(0, RS)
-            pair(0, 2, u0, RC)
-            u2 = fills([(I, "idb", 2)])
-            strand(2, RS)
-            pair(1, 1, u0, RA)
-            pair(2, 1, u2, RB)
-            strand(1, RE if ab else RS)
-            pair(3, 3, u0, RB)
-            u1 = fills([(I, "idb", 1)] + ([(N_, "nid", 3)] if ab else []))
-            pair(4, 3, u2, RA)
-            strand(3, RE if ab else RS)
-            if ab:
-                act(SUB, D(5), pb[u1][:, 0:SUB], F.Abs, w=(dt(5),), b=(u1,))
-                red(lambda k: D(5, k, 4), RD, dt(5))
-            else:
-                pair(5, 3, u1, RC)
+            red(lambda k: D(j, k, 4), (RA, RC, RB)[(s ^ other) - 1], dt(j))
+        a, b_, c_, d = [s for call in GC for s in call]
+        ua = fills(a)
+        pair(0, b_, a, ua)
+        ub = fills(b_)
+        pair(1, c_, a, ua)
+        pair(2, c_, b_, ub)
+        pair(3, d, a, ua)
+        uc = fills(c_)
+        pair(4, d, b_, ub)
+        red(lambda k: G(d, H, p, k, 4), RS, gt(d, H, p))
+        pair(5, d, c_, uc)
         ct = "ct%d" % (turn["t"] % NT)
         turn["t"] += 1
-        copy("ct", 96, B(ct, 3, 387, 4), pb[SUMS][:, 0:96], (ct,), SUMS)
-        for q in range(3):
-            lo = q * wid[c] + 32 * p - first[c]
-            mms(C, lo, lo + 32, [(B(ct, 3 - h + 128 * q, 131 - h + 128 * q), B("sel", 32 * h, 32 * h + 32), (ct, "sel")) for h in range(4)])
+        copy("ct", 96, B(ct), pb[SUMS][:, 0:96], (ct,), SUMS)
+        one = lambda q, h, lo: lambda: g.tensor.matmul(out=pb[C][32 * h:32 * h + 32, lo:lo + 32], lhsT=B(ct, 32 * q, 32 * q + 32),
+                                                       rhs=B("sel", 32 * h, 32 * h + 32), start=True, stop=True)
+        op("pe", [one(q, h, q * wid[c] + 32 * p - first[c]) for q in range(3) for h in range(4)], PEC * 384, (ct, "sel"), (), (C,))
 
     def chunk(v, H, c, k):
         C, U, w = CRIT[k % len(CRIT)], UPD[k % len(UPD)], wid[c]
@@ -424,30 +425,29 @@ def rank_program(g, core, T, topo):
         at = "acc%d_%d" % (H, c)
         act(w, P("o", 0), pc(4, 5), F.Relu, n8, 1.0 if "u" in ONVEC else 0.5, accum=B("acc", 4 * H + c, 4 * H + c + 1), r=(n8t,), w=(n("o"), at), b=(C,))
         o = P("o", 0)
-        mc(5, 6, [(B("wl0"), o, ("wl0", n("o")))])
-        mc(6, 7, [(B("wl2"), o, ("wl2", n("o")))])
+        mc(5, 6, [(B("wl2"), o, ("wl2", n("o")))])
+        mc(6, 7, [(B("wl0"), o, ("wl0", n("o")))])
         tt(2 * w, P("y", 0, 2), P("ab", 0, 2), pc(5, 7), A.mult, r=(n("ab"),), w=(n("y"),), b=(C,))
         for q in range(2):
             m = B("wt", 128 * q, 128 * q + 128)
-            mc(q, q + 1, [(m, B("teps", 0, w), ("wt", "teps")), (m, P("y", 0), (n("y"),)), (m, P("y", 1), (n("y"),))])
+            mc(q, q + 1, [(m, P("y", 0), ("wt", n("y"))), (m, P("y", 1), (n("y"),))])
         if "tu" in ONVEC:
-            ts(2 * w, P("tu", 0, 2), pc(0, 2), 0.0, A.is_gt, 0.5, A.subtract, w=(n("tu"),), b=(C,))
+            ts(2 * w, P("tu", 0, 2), pc(0, 2), 0.0, A.is_ge, 0.5, A.subtract, w=(n("tu"),), b=(C,))
         else:
-            act(2 * w, P("tu", 0, 2), pc(0, 2), F.Sign, w=(n("tu"),), b=(C,))
+            act(2 * w, P("tu", 0, 2), pc(0, 2), F.Sign, 0.25, w=(n("tu"),), b=(C,))
         mc(2, 3, [(B("ca", 128 * q, 128 * q + 128), P("tu", q), ("ca", n("tu"))) for q in range(2)])
         om, omt = B("om%d" % H, first[c], first[c] + w), "om%d_%d" % (H, c)
-        z = 2.0 if "tu" in ONVEC else 1.0
+        z = 4.0 if "tu" in ONVEC else 2.0
         if "om" in ONVEC:
             ts(w, om, pc(2, 3), 5.5 / z, A.is_ge, w=(omt,), b=(C,))
         else:
             act(w, om, pc(2, 3), F.Relu, -5.0, z, w=(omt,), b=(C,))
-        if c == len(CH) - 1:
-            blend(v, H, k)
+        rest = blend(v, H, k) if c == PORD[-1] else iter((0,))
+        next(rest)
         lab[0] = "u"
         ts(2 * w, P("st", 0, 4), T["off%d" % v][:, tab(H, c, 0, 4)], -2048.0, A.add, r=tuple(otok(v, H, c, s) for s in range(4)), w=(n("st"),))
         mu(2, 5, [up("st", 0, 3)])
-        mu(0, 1, [(B("pi"), P("ab", 1), ("pi", n("ab")))])
-        mu(1, 2, [(B("pi"), P("ab", 0), ("pi", n("ab")))])
+        mu(0, 2, [(B("pi"), P("ab", 0, 2), ("pi", n("ab")))])
         gm = (B("wr"), om, ("wr", omt))
         for q in range(2):
             mu(5 + q, 6 + q, [(B("mz", 128 * q, 128 * q + 128), o, ("mz", n("o"))), gm])
@@ -458,24 +458,28 @@ def rank_program(g, core, T, topo):
         tt(2 * w, P("zz", 0, 2), pm, pu(0, 2), A.mult, r=(n("pm"),), w=(n("zz"),), b=(U,))
         for q in range(2):
             mu(6 + q, 7 + q, [(B("w5"), o, ("w5", n("o"))), gm])
-        mu(1, 4, [up("st", 0, 3)], True, False)
+        mu(1, 5, [up("st", 0, 4)], True, False)
         mu(1, 3, [up("f2", 0, 2), dn("f1", 0, 2)], False, False)
         mu(2, 4, [up("f1", 0, 2), dn("f2", 0, 2)], False, True)
-        mu(0, 1, [(B("pi"), P("ab", 2), ("pi", n("ab"))), up("zz", 0), up("zz", 1)])
         th = "thf%d_%d" % (H, v % 2)
-        ts(w, P("vv", 0), pu(0, 1), B("thf", 2 * H + v % 2, 2 * H + v % 2 + 1), A.is_gt, r=(th,), w=(n("vv"),), b=(U,))
-        copy("am", 3 * w, P("am", 0, 3), pu(1, 4), (n("am"),), U)
+        if VVC and (VVC > 1 or c != PORD[-1]):
+            mc(0, 1, [(B("pi"), P("ab", 2), ("pi", n("ab"))), up("zz", 0), up("zz", 1)])
+            ts(w, P("vv", 0), pc(0, 1), B("thf", 2 * H + v % 2, 2 * H + v % 2 + 1), A.is_gt, r=(th,), w=(n("vv"),), b=(C,))
+        else:
+            next(rest, None)
+            mu(0, 1, [(B("pi"), P("ab", 2), ("pi", n("ab"))), up("zz", 0), up("zz", 1)])
+            ts(w, P("vv", 0), pu(0, 1), B("thf", 2 * H + v % 2, 2 * H + v % 2 + 1), A.is_gt, r=(th,), w=(n("vv"),), b=(U,))
+        next(rest, None)
+        copy("am", 4 * w, P("am", 0, 4), pu(1, 5), (n("am"),), U)
         vv = P("vv", 0)
-        big = (I, B("tbig", 0, w), ("idb", "tbig"))
-        dk = (B("dk"), vv, ("dk", n("vv")))
-        mu(0, 2, [up("am", 0, 2)], True, False)
+        mu(2, 4, [(I, B("tbig", 0, 2 * w), ("idb", "tbig"))], True, False)
+        mu(4, 6, [(I, B("t2k", 0, 2 * w), ("idb", "t2k"))], False, False)
         for q in range(2):
             mu(q, q + 1, [(B("i4k"), vv, ("i4k", n("vv")))], False, False)
-        mu(4, 6, [(I, B("t2k", 0, 2 * w), ("idb", "t2k"))], False, False)
-        mu(5, 6, [up("st", 3)], False, False)
-        mu(4, 5, [up("am", 2)], False, True)
-        mu(2, 3, [big, (B("i32"), P("am", 2), ("i32", n("am"))), dk])
-        mu(3, 4, [big, (B("i32"), P("st", 3), ("i32", n("st"))), dk])
+            mu(2 + q, 3 + q, [(B("dk"), vv, ("dk", n("vv")))], False, False)
+        mu(0, 2, [up("am", 0, 2)], False, False)
+        mu(4, 6, [up("am", 2, 4)], False, False)
+        mu(2, 4, [(B("i32"), P("am", 2, 4), ("i32", n("am")))], False, True)
         if "sr" in ONVEC:
             ts(2 * w, P("sr", 0, 2), pu(0, 2), -2048.0, A.add, 0.0, A.max, w=(n("sr"),), b=(U,))
         else:
@@ -502,19 +506,20 @@ def rank_program(g, core, T, topo):
         else:
             act(3 * w, snd[:, tab(H, c, 0, 3, 3)], pu(1, 4), F.Identity, 2048.0, w=(sdt,), b=(U,))
             act(w, ysb[:, first[c]:first[c] + w], pu(0, 1), F.Identity, 2048.0, w=(otok(VI, H, c, 0),), b=(U,))
-        tr = []
-        for s in (1, 2, 3):
-            dst = T.cores[(rank + STEP[s]) % len(T.cores)]
-            rid, pid, _ = topo.addr(dst)
-            e = topo.engines(core, dst)
-            if v < VI - 1:
-                land = T["off%d" % (v + 1)][:, tab(H, c, s)]
-            else:
-                land = ysb[:, s * TW + first[c]:s * TW + first[c] + w]
-            tr.append(RemoteDMATransfer(dst_ids=[DstId(rid=rid, pnc=pid)], dma_engine_mask=(1 << e[2 * s - 2]) | (1 << e[2 * s - 1]),
-                                        remote_sem=T.sem["arr%d_%d" % (v, k % (2 * len(CH)))], src=snd[:, tab(H, c, s - 1, 1, 3)], dst=land))
-        op("pool", [lambda: g.remote_dma_fused(tr, local_sem=T.sem.sent)], 1000.0, (sdt,), ("go%d" % k,), ext="send")
-        op(None, [], 0.0, ("go%d" % k,), tuple(otok(v + 1, H, c, s) for s in (1, 2, 3)), ext=("arr%d_%d" % (v, k % (2 * len(CH))), 6), lat=NET)
+        for j, call in enumerate(CALLS):
+            tr, sem = [], "arr%d_%d_%d" % (v, k % (2 * len(CH)), j)
+            for s, lo, hi in call:
+                dst = T.cores[(rank + STEP[s]) % len(T.cores)]
+                rid, pid, _ = topo.addr(dst)
+                if v < VI - 1:
+                    land = T["off%d" % (v + 1)][:, tab(H, c, s)]
+                else:
+                    land = ysb[:, s * TW + first[c]:s * TW + first[c] + w]
+                tr.append(RemoteDMATransfer(dst_ids=[DstId(rid=rid, pnc=pid)], dma_engine_mask=sum(1 << e for e in topo.engines(core, dst)[lo:hi]),
+                                            remote_sem=T.sem[sem], src=snd[:, tab(H, c, s - 1, 1, 3)], dst=land))
+            ne = sum(hi - lo for s, lo, hi in call)
+            op("pool", [(lambda t_: lambda: g.remote_dma_fused(t_, local_sem=T.sem.sent))(tr)], 1000.0, (sdt,), (sem,), ext=("send", ne))
+            op(None, [], 0.0, (sem,), tuple(otok(v + 1, H, c, s) for s, lo, hi in call), ext=(sem, ne), lat=NET)
 
     def blend(v, H, k):
         C, xs, li = CRIT[k % len(CRIT)], T["xs%d" % H], T["lists%d" % H]
@@ -528,6 +533,7 @@ def rank_program(g, core, T, topo):
         ts(22, li[:, 0:22], lt[:, 0:22], k16, A.add, r=(ltt, k16t), w=(lit,))
         ts(6, li[:, 24:30], lt[:, 16:22], k17, A.add, r=(ltt, k17t), w=(lit + "x",))
         gs, gx, tq = ["%s%d" % (s, H) for s in ("gs", "gx", "tq")]
+        yield
         act(0, B(gs), T["g0_%d" % H][:, 0:1536].indirect(li[:, 16:22]), F.Copy, r=(lit,) + tuple(gt(0, H, p) for p in range(3)), w=(gs,), cost=70 + TW * GAM)
         act(0, B(gx), xs[:, 0:3072].indirect(li[:, 24:30]), F.Copy, r=(lit + "x",) + xt(H), w=(gx,), cost=70 + TW * GAM)
         at = 0
@@ -546,7 +552,7 @@ def rank_program(g, core, T, topo):
                 dma("sp", T.yx[64 * H:64 * H + 64, 1536 * c:1536 * c + 1536], xs[64 * c:64 * c + 64, 1536 * c:1536 * c + 1536], "dout", ("x%d" % H,))
             return
         nc, ab = len(CH), "accb%d" % H
-        cp(4, B(ab, 0, nc), B("acc", 4 * H, 4 * H + nc), r=tuple("acc%d_%d" % (H, c) for c in range(nc)), w=(ab,))
+        act(4, B(ab, 0, nc), B("acc", 4 * H, 4 * H + nc), F.Copy, r=tuple("acc%d_%d" % (H, c) for c in range(nc)), w=(ab,))
         mms(C, 479, 480, [(B("wsn", 64 * e, 64 * e + 128), B(ab, q, q + 1), ("wsn", "wsnx", ab)) for q in range(nc) for e in range(2)])
         cp(1, ici[:, 8 + 2 * H:9 + 2 * H], pb[C][:, 479:480], w=("ia%d" % H,), b=(C,))
         ts(1, ici[:, 9 + 2 * H:10 + 2 * H], ici[:, 8 + 2 * H:9 + 2 * H], 31, A.bitwise_and, r=("ia%d" % H,), w=("ib%d" % H,))
@@ -557,16 +563,12 @@ def rank_program(g, core, T, topo):
     for v in range(VI):
         for H in range(2):
             for c, ps in enumerate(CH):
-                lab[0] = "g"
+                lab[0], lab[1] = "g", "e" if v == VI - 1 else ""
                 for p in ps:
-                    for s in (0, 2, 1, 3):
-                        gather(v, H, c, p, s)
-                if BYDMA(v, H, c):
-                    for j, s in enumerate((2, 1, 3)):
-                        cols = slice(SUB * ps[0], SUB * ps[-1] + SUB)
-                        mine = tuple(gt(s, H, p) for p in ps)
-                        op("pool", [(lambda o_, i_: lambda: g.dma_start(out=o_, in_=i_, accum_op=A.add))(T["g%d_%d" % (s, H)][:, cols], T["g0_%d" % H][:, cols])],
-                           1000.0, mine + tuple(gt(0, H, p) for p in ps), mine, ext=("ds%d_%d_%d" % (v, H * len(CH) + c, j), 16), lat=3500.0)
+                    for call in GC:
+                        gather(v, H, c, p, call)
+            for c in PORD:
+                ps = CH[c]
                 lab[0] = "m"
                 for p in ps:
                     piece(v, H, c, p, CRIT[k % len(CRIT)])
@@ -610,11 +612,12 @@ def rank_program(g, core, T, topo):
         for j, f in enumerate(x["fns"]):
             ins = f()
             if x["ext"] is None:
-                cnt[q] += 1
-                ident[i] = ("s_" + q, cnt[q])
-                ins.then_inc(T.sem["s_" + q], 1)
-            elif x["ext"] == "send":
-                total["sent"] = total.get("sent", 0) + 6
+                if j == len(x["fns"]) - 1:
+                    cnt[q] += 1
+                    ident[i] = ("s_" + q, cnt[q])
+                    ins.then_inc(T.sem["s_" + q], 1)
+            elif x["ext"][0] == "send":
+                total["sent"] = total.get("sent", 0) + x["ext"][1]
             else:
                 ident[i] = x["ext"]
                 total[x["ext"][0]] = total.get(x["ext"][0], 0) + 16

from concourse.bass import DstId, RemoteDMATransfer
from concourse.mybir import AluOpType as A, ActivationFunctionType as F

VI = 4
TW = 96
SUB = 512
CH = ((0,), (1,), (2,))
PORD = (0, 1, 2)
VVC = 2
STEP = (0, 1, 2, 4)
CALLS = (((1, 0, 2), (2, 2, 6), (3, 6, 8)),)
FILLS, SUMS, CRIT, UPD = (0, 1), 2, (3, 4), (5, 6, 7)
ONVEC = ("src",)
ND, NT, NW = 4, 6, 6
GC = ((0,), (2,), (1,), (3,))
BYVEC = lambda v, H, p, s: H == 0 and p == 0 and s == 0

CY, PEC, GAM, SCA, WAKE, NET, FIX = 0.85, 0.38, 1.3, 3.0, 220.0, 5000.0, 12.0
TOL, SWEEPS, SHAKE = 80.0, 900, 60.0
CASES = ((0.95, 0.95, 200.0, 3500.0), (0.95, 0.95, 280.0, 5500.0), (1.0, 1.3, 200.0, 4000.0), (1.0, 0.75, 200.0, 4000.0), (1.3, 1.0, 200.0, 4500.0))
QUEUES = ("pe", "dve", "act", "pool", "sp", None)

SCRATCH = {"thi": ("sbuf", [128, 8], "int32"), "ici": ("sbuf", [128, 16], "int32"), "ip": ("sbuf", [128, 1], "int32")}
PLACE = {}
for _h in range(2):
    SCRATCH["xs%d" % _h] = ("sbuf", [128, 4096], "bfloat16")
    SCRATCH["homi%d" % _h] = ("sbuf", [128, 768], "int32")
    SCRATCH["ysb%d" % _h] = ("sbuf", [128, 384], "float32")
    SCRATCH["lists%d" % _h] = ("sbuf", [128, 32], "uint16")
    SCRATCH["g0_%d" % _h] = ("sbuf", [128, 1536], "bfloat16")
    SCRATCH["g1_%d" % _h] = ("sbuf", [128, 4608], "bfloat16")
for _v in range(VI):
    SCRATCH["off%d" % _v] = ("sbuf", [128, 768], "uint16")
    SCRATCH["snd%d" % _v] = ("sbuf", [128, 576], "uint16" if _v < VI - 1 else "float32")
for _b in range(8):
    SCRATCH["pb%d" % _b] = ("psum", [128, 512], "float32")
for _p in range(ND):
    SCRATCH["d%d" % _p] = ("sbuf", [128, 6 * SUB], "bfloat16")


def _pack(buf, dtype, names):
    at = 0
    for n, w in names:
        PLACE[n] = (buf, at, w)
        at += (w + 15) // 16 * 16
    SCRATCH[buf] = ("sbuf", [128, at], dtype)


for _p in range(NW):
    for _k, _d, _l in (("h", "float16", (("ab", 3), ("y", 2), ("zz", 2), ("st", 4), ("f1", 2), ("f2", 2), ("vv", 1), ("e1", 2), ("e2", 2), ("src", 2),
                                         ("g1", 2), ("g2", 2), ("am", 4))),
                       ("b", "bfloat16", (("u", 1), ("o", 1), ("tu", 2), ("pm", 2))),
                       ("f", "float32", (("sr", 2), ("pp", 2))),
                       ("i", "int32", (("ui", 2), ("nb", 2)))):
        _pack("w%s%d" % (_k, _p), _d, [("%s_%d" % (_n, _p), 64 * _w) for _n, _w in _l])
_pack("cts", "float16", [("ct%d" % _p, 96) for _p in range(NT)] + [("dk", 128)])
_pack("blb", "bfloat16", [("%s%d" % (_n, _h), _w) for _h in range(2) for _n, _w in (("om", 96), ("gs", 96), ("gx", 96), ("tq", 192), ("accb", 4))])
_pack("conb", "bfloat16", [(_n, 128) for _n in ("idb", "nid", "i32", "npt", "i4k", "onb", "t2k", "tbig", "pit", "bt0", "bt", "sel", "pi", "bm0", "bm", "lt0", "lt1", "lt",
                                                "wr", "w5", "wl0", "wl2", "sp0", "sp2", "rw", "dke", "dko")] +
      [("hm", 256), ("wsn", 192), ("red0", 64), ("red1", 64), ("red", 64), ("m192", 192), ("wz", 384), ("ca", 256), ("cat", 256), ("wt", 256), ("mz", 256),
       ("al", 288), ("ia", 160), ("jr", 160)] + [("tm%d" % _n, 160) for _n in range(11)])
_pack("conf", "float32", [("kf", 8), ("ek", 16), ("acc", 8), ("thf", 4), ("lt32", 64), ("two", 8)] + [("col%d" % _n, 1) for _n in range(24)])
SEMAPHORES = ["s_pe", "s_dve", "s_act", "s_pool", "sent", "dout"] + ["d%s%d" % (_n, _h) for _n in "xht" for _h in range(4)]
SEMAPHORES += ["arr%d_%d_%d" % (_v, _c, _j) for _v in range(VI) for _c in range(2 * len(CH)) for _j in range(len(CALLS))]
CACHE = {}


def schedule(nodes):
    n = len(nodes)
    fwd, back = [[] for _ in range(n)], [[] for _ in range(n)]
    for i, x in enumerate(nodes):
        for d in x["deps"] | x["odeps"]:
            gap = nodes[d]["lat"] + WAKE if d in x["deps"] else 0.0
            fwd[d].append((i, gap))
            back[i].append((d, gap))
    cost = [x["cost"] for x in nodes]
    tail = [x["lat"] for x in nodes]
    on = [x["q"] for x in nodes]

    def sweep(succ, pred, prio, ready):
        left = [len(p) for p in pred]
        free, cand, pick, order, end = {q: 0.0 for q in QUEUES}, {q: [] for q in QUEUES}, {}, [], [0.0] * n
        for i in range(n):
            if left[i] == 0:
                cand[on[i]].append(i)
        dirty = QUEUES
        while True:
            for q in dirty:
                pick[q] = None
                if cand[q]:
                    first = max(free[q] if q else 0.0, min([ready[i] for i in cand[q]]))
                    i = max([i for i in cand[q] if ready[i] <= first + TOL], key=lambda i: prio[i])
                    pick[q] = (max(first, ready[i]), i)
            if len(order) == n:
                return order, end
            s, i = min([p for p in pick.values() if p])
            cand[on[i]].remove(i)
            order.append(i)
            e = free[on[i]] = end[i] = s + cost[i]
            dirty = [on[i]]
            for j, gap in succ[i]:
                ready[j] = max(ready[j], e + gap)
                left[j] -= 1
                if left[j] == 0:
                    cand[on[j]].append(j)
                    dirty.append(on[j])

    def span(order, f, gam, wake, net):
        free, end = {q: 0.0 for q in QUEUES}, [0.0] * n
        for i in order:
            x, q = nodes[i], on[i]
            t = max([end[d] for d in x["deps"]] + [free[q] if q else 0.0]) + cost[i] * (1.0 if q in ("pool", "sp") else f * gam if x["lab"] == "g" else f)
            free[q] = t
            end[i] = t + wake + (tail[i] if q else net)
        return max(end)
    prio = [0.0] * n
    for i in range(n - 1, -1, -1):
        prio[i] = cost[i] + max([prio[j] + gap for j, gap in fwd[i]] + [tail[i]])
    best, seed = None, 1
    for it in range(SWEEPS):
        order, end = sweep(fwd, back, prio, [0.0] * n)
        prio = sweep(back, fwd, [e + t for e, t in zip(end, tail)], list(tail))[1]
        total = sum(span(order, *m) for m in CASES)
        if best is None or total < best[0]:
            best = (total, order, prio)
        if it % 3 == 2:
            prio = []
            for p in best[2]:
                seed = seed * 16807 % 2147483647
                prio.append(p + SHAKE * (seed / 1073741823.5 - 1.0))
    CACHE["span"] = best[0] / len(CASES)
    return best[1]


def rank_program(g, core, T, topo):
    rank = T.rank_of(core)
    if rank is None:
        return
    Q = {"pe": g.tensor, "dve": g.vector, "act": g.scalar, "pool": g, "sp": g.sync}
    nodes, lastw, readers, banks = [], {}, {}, {}
    pb = [T["pb%d" % b] for b in range(8)]
    lab = ["", ""]

    def B(name, lo=0, hi=None, st=1):
        buf, at, w = PLACE[name]
        hi = w if hi is None else hi
        return T[buf][:, at + lo:at + hi:st] if st > 1 else T[buf][:, at + lo:at + hi]

    def op(q, fns, cost, r=(), w=(), b=(), ext=None, lat=0.0):
        i = len(nodes)
        deps, odeps = set(), set()
        for t in r:
            if t in lastw:
                deps.add(lastw[t])
        for t in w:
            if t in lastw:
                deps.add(lastw[t])
            deps |= readers.get(t, set())
        for t in b:
            for q2, d in banks.get(t, {}).items():
                (odeps if q2 == q else deps).add(d)
        nodes.append({"q": q, "fns": fns, "cost": cost, "deps": deps, "odeps": odeps - deps, "ext": ext, "lat": lat, "lab": lab[0], "w": w, "b": b})
        for t in r:
            readers.setdefault(t, set()).add(i)
        for t in w:
            lastw[t] = i
            readers[t] = set()
        for t in b:
            banks.setdefault(t, {})[q] = i
        return i

    def tt(n, out, in0, in1, o, r=(), w=(), b=(), cost=None):
        op("dve", [lambda: g.vector.tensor_tensor(out=out, in0=in0, in1=in1, op=o)], cost or FIX + CY * max(64, n * (1 if b else 2)), r, w, b)

    def ts(n, out, in0, s1, o0, s2=None, o1=None, r=(), w=(), b=(), cost=None):
        if o1 is None:
            op("dve", [lambda: g.vector.tensor_scalar(out=out, in0=in0, scalar1=s1, scalar2=None, op0=o0)], cost or FIX + CY * max(64, n), r, w, b)
        else:
            op("dve", [lambda: g.vector.tensor_scalar(out=out, in0=in0, scalar1=s1, scalar2=s2, op0=o0, op1=o1)], cost or FIX + CY * max(64, n), r, w, b)

    def cp(n, out, in_, r=(), w=(), b=(), cost=None):
        op("dve", [lambda: g.vector.tensor_copy(out=out, in_=in_)], cost or FIX + CY * max(64, n), r, w, b)

    def act(n, out, in_, func, bias=0.0, scale=1.0, accum=None, r=(), w=(), b=(), cost=None):
        kw = {} if accum is None else {"accum_out": accum}
        op("act", [lambda: g.scalar.activation(out=out, in_=in_, func=func, bias=bias, scale=scale, **kw)], cost or FIX + CY * max(64, n), r, w, b)

    def copy(kind, n, out, in_, w, bank):
        if kind in ONVEC:
            cp(n, out, in_, w=w, b=(bank,))
        else:
            act(n, out, in_, F.Copy, w=w, b=(bank,))

    def shift(kind, n, out, in_, x, r=(), w=(), b=()):
        if kind in ONVEC:
            ts(n, out, in_, x, A.add, r=r, w=w, b=b)
        else:
            act(n, out, in_, F.Identity, x, r=r, w=w, b=b)

    def mm(bank, out, n, terms, start=True, stop=True):
        def one(l, x, s, e):
            return lambda: g.tensor.matmul(out=out, lhsT=l, rhs=x, start=s, stop=e)
        fns = [one(x[0], x[1], start and j == 0, stop and j == len(terms) - 1) for j, x in enumerate(terms)]
        op("pe", fns, PEC * max(64, n) * len(terms), tuple({t for x in terms for t in x[2]}), (), (bank,))

    def mms(bank, lo, hi, terms, start=True, stop=True):
        mm(bank, pb[bank][:, lo:hi], hi - lo, terms, start, stop)

    def dma(q, out, in_, sem, r=(), w=(), lat=2500.0):
        op(q, [lambda: Q[q].dma_start(out=out, in_=in_)], 60.0, r, w, ext=(sem, 16), lat=lat)

    for H in range(2):
        for c in range(2):
            rows, to = slice(64 * H, 64 * H + 64), slice(64 * c, 64 * c + 64)
            dma("act", T["homi%d" % H][to, 0:672], T.hom[rows, TW * c:TW * c + 672], "dh%d" % (2 * H + c), (), ("homi%d_%d" % (H, c),), 3000.0 + 3000 * H)
            dma("sp", T["xs%d" % H][to, :], T.x[rows, :], "dx%d" % (2 * H + c), (), ("xl%d_%d" % (H, c),), 5000.0 + 3000 * H)
    for H in range(2):
        for c in range(2):
            dma("sp", T.thi[64 * c:64 * c + 64, 4 * H:4 * H + 1], T.th[64 * H:64 * H + 64, :], "dt%d" % (2 * H + c), (), ("thi%d_%d" % (H, c),), 8000.0)

    def iota(out, pattern, base, cm, w, n, flag=True):
        kw = {"allow_small_or_imprecise_dtypes": True} if flag else {}
        op("pool", [lambda: g.iota(out, pattern, base, cm, **kw)], 140 + 2 * CY * n, (), (w,))

    def sel(name, src, pattern, o, base, cm, n=128, rows=slice(0, 128), tok=None):
        out, in_ = B(name)[rows, :], B(src)[rows, :]
        op("pool", [lambda: g.affine_select(out, in_, pattern, o, 0.0, base, cm)], 180 + 2 * CY * n, (src,), (tok or name,))

    def fill(name, x, lo=0, hi=None):
        op("dve", [lambda: g.vector.memset(B(name, lo, hi), x)], FIX + CY * 64, (), (name,))
    ncol = [0]

    def col(in_, s1, o0, s2=None, o1=None, r=()):
        name = "col%d" % ncol[0]
        ncol[0] += 1
        ts(1, B(name), in_, s1, o0, s2, o1, r=r, w=(name,))
        return B(name), name

    def summed(name, lo, n, bank, parts):
        for j, terms in enumerate(parts):
            mms(bank, n * j, n * j + n, terms)
        act(n * len(parts), B(name, lo, lo + n * len(parts)), pb[bank][:, 0:n * len(parts)], F.Copy, w=(name,), b=(bank,))
    iota(T.ip[:], [[0, 1]], 0, 1, "ip", 1, False)
    fill("onb", 1.0)
    sel("idb", "onb", [[-1, 128]], A.is_equal, 0, 1)
    for lo, hi, x in ((0, 32, 0.0), (8, 64, 2.0), (16, 32, 0.0), (32, 40, -1.0), (40, 56, -2.0)):
        fill("red0", x, lo, hi)
    sel("red1", "red0", [[0, 8], [-16, 8]], A.is_ge, 0, 1, 64)
    sel("red", "red1", [[0, 8], [16, 8]], A.is_ge, 15, -1, 64)
    RA, RB, RS, RC = [B("red", 8 * j, 8 * j + 24) for j in (0, 1, 2, 5)]
    iota(B("ia"), [[1, 160]], 0, 0, "ia", 160)
    sel("sel", "onb", [[-1, 4], [-4, 32]], A.is_equal, 0, 1)
    sel("bm0", "onb", [[-16, 8], [0, 16]], A.is_ge, 0, 1)
    sel("bm", "bm0", [[16, 8], [0, 16]], A.is_ge, 15, -1)
    sel("lt0", "onb", [[0, 4], [-16, 8], [0, 4]], A.is_ge, -5, 1)
    sel("lt1", "lt0", [[0, 4], [16, 8], [0, 4]], A.is_ge, 11, -1)
    TURN = [[-4, 4], [-16, 8], [-1, 4]]
    sel("lt", "lt1", TURN, A.is_gt, 0, 1)
    sel("pit", "onb", TURN, A.is_equal, 0, 1)
    sel("pi", "onb", [[-4, 8], [-32, 4], [-1, 4]], A.is_equal, 0, 1)
    sel("bt0", "onb", [[0, 4], [-16, 8], [0, 4]], A.is_ge, 0, 1)
    sel("bt", "bt0", [[0, 4], [16, 8], [0, 4]], A.is_ge, 15, -1)
    sel("wr", "bm", [[1, 128]], A.is_ge, 0, -1)
    iota(B("rw"), [[0, 8], [256, 16]], 0, 0, "rw", 128)
    for name, x in (("t2k", 2048.0), ("tbig", 65536.0 - 2.0 ** 23), ("m192", -192.0)):
        fill(name, x)
    for name, src, x in (("nid", "idb", -1.0), ("i32", "idb", 32.0), ("i4k", "idb", 4096.0), ("npt", "pit", -1.0)):
        act(128, B(name), B(src), F.Identity, scale=x, r=(src,), w=(name,))
    I, N_ = B("idb"), B("nid")
    ici = T.ici
    for j, (sh, m) in enumerate(((0, 15), (0, 3), (2, 3), (0, 7), (5, 3), (5, 1), (4, 1), (6, 1))):
        ts(1, ici[:, j:j + 1], T.ip[:], sh, A.arith_shift_right, m, A.bitwise_and, r=("ip",), w=("i%d" % j,))
    cp(8, B("kf"), ici[:, 0:8], r=tuple("i%d" % j for j in range(8)), w=("kf",))
    kc, cc, sd, i8, hb, gp, od, cpy = [B("kf", j, j + 1) for j in range(8)]
    KF = ("kf",)
    ts(128, B("dk"), I, kc, A.mult, 1184.0, A.mult, r=("idb", "kf"), w=("dk",))
    tg, tgt = col(T.ip[:], kc, A.subtract, 16.0, A.add, r=("ip", "kf"))
    ts(80, B("jr"), B("ia"), tg, A.subtract, r=("ia", tgt), w=("jr",))
    ntm = [0]

    def term(src, a, b_, r):
        name = "tm%d" % ntm[0]
        ntm[0] += 1
        ts(80, B(name), B(src), a, A.subtract, b_, A.is_equal, r=(src,) + r, w=(name,))
        return lambda d, n=128: (B(name, 16 - d, 16 - d + n), name)
    pos = lambda x: (I, x[0], ("idb", x[1]))
    neg = lambda x: (N_, x[0], ("nid", x[1]))
    post = lambda x: (B("pit"), x[0], ("pit", x[1]))
    negt = lambda x: (B("npt"), x[0], ("npt", x[1]))
    z1, z1t = col(kc, 5.0, A.is_ge, 999.0, A.mult, r=KF)
    z2, z2t = col(kc, 11.0, A.is_ge, -995.0, A.mult, r=KF)
    Z = term("jr", z1, z2, (z1t, z2t))
    n8, n8t = col(kc, 8.0, A.is_ge, -1.0, A.mult, r=KF)
    v1, v1t = col(cc, 3.0, A.is_ge, 999.0, A.mult, r=KF)
    v2, v2t = col(n8, -999.0, A.mult, v1, A.add, r=(n8t, v1t))
    v3, v3t = col(sd, 4.0, A.mult, v2, A.add, r=("kf", v2t))
    c1, c1t = col(cc, 1.0, A.is_ge, r=KF)
    c2, c2t = col(cc, 2.0, A.is_ge, r=KF)
    LO, HI, LO8, HI8 = [term("jr", a, b_, (at, bt)) for a, at, b_, bt in ((c2, c2t, v3, v3t), (c1, c1t, v3, v3t), (c2, c2t, v2, v2t), (c1, c1t, v2, v2t))]
    summed("wz", 0, 128, 4, [[post(Z(1)), post(Z(2))], [negt(Z(0)), negt(Z(1))], [pos(LO(0)), neg(HI(1)), pos(LO8(8)), neg(HI8(9))]])
    a1, a1t = col(i8, 7.0, A.is_ge, 999.0, A.mult, r=KF)
    a2, a2t = col(i8, n8, A.subtract, r=("kf", n8t))
    a3, a3t = col(kc, 7.0, A.is_ge, 999.0, A.mult, r=KF)
    TA, TA2, TB = term("jr", i8, a1, ("kf", a1t)), term("jr", a2, a1, (a1t, a2t)), term("jr", kc, a3, ("kf", a3t))
    for q, (terms, x, xt_, lim) in enumerate((([pos(TA(5)), neg(TA2(6)), neg(TA2(-1))], a2, a2t, 6.0), ([pos(TB(5)), neg(TB(8)), neg(TB(1))], kc, "kf", 4.0))):
        sg, sgt = col(x, lim, A.is_lt, 0.5, A.subtract, r=(xt_,))
        mms(6, 128 * q, 128 * q + 128, terms)
        act(128, B("ca", 128 * q, 128 * q + 128), pb[6][:, 128 * q:128 * q + 128], F.Identity, scale=sg, r=(sgt,), w=("ca",), b=(6,))
    summed("cat", 0, 128, 5, [[(B("ca", 128 * q, 128 * q + 128), N_, ("ca", "nid"))] for q in range(2)])
    summed("wt", 0, 256, 5, [[(B("lt"), B("cat"), ("lt", "cat"))]])
    ts(16, B("ek"), B("ia", 0, 16), kc, A.is_equal, r=("ia", "kf"), w=("ek",))
    two = B("two")
    tt(2, two[:, 0:2], B("ek", 0, 3, 2), B("ek", 4, 7, 2), A.subtract, r=("ek",), w=("two0",))
    tt(2, two[:, 2:4], B("ek", 4, 7, 2), B("ek", 8, 11, 2), A.subtract, r=("ek",), w=("two1",))
    for j in range(2):
        ts(1, two[:, 4 + j:5 + j], B("ek", 2 * j, 2 * j + 1), 2.0, A.mult, two[:, 2 + j:3 + j], A.add, r=("ek", "two1"), w=("two%d" % (2 + j),))
        ts(64, B(("wl0", "wl2")[j]), B("bt"), two[:, j:j + 1], A.mult, r=("bt", "two0"), w=(("wl0", "wl2")[j],))
        ts(64, B(("sp0", "sp2")[j]), B("bm"), two[:, 4 + j:5 + j], A.mult, r=("bm", "two%d" % (2 + j)), w=(("sp0", "sp2")[j],))
    ts(64, B("wsn", 0, 128), B("bm"), n8, A.mult, r=("bm", n8t), w=("wsn",))
    cp(64, B("wsn", 128, 192), B("wsn", 0, 64), r=("wsn",), w=("wsnx",))
    op("pool", [lambda: g.affine_select(B("w5"), B("wsn", 0, 128), [[0, 8], [1, 16]], A.is_ge, 0.0, -5, 0)], 410, ("wsn",), ("w5",))
    summed("mz", 0, 128, 7, [[pos((B("w5"), "w5")), pos((B(s), s))] for s in ("sp2", "sp0")])
    b1, b1t = col(gp, 32.0, A.mult, 16.0, A.add, r=KF)
    b2, b2t = col(cpy, 6.0, A.mult, b1, A.add, r=("kf", b1t))
    b3, b3t = col(hb, 32.0, A.mult, 32.0, A.add, r=KF)
    UA, UB, UC = term("ia", b2, 0.0, (b2t,)), term("ia", b2, 64.0, (b2t,)), term("ia", b3, 0.0, (b3t,))
    ko, kot = col(kc, od, A.mult, r=KF)
    ke, ket = col(kc, ko, A.subtract, r=("kf", kot))
    act(128, B("dke"), I, F.Identity, scale=ke, r=("idb", ket), w=("dke",))
    act(128, B("dko"), I, F.Identity, scale=ko, r=("idb", kot), w=("dko",))
    summed("al", 0, 144, 7, [[(B(m), u(16, 144)[0], (m, u(0)[1])) for u in (UA, UB, UC)] for m in ("dke", "dko")])
    summed("hm", 0, 64, 6, [[pos((B("idb", 64 * (j // 2), 64 * (j // 2) + 64), "idb"))] for j in range(4)])
    k16, k16t = col(kc, 16.0, A.mult, r=KF)
    k17, k17t = col(cpy, 1536.0, A.mult, k16, A.add, r=("kf", k16t))
    for H in range(2):
        cp(1, B("thf", 2 * H, 2 * H + 1), T.thi[:, 4 * H:4 * H + 1], r=("thi%d_0" % H, "thi%d_1" % H), w=("thf%d_0" % H,))

    first = [32 * c[0] for c in CH]
    wid = [32 * len(c) for c in CH]

    def tab(H, c, s, n=1, per=4):
        lo = per * (TW * H + first[c]) + s * wid[c]
        return slice(lo, lo + n * wid[c])
    otok = lambda v, H, c, s: "off%d_%d_%d_%d" % (v, H, c, s)
    for H in range(2):
        for c in range(len(CH)):
            for s in (0, 2, 1, 3):
                lo = s * 192 + first[c]
                cp(wid[c], T.off0[:, tab(H, c, s)], T["homi%d" % H][:, lo:lo + wid[c]], r=("homi%d_0" % H, "homi%d_1" % H), w=(otok(0, H, c, s),))
    xt = lambda H: ("x%d" % H, "xl%d_0" % H, "xl%d_1" % H)
    gt = lambda s, H, p: "g%d_%d_%d" % (s, H, p)

    def G(s, H, p, lo=0, st=1, n=1):
        at = SUB * (3 * p + s - 1 if s else p)
        return T["g%d_%d" % (min(s, 1), H)][:, at + lo:at + n * SUB:st]

    def gather(v, H, c, p, call):
        s, n = call[0], len(call)
        in_ = T["xs%d" % H][:, 0:4096].indirect(T["off%d" % v][:, tab(H, c, s, n)])
        r, w = xt(H) + tuple(otok(v, H, c, e) for e in call), tuple(gt(e, H, p) for e in call)
        if BYVEC(v, H, p, s):
            cp(0, G(s, H, p, n=n), in_, r=r, w=w, cost=55 + GAM * SUB * n)
        else:
            act(0, G(s, H, p, n=n), in_, F.Copy, r=r, w=w, cost=70 + GAM * SUB * n)
    turn = {"f": 0, "d": 0, "t": 0}

    def piece(v, H, c, p, C):
        dn = turn["d"] % ND
        turn["d"] += 1
        D = lambda j, lo=0, st=1: T["d%d" % dn][:, SUB * j + lo:SUB * j + SUB:st]
        dt = lambda j: "d%d_%d" % (dn, j)
        todo = [10, 0]

        def red(view, m, tok):
            one = lambda k, l, s, e: lambda: g.tensor.matmul(out=pb[SUMS][:, k:96:4], lhsT=l, rhs=m, start=s, stop=e)
            op("pe", [one(k, view(k), todo[1] == 0 and k == 0, todo[1] == todo[0] - 1 and k == 3) for k in range(4)], PEC * 256, (tok, "red"), (), (SUMS,))
            todo[1] += 1

        def fills(s):
            bank = FILLS[turn["f"] % len(FILLS)]
            turn["f"] += 1
            mms(bank, 0, SUB, [(I, G(s, H, p), ("idb", gt(s, H, p)))])
            red(lambda k: G(s, H, p, k, 4), RS, gt(s, H, p))
            return bank

        def pair(j, s, other, bank):
            tt(SUB, D(j), G(s, H, p), pb[bank][:, 0:SUB], A.max, r=(gt(s, H, p),), w=(dt(j),), b=(bank,))
            red(lambda k: D(j, k, 4), (RA, RC, RB)[(s ^ other) - 1], dt(j))
        a, b_, c_, d = [s for call in GC for s in call]
        ua = fills(a)
        pair(0, b_, a, ua)
        ub = fills(b_)
        pair(1, c_, a, ua)
        pair(2, c_, b_, ub)
        pair(3, d, a, ua)
        uc = fills(c_)
        pair(4, d, b_, ub)
        red(lambda k: G(d, H, p, k, 4), RS, gt(d, H, p))
        pair(5, d, c_, uc)
        ct = "ct%d" % (turn["t"] % NT)
        turn["t"] += 1
        copy("ct", 96, B(ct), pb[SUMS][:, 0:96], (ct,), SUMS)
        one = lambda q, h, lo: lambda: g.tensor.matmul(out=pb[C][32 * h:32 * h + 32, lo:lo + 32], lhsT=B(ct, 32 * q, 32 * q + 32),
                                                       rhs=B("sel", 32 * h, 32 * h + 32), start=True, stop=True)
        op("pe", [one(q, h, q * wid[c] + 32 * p - first[c]) for q in range(3) for h in range(4)], PEC * 384, (ct, "sel"), (), (C,))

    def chunk(v, H, c, k):
        C, U, w = CRIT[k % len(CRIT)], UPD[k % len(UPD)], wid[c]
        n = lambda s: "%s_%d" % (s, k % NW)
        P = lambda s, a, b_=None: B(n(s), a * w, (a + 1 if b_ is None else b_) * w)
        pc = lambda a, b_: pb[C][:, a * w:b_ * w]
        pu = lambda a, b_: pb[U][:, a * w:b_ * w]
        mc = lambda a, b_, terms: mms(C, a * w, b_ * w, terms)
        mu = lambda a, b_, terms, start=True, stop=True: mms(U, a * w, b_ * w, terms, start, stop)
        up = lambda s, a, b_=None: (I, P(s, a, b_), ("idb", n(s)))
        dn = lambda s, a, b_=None: (N_, P(s, a, b_), ("nid", n(s)))
        lab[0] = "c"
        copy("ab", 3 * w, P("ab", 0, 3), pc(0, 3), (n("ab"),), C)
        mc(3, 4, [(B("wz", 128 * q, 128 * q + 128), P("ab", q), ("wz", n("ab"))) for q in range(2)])
        if "u" in ONVEC:
            ts(w, P("u", 0), pc(3, 4), 0.0, A.is_ge, 0.5, A.subtract, w=(n("u"),), b=(C,))
        else:
            act(w, P("u", 0), pc(3, 4), F.Sign, 0.5, w=(n("u"),), b=(C,))
        mc(4, 5, [(B("wz", 256, 384), P("u", 0), ("wz", n("u")))])
        at = "acc%d_%d" % (H, c)
        act(w, P("o", 0), pc(4, 5), F.Relu, n8, 1.0 if "u" in ONVEC else 0.5, accum=B("acc", 4 * H + c, 4 * H + c + 1), r=(n8t,), w=(n("o"), at), b=(C,))
        o = P("o", 0)
        mc(5, 6, [(B("wl2"), o, ("wl2", n("o")))])
        mc(6, 7, [(B("wl0"), o, ("wl0", n("o")))])
        tt(2 * w, P("y", 0, 2), P("ab", 0, 2), pc(5, 7), A.mult, r=(n("ab"),), w=(n("y"),), b=(C,))
        for q in range(2):
            m = B("wt", 128 * q, 128 * q + 128)
            mc(q, q + 1, [(m, P("y", 0), ("wt", n("y"))), (m, P("y", 1), (n("y"),))])
        if "tu" in ONVEC:
            ts(2 * w, P("tu", 0, 2), pc(0, 2), 0.0, A.is_ge, 0.5, A.subtract, w=(n("tu"),), b=(C,))
        else:
            act(2 * w, P("tu", 0, 2), pc(0, 2), F.Sign, 0.25, w=(n("tu"),), b=(C,))
        mc(2, 3, [(B("ca", 128 * q, 128 * q + 128), P("tu", q), ("ca", n("tu"))) for q in range(2)])
        om, omt = B("om%d" % H, first[c], first[c] + w), "om%d_%d" % (H, c)
        z = 4.0 if "tu" in ONVEC else 2.0
        if "om" in ONVEC:
            ts(w, om, pc(2, 3), 5.5 / z, A.is_ge, w=(omt,), b=(C,))
        else:
            act(w, om, pc(2, 3), F.Relu, -5.0, z, w=(omt,), b=(C,))
        rest = blend(v, H, k) if c == PORD[-1] else iter((0,))
        next(rest)
        lab[0] = "u"
        ts(2 * w, P("st", 0, 4), T["off%d" % v][:, tab(H, c, 0, 4)], -2048.0, A.add, r=tuple(otok(v, H, c, s) for s in range(4)), w=(n("st"),))
        mu(2, 5, [up("st", 0, 3)])
        mu(0, 2, [(B("pi"), P("ab", 0, 2), ("pi", n("ab")))])
        gm = (B("wr"), om, ("wr", omt))
        for q in range(2):
            mu(5 + q, 6 + q, [(B("mz", 128 * q, 128 * q + 128), o, ("mz", n("o"))), gm])
        pm = P("pm", 0, 2)
        ts(2 * w, pm, pu(5, 7), 2.0, A.is_equal, w=(n("pm"),), b=(U,))
        tt(2 * w, P("f1", 0, 2), pm, pu(2, 4), A.mult, r=(n("pm"),), w=(n("f1"),), b=(U,))
        tt(2 * w, P("f2", 0, 2), pm, pu(3, 5), A.mult, r=(n("pm"),), w=(n("f2"),), b=(U,))
        tt(2 * w, P("zz", 0, 2), pm, pu(0, 2), A.mult, r=(n("pm"),), w=(n("zz"),), b=(U,))
        for q in range(2):
            mu(6 + q, 7 + q, [(B("w5"), o, ("w5", n("o"))), gm])
        mu(1, 5, [up("st", 0, 4)], True, False)
        mu(1, 3, [up("f2", 0, 2), dn("f1", 0, 2)], False, False)
        mu(2, 4, [up("f1", 0, 2), dn("f2", 0, 2)], False, True)
        th = "thf%d_%d" % (H, v % 2)
        if VVC and (VVC > 1 or c != PORD[-1]):
            mc(0, 1, [(B("pi"), P("ab", 2), ("pi", n("ab"))), up("zz", 0), up("zz", 1)])
            ts(w, P("vv", 0), pc(0, 1), B("thf", 2 * H + v % 2, 2 * H + v % 2 + 1), A.is_gt, r=(th,), w=(n("vv"),), b=(C,))
        else:
            next(rest, None)
            mu(0, 1, [(B("pi"), P("ab", 2), ("pi", n("ab"))), up("zz", 0), up("zz", 1)])
            ts(w, P("vv", 0), pu(0, 1), B("thf", 2 * H + v % 2, 2 * H + v % 2 + 1), A.is_gt, r=(th,), w=(n("vv"),), b=(U,))
        next(rest, None)
        copy("am", 4 * w, P("am", 0, 4), pu(1, 5), (n("am"),), U)
        vv = P("vv", 0)
        mu(2, 4, [(I, B("tbig", 0, 2 * w), ("idb", "tbig"))], True, False)
        mu(4, 6, [(I, B("t2k", 0, 2 * w), ("idb", "t2k"))], False, False)
        for q in range(2):
            mu(q, q + 1, [(B("i4k"), vv, ("i4k", n("vv")))], False, False)
            mu(2 + q, 3 + q, [(B("dk"), vv, ("dk", n("vv")))], False, False)
        mu(0, 2, [up("am", 0, 2)], False, False)
        mu(4, 6, [up("am", 2, 4)], False, False)
        mu(2, 4, [(B("i32"), P("am", 2, 4), ("i32", n("am")))], False, True)
        if "sr" in ONVEC:
            ts(2 * w, P("sr", 0, 2), pu(0, 2), -2048.0, A.add, 0.0, A.max, w=(n("sr"),), b=(U,))
        else:
            act(2 * w, P("sr", 0, 2), pu(0, 2), F.Relu, -2048.0, w=(n("sr"),), b=(U,))
        tt(2 * w, P("pp", 0, 2), P("sr", 0, 2), pu(4, 6), A.mult, r=(n("sr"),), w=(n("pp"),), b=(U,))
        tt(2 * w, P("e1", 0, 2), P("am", 0, 2), pu(6, 8), A.mult, r=(n("am"),), w=(n("e1"),), b=(U,))
        tt(2 * w, P("ui", 0, 2), P("pp", 0, 2), pu(2, 4), A.add, r=(n("pp"),), w=(n("ui"),), b=(U,))
        ts(2 * w, P("nb", 0, 2), P("ui", 0, 2), 5, A.arith_shift_right, 4095, A.bitwise_and, r=(n("ui"),), w=(n("nb"),))
        shift("src", 2 * w, P("src", 0, 2), P("nb", 0, 2), -2048.0, r=(n("nb"),), w=(n("src"),))
        low = [up("am", 0, 2), dn("e1", 0, 2), up("e2", 0, 2)]
        tt(2 * w, P("e2", 0, 2), P("src", 0, 2), pu(6, 8), A.mult, r=(n("src"),), w=(n("e2"),), b=(U,))
        mu(4, 6, low, True, False)
        mu(6, 7, [up("e1", 0), up("src", 0), dn("e2", 0)], False, True)
        mu(0, 2, low, True, False)
        mu(2, 4, [up("e1", 0, 2), up("src", 0, 2), dn("e2", 0, 2)], False, False)
        tt(2 * w, P("g1", 0, 2), pm, pu(4, 6), A.mult, r=(n("pm"),), w=(n("g1"),), b=(U,))
        tt(2 * w, P("g2", 0, 2), pm, pu(5, 7), A.mult, r=(n("pm"),), w=(n("g2"),), b=(U,))
        mu(0, 2, [up("g2", 0, 2), dn("g1", 0, 2)], False, False)
        mu(1, 3, [up("g1", 0, 2), dn("g2", 0, 2)], False, True)
        snd, sdt, ysb = T["snd%d" % v], "snd%d_%d_%d" % (v, H, c), T["ysb%d" % H]
        if v < VI - 1:
            shift("snd", 3 * w, snd[:, tab(H, c, 0, 3, 3)], pu(1, 4), 2048.0, w=(sdt,), b=(U,))
            shift("snd", w, T["off%d" % (v + 1)][:, tab(H, c, 0)], pu(0, 1), 2048.0, w=(otok(v + 1, H, c, 0),), b=(U,))
        else:
            act(3 * w, snd[:, tab(H, c, 0, 3, 3)], pu(1, 4), F.Identity, 2048.0, w=(sdt,), b=(U,))
            act(w, ysb[:, first[c]:first[c] + w], pu(0, 1), F.Identity, 2048.0, w=(otok(VI, H, c, 0),), b=(U,))
        for j, call in enumerate(CALLS):
            tr, sem = [], "arr%d_%d_%d" % (v, k % (2 * len(CH)), j)
            for s, lo, hi in call:
                dst = T.cores[(rank + STEP[s]) % len(T.cores)]
                rid, pid, _ = topo.addr(dst)
                if v < VI - 1:
                    land = T["off%d" % (v + 1)][:, tab(H, c, s)]
                else:
                    land = ysb[:, s * TW + first[c]:s * TW + first[c] + w]
                tr.append(RemoteDMATransfer(dst_ids=[DstId(rid=rid, pnc=pid)], dma_engine_mask=sum(1 << e for e in topo.engines(core, dst)[lo:hi]),
                                            remote_sem=T.sem[sem], src=snd[:, tab(H, c, s - 1, 1, 3)], dst=land))
            ne = sum(hi - lo for s, lo, hi in call)
            op("pool", [(lambda t_: lambda: g.remote_dma_fused(t_, local_sem=T.sem.sent))(tr)], 1000.0, (sdt,), (sem,), ext=("send", ne))
            op(None, [], 0.0, (sem,), tuple(otok(v + 1, H, c, s) for s, lo, hi in call), ext=(sem, ne), lat=NET)

    def blend(v, H, k):
        C, xs, li = CRIT[k % len(CRIT)], T["xs%d" % H], T["lists%d" % H]
        lab[0] = "b"
        oms = tuple("om%d_%d" % (H, c) for c in range(len(CH)))
        for e in range(2):
            mms(C, 480 + 16 * e, 496 + 16 * e, [(B("rw")[0:1, :], B("onb", 0, 16)[0:1, :], ("rw", "onb"))] +
                [(B("al", 144 * e + 16 - r, 144 * e + 144 - r), B("om%d" % H, 16 * r, 16 * r + 16), ("al",) + oms) for r in range(6)])
        lt, ltt, lit = B("lt32", 32 * H, 32 * H + 32), "lt32_%d" % H, "li%d" % H
        op("dve", [lambda: g.vector.transpose(out=lt, in_=pb[C][:, 480:512])], FIX + 64 * CY, (), (ltt,), (C,))
        ts(22, li[:, 0:22], lt[:, 0:22], k16, A.add, r=(ltt, k16t), w=(lit,))
        ts(6, li[:, 24:30], lt[:, 16:22], k17, A.add, r=(ltt, k17t), w=(lit + "x",))
        gs, gx, tq = ["%s%d" % (s, H) for s in ("gs", "gx", "tq")]
        yield
        act(0, B(gs), T["g0_%d" % H][:, 0:1536].indirect(li[:, 16:22]), F.Copy, r=(lit,) + tuple(gt(0, H, p) for p in range(3)), w=(gs,), cost=70 + TW * GAM)
        act(0, B(gx), xs[:, 0:3072].indirect(li[:, 24:30]), F.Copy, r=(lit + "x",) + xt(H), w=(gx,), cost=70 + TW * GAM)
        at = 0
        last = v == VI - 1
        if last:
            mms(C, at, at + TW, [(I, B(s), ("idb", s)) for s in (gs, gx)])
        else:
            for c in range(2):
                mms(C, at + TW * c, at + TW * c + TW, [(B("hm", 128 * c, 128 * c + 128), B(s), ("hm", s)) for s in (gs, gx)])
        nn = TW if last else 2 * TW
        act(nn, B(tq, 0, nn), pb[C][:, at:at + nn], F.Identity, 191.75, 0.5, w=(tq,), b=(C,))
        tt(0, xs[:, 0:3072].indirect(li[:, 24:30] if last else li[:, 0:12]), B(tq, 0, nn), B("m192", 0, nn), A.add,
           r=(tq, "m192", lit, lit + "x"), w=("x%d" % H,), cost=55 + nn * SCA)
        if last:
            for c in range(2):
                dma("sp", T.yx[64 * H:64 * H + 64, 1536 * c:1536 * c + 1536], xs[64 * c:64 * c + 64, 1536 * c:1536 * c + 1536], "dout", ("x%d" % H,))
            return
        nc, ab = len(CH), "accb%d" % H
        act(4, B(ab, 0, nc), B("acc", 4 * H, 4 * H + nc), F.Copy, r=tuple("acc%d_%d" % (H, c) for c in range(nc)), w=(ab,))
        mms(C, 479, 480, [(B("wsn", 64 * e, 64 * e + 128), B(ab, q, q + 1), ("wsn", "wsnx", ab)) for q in range(nc) for e in range(2)])
        cp(1, ici[:, 8 + 2 * H:9 + 2 * H], pb[C][:, 479:480], w=("ia%d" % H,), b=(C,))
        ts(1, ici[:, 9 + 2 * H:10 + 2 * H], ici[:, 8 + 2 * H:9 + 2 * H], 31, A.bitwise_and, r=("ia%d" % H,), w=("ib%d" % H,))
        w = (v + 1) % 2
        tt(1, B("thf", 2 * H + w, 2 * H + w + 1), ici[:, 9 + 2 * H:10 + 2 * H], T.thi[:, 4 * H:4 * H + 1], A.add, r=("ib%d" % H, "thi%d_0" % H, "thi%d_1" % H), w=("thf%d_%d" % (H, w),))

    k = 0
    for v in range(VI):
        for H in range(2):
            for c, ps in enumerate(CH):
                lab[0], lab[1] = "g", "e" if v == VI - 1 else ""
                for p in ps:
                    for call in GC:
                        gather(v, H, c, p, call)
            for c in PORD:
                ps = CH[c]
                lab[0] = "m"
                for p in ps:
                    piece(v, H, c, p, CRIT[k % len(CRIT)])
                chunk(v, H, c, k)
                k += 1
            if v == 0:
                dma("sp", T.yx[64 * H:64 * H + 64, 3072:4096], T["xs%d" % H][0:64, 3072:4096], "dout", ("xl%d_0" % H,))
    for H in range(2):
        for s in range(4):
            for c in range(2):
                lo = 192 * s + TW * c
                dma(("sp", "act")[c], T.ys[64 * H:64 * H + 64, lo:lo + TW], T["ysb%d" % H][64 * c:64 * c + 64, TW * s:TW * s + TW], "dout",
                    tuple(otok(VI, H, e, s) for e in range(len(CH))))

    if "order" not in CACHE:
        CACHE["order"] = schedule(nodes)
        CACHE["nodes"] = nodes
    known = {q: {} for q in Q}
    cnt = {q: 0 for q in Q}
    snap, ident, seen, total = {}, {}, set(), {}

    def wait(q, deps):
        todo = sorted({d for d in deps if known[q].get(d[0], 0) < d[1]}, key=lambda d: (-len(snap.get(d, {})), d[0], -d[1]))
        for s, k in todo:
            if known[q].get(s, 0) >= k:
                continue
            Q[q].wait_ge(T.sem[s], k)
            seen.add((s, k))
            known[q][s] = k
            for s2, k2 in snap.get((s, k), {}).items():
                if known[q].get(s2, 0) < k2:
                    known[q][s2] = k2
    for i in CACHE["order"]:
        x = nodes[i]
        q = x["q"]
        if q is None:
            ident[i] = x["ext"]
            total[x["ext"][0]] = x["ext"][1]
            continue
        wait(q, [ident[d] for d in x["deps"] if d in ident])
        for j, f in enumerate(x["fns"]):
            ins = f()
            if x["ext"] is None:
                if j == len(x["fns"]) - 1:
                    cnt[q] += 1
                    ident[i] = ("s_" + q, cnt[q])
                    ins.then_inc(T.sem["s_" + q], 1)
            elif x["ext"][0] == "send":
                total["sent"] = total.get("sent", 0) + x["ext"][1]
            else:
                ident[i] = x["ext"]
                total[x["ext"][0]] = total.get(x["ext"][0], 0) + 16
                ins.then_inc(T.sem[x["ext"][0]], 16)
        if i in ident:
            snap[ident[i]] = dict(known[q])
    ends = [("s_" + q, cnt[q]) for q in ("pe", "dve", "act", "pool")] + sorted(total.items())
    known["pool"].clear()
    snap.clear()
    wait("pool", [e for e in ends if e not in seen])
